import numpy as np
import ml_dtypes


def mxq(x, axis, fmt="e4m3"):
    dtype, down = {"e4m3": (ml_dtypes.float8_e4m3fn, 7), "e5m2": (ml_dtypes.float8_e5m2, 14)}[fmt]
    v = np.moveaxis(np.asarray(x, np.float32).astype(ml_dtypes.bfloat16).astype(np.float64), axis, -1)
    blocks = v.reshape(v.shape[:-1] + (-1, 32))
    amax = np.abs(blocks).max(-1, keepdims=True)
    byte = np.maximum(np.where(amax > 0, np.frexp(amax)[1] - 1 + 127, 0) - down, 1)
    scale = np.exp2(byte - 127.0)
    codes = (blocks / scale).astype(np.float32).astype(dtype).astype(np.float64)
    return np.moveaxis((codes * scale).reshape(v.shape), -1, axis)


WIDE = False


def mx_kscale(k):
    if not WIDE:
        return np.ones(k)
    levels = np.array([10, -10, 5, -5, 0])
    if k % 512:
        return np.exp2(np.random.permutation(np.resize(levels, k // 32))).repeat(32)
    a = np.empty((k // 512, 16))
    for p in range(k // 512):
        a[p, :8] = np.random.permutation(np.resize(levels, 8))
        for g in range(8):
            far = levels[np.abs(levels - a[p, g]) >= 10]
            a[p, g + 8] = far[np.random.randint(len(far))]
    return np.exp2(a.ravel()).repeat(32)


def f64(x):
    return np.asarray(x).astype(np.float64)


def striped(idx):
    return np.tile(idx.reshape(-1, 16).T, (8, 1)).astype(np.uint16)


def unstriped(offs):
    return offs[:16].T.reshape(-1).astype(np.int64)


E2M1 = np.array([0.0, 0.5, 1.0, 1.5, 2.0, 3.0, 4.0, 6.0, -0.0, -0.5, -1.0, -1.5, -2.0, -3.0, -4.0, -6.0])


def pack_weight(w, fmt):
    k, n = w.shape
    w = f64(np.asarray(w, np.float32).astype(ml_dtypes.bfloat16)).reshape(k // 32, 32, n)
    amax = np.abs(w).max(1)
    if fmt == "e4m3":
        byte = np.frexp(amax)[1] - 1 + 127 - 7
    else:
        mant, ex = np.frexp(amax / 6.0)
        byte = np.where(mant > 0.5, ex, ex - 1) + 127
    byte = np.clip(np.where(amax > 0, byte, 1), 1, 254)
    scaled = (w * np.exp2(127.0 - byte)[:, None, :]).reshape(k, n).astype(np.float32)
    by_word = np.ascontiguousarray(scaled.reshape(k // 512, 128, 4, n).transpose(0, 1, 3, 2))
    if fmt == "e4m3":
        words = by_word.astype(ml_dtypes.float8_e4m3fn).view(np.uint8)
    else:
        c = by_word.astype(ml_dtypes.float4_e2m1fn).view(np.uint8) & 0xF
        words = (c[..., 0::2] | (c[..., 1::2] << 4)).reshape(k // 512, 128, 2 * n)
    return np.ascontiguousarray(words), np.ascontiguousarray(byte.astype(np.uint8).reshape(k // 512, 16, n))


def unpack_weight(words, scales, fmt):
    g, _, n = scales.shape
    words = np.ascontiguousarray(words).reshape(g, 128, n, -1)
    if fmt == "e4m3":
        vals = words.view(ml_dtypes.float8_e4m3fn).astype(np.float64)
    else:
        nib = np.empty((g, 128, n, 4), np.uint8)
        nib[..., 0::2] = words & 0xF
        nib[..., 1::2] = words >> 4
        vals = E2M1[nib]
    vals = vals * np.repeat(np.exp2(scales.astype(np.float64) - 127.0), 8, axis=1)[..., None]
    return vals.transpose(0, 1, 3, 2).reshape(g * 512, n)


def d_relu(v):
    return (v > 0).astype(np.float64)


K, T, E, C, H, N = 128, 768, 12, 128, 512, 1024


def by_expert(wq, xq):
    return np.concatenate([wq[e].T @ xq[:, e * C:(e + 1) * C] for e in range(E)], axis=1)


def setup_inputs():
    n = np.random.standard_normal
    v = mx_kscale(N)
    u = mx_kscale(H)
    first = np.random.permutation(np.repeat(np.arange(E), T // E))
    second = (first + 1 + np.random.permutation(np.repeat(np.arange(E - 1), -(-T // (E - 1)))[:T])) % E
    while np.bincount(second, minlength=E).max() != T // E:
        load = np.bincount(second, minlength=E); hi, lo = int(load.argmax()), int(load.argmin())
        t = np.flatnonzero((second == hi) & (first != lo))[0]; second[t] = lo
    slot_token = np.empty(E * C, np.int64); pos = np.empty((2, T), np.int64); fill = np.zeros(E, np.int64)
    place = np.stack([np.random.permutation(C) for _ in range(E)])
    for r, deal in enumerate((first, second)):
        for t in np.random.permutation(T):
            e = deal[t]; j = e * C + place[e, fill[e]]; fill[e] += 1; slot_token[j] = t; pos[r, t] = j
    g = np.random.uniform(0.2, 0.8, T)
    dy = pack_weight(n((N, T)) * v[:, None], "e4m3")
    w2t = [pack_weight(m, "e2m1") for m in n((E, N, H)) / np.sqrt(N) / v[None, :, None] * u]
    w1t = pack_weight(n((H, K)) / np.sqrt(H) / u[:, None], "e4m3")
    return {
        "dy_words": dy[0],
        "dy_scales": dy[1],
        "w2t_words": np.stack([m[0] for m in w2t]),
        "w2t_scales": np.stack([m[1] for m in w2t]),
        "w1t_words": w1t[0],
        "w1t_scales": w1t[1],
        "a": (n((H, T))).astype(np.float32),
        "gate": np.stack([np.tile(g, (128, 1)), np.tile(1.0 - g, (128, 1))]).astype(np.float32),
        "offs": striped(slot_token),
        "pos1": striped(pos[0]),
        "pos2": striped(pos[1]),
    }


def reference(dy_words, dy_scales, w2t_words, w2t_scales, w1t_words, w1t_scales, a, gate, offs, pos1, pos2):
    w2t = np.stack([unpack_weight(w2t_words[e], w2t_scales[e], "e2m1") for e in range(E)])
    w1t = unpack_weight(w1t_words, w1t_scales, "e4m3")
    idx = unstriped(offs)
    gq = unpack_weight(dy_words, dy_scales, "e4m3")[:, idx]
    y = by_expert(w2t, gq)
    dh = sum(f64(gate[r, :1]) * y[:, unstriped(p)] for r, p in enumerate((pos1, pos2)))
    return w1t.T @ mxq(dh * d_relu(f64(a)), 0, "e4m3")

@@ -1,0 +1,197 @@
+from contextlib import ExitStack
+
+import concourse.mybir as mybir
+from concourse.masks import make_identity
+
+K, T, E, C, H, N = 128, 768, 12, 128, 512, 1024
+FLOPS = 2 * N * H * E * C + 2 * H * K * T
+
+F32 = mybir.dt.float32
+BF16 = mybir.dt.bfloat16
+I32 = mybir.dt.int32
+U32 = mybir.dt.uint32
+U16 = mybir.dt.uint16
+U8 = mybir.dt.uint8
+FP8X4 = mybir.dt.float8_e4m3fn_x4
+FP4X4 = mybir.dt.float4_e2m1fn_x4
+MULT = mybir.AluOpType.mult
+SIGN = mybir.ActivationFunctionType.Sign
+RELU = mybir.ActivationFunctionType.Relu
+
+P = 128
+SLOTS = E * C
+PASSES = N // 512
+ROW_TILES = H // P
+EXPERT_UNITS = ((0, 4), (4, 8), (8, 11), (11, 12))
+TOKEN_CHUNKS = ((0, 512), (512, 768))
+
+
+def tile_moe_sub_relu_kernel(
+    tc, dy_words, dy_scales, w2t_words, w2t_scales, w1t_words, w1t_scales, a, gate, offs, pos1, pos2, out
+):
+    nc = tc.nc
+    with ExitStack() as ctx:
+        keep = ctx.enter_context(tc.tile_pool(name="keep", bufs=1))
+        ring = ctx.enter_context(tc.tile_pool(name="ring", bufs=6))
+        psum = ctx.enter_context(tc.psum_pool(name="psum", bufs=1))
+
+        def held(shape, dtype, name):
+            return keep.tile(shape, dtype, name=name, align_bytes=64)
+
+        offs_sb = keep.tile([P, SLOTS // 16], U16, name="offs_sb")
+        pos_sb = [keep.tile([P, T // 16], U16, name=f"pos{r}_sb") for r in range(2)]
+        dy_s = held([P, T], U8, "dy_s")
+        dy_w = [held([P, T], U32, f"dy_w{s}") for s in range(PASSES)]
+        w2_s = [held([P, E * PASSES, 256], U8, f"w2_s{h}") for h in range(2)]
+        w2_w = [[held([P, 4 * PASSES, 512], U8, f"w2_w{h}_{c}") for c in range(3)] for h in range(2)]
+        w1_s = held([P, K], U8, "w1_s")
+        w1_w = held([P, K], U32, "w1_w")
+        slot_s = [held([P, SLOTS], U8, f"slot_s{s}") for s in range(PASSES)]
+        slot_w = [held([P, SLOTS], U32, f"slot_w{s}") for s in range(PASSES)]
+        y = [held([P, SLOTS], F32, f"y{b}") for b in range(ROW_TILES)]
+        gate_sb = held([P, 2, T], F32, "gate_sb")
+        a_sb = [held([P, 4, t1 - t0], F32, f"a_sb{t0}") for t0, t1 in TOKEN_CHUNKS]
+        zeros = held([P, P], F32, "zeros")
+        ident = held([P, P], F32, "ident")
+
+        nc.gpsimd.memset(dy_s[:].bitcast(I32), 0)
+        nc.vector.memset(zeros[:], 0.0)
+        nc.vector.memset(w2_s[0][:].bitcast(I32), 0)
+        nc.vector.memset(slot_s[1][:].bitcast(I32), 0)
+        nc.vector.memset(w2_s[1][:].bitcast(I32), 0)
+        nc.gpsimd.memset(w1_s[:].bitcast(I32), 0)
+        nc.scalar.activation(ident[:], zeros[:], SIGN)
+        make_identity(nc, ident[:], nomemset=True)
+
+        def load_w2(h):
+            rows = w2t_scales.rearrange("e s b i -> b (e s) i")
+            for q in range(4):
+                nc.sync.dma_start(
+                    w2_s[h][32 * q : 32 * q + 4].bitcast(I32),
+                    rows[4 * q : 4 * q + 4, :, 256 * h : 256 * (h + 1)].bitcast(I32),
+                )
+            for c in range(3):
+                words = w2t_words[4 * c : 4 * c + 4].rearrange("e s p x -> p (e s) x")
+                nc.sync.dma_start(w2_w[h][c][:].bitcast(I32), words[:, :, 512 * h : 512 * (h + 1)].bitcast(I32))
+
+        nc.sync.dma_start(offs_sb[:], offs)
+        nc.sync.dma_start(dy_w[0][:].bitcast(I32), dy_words[0].rearrange("p t d -> p (t d)").bitcast(I32))
+        for q in range(4):
+            nc.sync.dma_start(dy_s[32 * q : 32 * q + 8, :].bitcast(I32), dy_scales[:, 4 * q : 4 * q + 4, :].bitcast(I32))
+        nc.sync.dma_start(dy_w[1][:].bitcast(I32), dy_words[1].rearrange("p t d -> p (t d)").bitcast(I32))
+        load_w2(0)
+        nc.sync.dma_start(pos_sb[0][:], pos1)
+        nc.sync.dma_start(pos_sb[1][:], pos2)
+        nc.sync.dma_start(gate_sb[:], gate.rearrange("r p t -> p r t"))
+        load_w2(1)
+        for (t0, t1), tile in zip(TOKEN_CHUNKS, a_sb):
+            nc.sync.dma_start(tile[:], a.rearrange("(p j) t -> p j t", j=4)[:, :, t0:t1])
+        nc.sync.dma_start(w1_w[:].bitcast(I32), w1t_words[0].rearrange("p k d -> p (k d)").bitcast(I32))
+        for q in range(4):
+            nc.sync.dma_start(w1_s[32 * q : 32 * q + 4, :].bitcast(I32), w1t_scales[0, 4 * q : 4 * q + 4, :].bitcast(I32))
+
+        def gather_words(e0, e1, s):
+            nc.vector.tensor_copy(
+                slot_w[s][:, e0 * C : e1 * C], dy_w[s][:].indirect(offs_sb[:, e0 * C // 16 : e1 * C // 16])
+            )
+
+        gather_words(*EXPERT_UNITS[0], 0)
+        for j0 in range(0, SLOTS, 512):
+            nc.vector.tensor_copy(slot_s[0][:, j0 : j0 + 512], dy_s[:].indirect(offs_sb[:, j0 // 16 : (j0 + 512) // 16]))
+        for q in range(4):
+            nc.scalar.dma_start(
+                slot_s[1][32 * q : 32 * q + 4, :].bitcast(I32), slot_s[0][32 * q + 4 : 32 * q + 8, :].bitcast(I32)
+            )
+
+        def experts_product(e0, e1, b):
+            h, half = divmod(b, 2)
+            bank = psum.tile([P, (e1 - e0) * C], F32, name="y_bank", tag="y_bank", bufs=3)
+            for e in range(e0, e1):
+                cols = slice(e * C, (e + 1) * C)
+                for s in range(PASSES):
+                    nc.tensor.matmul_mx(
+                        out=bank[:, (e - e0) * C : (e - e0 + 1) * C],
+                        lhsT=w2_w[h][e // 4][:, (e % 4) * PASSES + s, 256 * half : 256 * (half + 1)].bitcast(FP4X4),
+                        lhsT_scale=w2_s[h][:, e * PASSES + s, P * half : P * (half + 1)],
+                        rhs=slot_w[s][:, cols].bitcast(FP8X4),
+                        rhs_scale=slot_s[s][:, cols],
+                        start=(s == 0),
+                        stop=(s == PASSES - 1),
+                    )
+            nc.scalar.copy(y[b][:, e0 * C : e1 * C], bank[:])
+
+        gather_words(*EXPERT_UNITS[0], 1)
+        for e0, e1 in EXPERT_UNITS[1:]:
+            for s in range(PASSES):
+                gather_words(e0, e1, s)
+        for e0, e1 in EXPERT_UNITS:
+            experts_product(e0, e1, 0)
+        for b in range(1, ROW_TILES):
+            for e0 in range(0, E, 4):
+                experts_product(e0, e0 + 4, b)
+
+        dh_t = []
+        for t0, t1 in TOKEN_CHUNKS:
+            tiles = (t1 - t0) // P
+            rounded = held([P, tiles, 2, P, 2], BF16, f"dh_t{t0}")
+            dh_t.append(rounded)
+            for b in range(ROW_TILES):
+                gated = []
+                for r in range(2):
+                    u = ring.tile([P, t1 - t0], F32, name="gated", tag="gated")
+                    nc.vector.tensor_tensor(
+                        u[:], y[b][:].indirect(pos_sb[r][:, t0 // 16 : t1 // 16]), gate_sb[:, r, t0:t1], MULT
+                    )
+                    gated.append(u)
+                bank = psum.tile([P, tiles, P], F32, name="dh_bank", tag="dh_bank", bufs=2)
+                for m in range(tiles):
+                    for r in range(2):
+                        nc.tensor.matmul(
+                            bank[:, m, :],
+                            gated[r][:, m * P : (m + 1) * P],
+                            ident[:],
+                            start=(r == 0),
+                            stop=(r == 1),
+                            is_transpose=True,
+                        )
+                nc.scalar.copy(
+                    rounded[:, :, :, 32 * b : 32 * (b + 1), :],
+                    bank[:].rearrange("t m (p u e) -> t m u p e", u=2, e=2),
+                )
+
+        for (t0, t1), rounded, a_rows in zip(TOKEN_CHUNKS, dh_t, a_sb):
+            width = t1 - t0
+            mask = held([P, width, 4], BF16, f"mask{t0}")
+            da = held([P, width, 4], BF16, f"da{t0}")
+            da_w = held([P, width], U32, f"da_w{t0}")
+            da_s = held([P, width], U8, f"da_s{t0}")
+            for c0 in range(0, width, P):
+                piece = mask[:, c0 : c0 + P, :]
+                nc.scalar.activation(piece, a_rows[:, :, c0 : c0 + P].rearrange("p j t -> p t j"), SIGN)
+                nc.scalar.activation(piece, piece, RELU)
+            for c0 in range(0, width, 2 * P):
+                bank = psum.tile([P, 2, 2 * P], F32, name="turn_bank", tag="turn_bank", bufs=2)
+                for m in range(2):
+                    for u in range(2):
+                        words = rounded[:, c0 // P + m, u].rearrange("t p e -> t (p e)").bitcast(F32)
+                        nc.tensor.transpose(bank[:, u, m * P : (m + 1) * P], words, ident[:])
+                nc.vector.tensor_tensor(
+                    da[:, c0 : c0 + 2 * P, :].rearrange("p t (u e) -> p t u e", u=2),
+                    bank[:].bitcast(BF16).rearrange("p u (t e) -> p t u e", e=2),
+                    mask[:, c0 : c0 + 2 * P, :].rearrange("p t (u e) -> p t u e", u=2),
+                    MULT,
+                )
+            nc.vector.quantize_mx(da_w[:].bitcast(FP8X4), da_s[:], da[:].rearrange("p t j -> p (t j)"))
+            bank = psum.tile([P, width], F32, name="out_bank", tag="out_bank", bufs=1)
+            nc.tensor.matmul_mx(
+                out=bank[:],
+                lhsT=w1_w[:].bitcast(FP8X4),
+                lhsT_scale=w1_s[:],
+                rhs=da_w[:].bitcast(FP8X4),
+                rhs_scale=da_s[:],
+                start=True,
+                stop=True,
+            )
+            result = held([P, width], F32, f"result{t0}")
+            nc.scalar.copy(result[:], bank[:])
+            nc.sync.dma_start(out[:, t0:t1], result[:])

@@ -32,7 +32,7 @@ def tile_moe_sub_relu_kernel(
     nc = tc.nc
     with ExitStack() as ctx:
         keep = ctx.enter_context(tc.tile_pool(name="keep", bufs=1))
-        ring = ctx.enter_context(tc.tile_pool(name="ring", bufs=6))
+        ring = ctx.enter_context(tc.tile_pool(name="ring", bufs=10))
         psum = ctx.enter_context(tc.psum_pool(name="psum", bufs=1))
 
         def held(shape, dtype, name):
@@ -49,63 +49,90 @@ def tile_moe_sub_relu_kernel(
         slot_s = [held([P, SLOTS], U8, f"slot_s{s}") for s in range(PASSES)]
         slot_w = [held([P, SLOTS], U32, f"slot_w{s}") for s in range(PASSES)]
         y = [held([P, SLOTS], F32, f"y{b}") for b in range(ROW_TILES)]
-        gate_sb = held([P, 2, T], F32, "gate_sb")
-        a_sb = [held([P, 4, t1 - t0], F32, f"a_sb{t0}") for t0, t1 in TOKEN_CHUNKS]
+        gate_sb = [held([P, 2, t1 - t0], F32, f"gate_sb{t0}") for t0, t1 in TOKEN_CHUNKS]
+        a_sb = [held([P, 4, 2 * P], F32, f"a_sb{n}") for n in range(T // (2 * P))]
+        gate_rows = held([P, 2, P], F32, "gate_rows")
+        gate_cols = held([P, 2, 8], F32, "gate_cols")
         zeros = held([P, P], F32, "zeros")
         ident = held([P, P], F32, "ident")
 
         nc.gpsimd.memset(dy_s[:].bitcast(I32), 0)
         nc.vector.memset(zeros[:], 0.0)
         nc.vector.memset(w2_s[0][:].bitcast(I32), 0)
-        nc.vector.memset(slot_s[1][:].bitcast(I32), 0)
+        nc.gpsimd.memset(slot_s[1][:].bitcast(I32), 0)
         nc.vector.memset(w2_s[1][:].bitcast(I32), 0)
         nc.gpsimd.memset(w1_s[:].bitcast(I32), 0)
         nc.scalar.activation(ident[:], zeros[:], SIGN)
         make_identity(nc, ident[:], nomemset=True)
 
-        def load_w2(h):
+        def load_w2_scales(h):
             rows = w2t_scales.rearrange("e s b i -> b (e s) i")
             for q in range(4):
                 nc.sync.dma_start(
                     w2_s[h][32 * q : 32 * q + 4].bitcast(I32),
                     rows[4 * q : 4 * q + 4, :, 256 * h : 256 * (h + 1)].bitcast(I32),
                 )
-            for c in range(3):
-                words = w2t_words[4 * c : 4 * c + 4].rearrange("e s p x -> p (e s) x")
-                nc.sync.dma_start(w2_w[h][c][:].bitcast(I32), words[:, :, 512 * h : 512 * (h + 1)].bitcast(I32))
+
+        def load_w2_words(h, c):
+            words = w2t_words[4 * c : 4 * c + 4].rearrange("e s p x -> p (e s) x")
+            nc.sync.dma_start(w2_w[h][c][:].bitcast(I32), words[:, :, 512 * h : 512 * (h + 1)].bitcast(I32))
+
+        def load_tokens(n):
+            nc.sync.dma_start(a_sb[n][:], a.rearrange("(p j) t -> p j t", j=4)[:, :, 2 * P * n : 2 * P * (n + 1)])
 
         nc.sync.dma_start(offs_sb[:], offs)
-        nc.sync.dma_start(dy_w[0][:].bitcast(I32), dy_words[0].rearrange("p t d -> p (t d)").bitcast(I32))
+        nc.sync.dma_start(gate_rows[:], gate.rearrange("r p (m n) -> (p m) r n", n=P)[0:P])
         for q in range(4):
             nc.sync.dma_start(dy_s[32 * q : 32 * q + 8, :].bitcast(I32), dy_scales[:, 4 * q : 4 * q + 4, :].bitcast(I32))
-        nc.sync.dma_start(dy_w[1][:].bitcast(I32), dy_words[1].rearrange("p t d -> p (t d)").bitcast(I32))
-        load_w2(0)
+        for s in range(PASSES):
+            nc.sync.dma_start(dy_w[s][:].bitcast(I32), dy_words[s].rearrange("p t d -> p (t d)").bitcast(I32))
+        load_tokens(0)
+        load_w2_scales(0)
+        for c in range(3):
+            load_w2_words(0, c)
         nc.sync.dma_start(pos_sb[0][:], pos1)
         nc.sync.dma_start(pos_sb[1][:], pos2)
-        nc.sync.dma_start(gate_sb[:], gate.rearrange("r p t -> p r t"))
-        load_w2(1)
-        for (t0, t1), tile in zip(TOKEN_CHUNKS, a_sb):
-            nc.sync.dma_start(tile[:], a.rearrange("(p j) t -> p j t", j=4)[:, :, t0:t1])
+        load_tokens(1)
+        load_w2_words(1, 0)
+        load_w2_scales(1)
+        load_w2_words(1, 1)
+        load_w2_words(1, 2)
+        load_tokens(2)
         nc.sync.dma_start(w1_w[:].bitcast(I32), w1t_words[0].rearrange("p k d -> p (k d)").bitcast(I32))
         for q in range(4):
             nc.sync.dma_start(w1_s[32 * q : 32 * q + 4, :].bitcast(I32), w1t_scales[0, 4 * q : 4 * q + 4, :].bitcast(I32))
+
+        def psum_bank(number, shape):
+            return psum.tile(shape, F32, name=f"bank{number}", tag=f"bank{number}")
+
+        bank = psum_bank(7, [P, 2, P])
+        for r in range(2):
+            nc.tensor.transpose(bank[:, r, :], gate_rows[:, r, :], ident[:])
+        nc.scalar.copy(gate_cols[:], bank[:, :, 0:8])
+        spread = [(0, 0, 4), (0, 1, 5), (1, None, 6)]
+        for n, only, number in spread:
+            t0, t1 = TOKEN_CHUNKS[n]
+            rs = range(2) if only is None else (only,)
+            bank = psum_bank(number, [P, len(rs), t1 - t0])
+            for x, r in enumerate(rs):
+                for m in range((t1 - t0) // P):
+                    column = gate_cols[:, r, t0 // P + m : t0 // P + m + 1].to_broadcast([P, P])
+                    nc.tensor.transpose(bank[:, x, m * P : (m + 1) * P], column, ident[:])
+            nc.scalar.copy(gate_sb[n][:, rs[0] : rs[-1] + 1, :], bank[:])
 
         def gather_words(e0, e1, s):
             nc.vector.tensor_copy(
                 slot_w[s][:, e0 * C : e1 * C], dy_w[s][:].indirect(offs_sb[:, e0 * C // 16 : e1 * C // 16])
             )
 
-        gather_words(*EXPERT_UNITS[0], 0)
         for j0 in range(0, SLOTS, 512):
             nc.vector.tensor_copy(slot_s[0][:, j0 : j0 + 512], dy_s[:].indirect(offs_sb[:, j0 // 16 : (j0 + 512) // 16]))
-        for q in range(4):
-            nc.scalar.dma_start(
-                slot_s[1][32 * q : 32 * q + 4, :].bitcast(I32), slot_s[0][32 * q + 4 : 32 * q + 8, :].bitcast(I32)
-            )
+        nc.scalar.dma_start(slot_s[1][0:112, :].bitcast(I32), slot_s[0][4:116, :].bitcast(I32))
 
-        def experts_product(e0, e1, b):
+
+        def experts_product(e0, e1, b, number):
             h, half = divmod(b, 2)
-            bank = psum.tile([P, (e1 - e0) * C], F32, name="y_bank", tag="y_bank", bufs=3)
+            bank = psum_bank(number, [P, (e1 - e0) * C])
             for e in range(e0, e1):
                 cols = slice(e * C, (e + 1) * C)
                 for s in range(PASSES):
@@ -120,57 +147,62 @@ def tile_moe_sub_relu_kernel(
                     )
             nc.scalar.copy(y[b][:, e0 * C : e1 * C], bank[:])
 
-        gather_words(*EXPERT_UNITS[0], 1)
-        for e0, e1 in EXPERT_UNITS[1:]:
+        for e0, e1 in EXPERT_UNITS:
             for s in range(PASSES):
                 gather_words(e0, e1, s)
-        for e0, e1 in EXPERT_UNITS:
-            experts_product(e0, e1, 0)
-        for b in range(1, ROW_TILES):
-            for e0 in range(0, E, 4):
-                experts_product(e0, e0 + 4, b)
+        for (e0, e1), number in zip(EXPERT_UNITS, (0, 2, 4, 5)):
+            experts_product(e0, e1, 0, number)
+        for b, numbers in ((1, (1, 3, 6)), (2, (0, 2, 4)), (3, (1, 3, 5))):
+            for c, number in enumerate(numbers):
+                experts_product(4 * c, 4 * c + 4, b, number)
 
-        dh_t = []
-        for t0, t1 in TOKEN_CHUNKS:
+        dh_t = [held([P, (t1 - t0) // P, 2, P, 2], BF16, f"dh_t{t0}") for t0, t1 in TOKEN_CHUNKS]
+        relu_on = [held([P, t1 - t0, 4], BF16, f"mask{t0}") for t0, t1 in TOKEN_CHUNKS]
+        for n, (t0, t1) in enumerate(TOKEN_CHUNKS):
+            for m in range((t1 - t0) // P):
+                piece = relu_on[n][:, m * P : (m + 1) * P, :].rearrange("p (g x) j -> p g x j", g=8)
+                signs = piece
+                if n == 1:
+                    b = 2 + m
+                    signs = dh_t[0][:, :, :, 32 * b : 32 * (b + 1), :].rearrange("q m u (x y) e -> q (m u) x (y e)", y=2)
+                pair, second = divmod(t0 // P + m, 2)
+                saved = a_sb[pair][:, :, second * P : (second + 1) * P]
+                nc.scalar.activation(signs, saved.rearrange("p j (g x) -> p g x j", g=8), SIGN)
+                nc.scalar.activation(piece, signs, RELU)
+
+        for n, b, number in ((0, 0, 4), (0, 1, 5), (1, 0, 4), (0, 2, 2), (0, 3, 3), (1, 1, 4), (1, 2, 5), (1, 3, 2)):
+            t0, t1 = TOKEN_CHUNKS[n]
             tiles = (t1 - t0) // P
-            rounded = held([P, tiles, 2, P, 2], BF16, f"dh_t{t0}")
-            dh_t.append(rounded)
-            for b in range(ROW_TILES):
-                gated = []
-                for r in range(2):
-                    u = ring.tile([P, t1 - t0], F32, name="gated", tag="gated")
-                    nc.vector.tensor_tensor(
-                        u[:], y[b][:].indirect(pos_sb[r][:, t0 // 16 : t1 // 16]), gate_sb[:, r, t0:t1], MULT
-                    )
-                    gated.append(u)
-                bank = psum.tile([P, tiles, P], F32, name="dh_bank", tag="dh_bank", bufs=2)
-                for m in range(tiles):
-                    for r in range(2):
-                        nc.tensor.matmul(
-                            bank[:, m, :],
-                            gated[r][:, m * P : (m + 1) * P],
-                            ident[:],
-                            start=(r == 0),
-                            stop=(r == 1),
-                            is_transpose=True,
-                        )
-                nc.scalar.copy(
-                    rounded[:, :, :, 32 * b : 32 * (b + 1), :],
-                    bank[:].rearrange("t m (p u e) -> t m u p e", u=2, e=2),
+            gated = []
+            for r in range(2):
+                u = ring.tile([P, t1 - t0], F32, name="gated", tag="gated")
+                nc.vector.tensor_tensor(
+                    u[:], y[b][:].indirect(pos_sb[r][:, t0 // 16 : t1 // 16]), gate_sb[n][:, r, :], MULT
                 )
+                gated.append(u)
+            bank = psum_bank(number, [P, tiles, P])
+            for m in range(tiles):
+                for r in range(2):
+                    nc.tensor.matmul(
+                        bank[:, m, :],
+                        gated[r][:, m * P : (m + 1) * P],
+                        ident[:],
+                        start=(r == 0),
+                        stop=(r == 1),
+                        is_transpose=True,
+                    )
+            nc.scalar.copy(
+                dh_t[n][:, :, :, 32 * b : 32 * (b + 1), :],
+                bank[:].rearrange("t m (p u e) -> t m u p e", u=2, e=2),
+            )
 
-        for (t0, t1), rounded, a_rows in zip(TOKEN_CHUNKS, dh_t, a_sb):
+        for (t0, t1), rounded, mask in zip(TOKEN_CHUNKS, dh_t, relu_on):
             width = t1 - t0
-            mask = held([P, width, 4], BF16, f"mask{t0}")
             da = held([P, width, 4], BF16, f"da{t0}")
             da_w = held([P, width], U32, f"da_w{t0}")
             da_s = held([P, width], U8, f"da_s{t0}")
-            for c0 in range(0, width, P):
-                piece = mask[:, c0 : c0 + P, :]
-                nc.scalar.activation(piece, a_rows[:, :, c0 : c0 + P].rearrange("p j t -> p t j"), SIGN)
-                nc.scalar.activation(piece, piece, RELU)
             for c0 in range(0, width, 2 * P):
-                bank = psum.tile([P, 2, 2 * P], F32, name="turn_bank", tag="turn_bank", bufs=2)
+                bank = psum_bank((0, 1, 6)[(t0 + c0) // (2 * P)], [P, 2, 2 * P])
                 for m in range(2):
                     for u in range(2):
                         words = rounded[:, c0 // P + m, u].rearrange("t p e -> t (p e)").bitcast(F32)
@@ -182,7 +214,7 @@ def tile_moe_sub_relu_kernel(
                     MULT,
                 )
             nc.vector.quantize_mx(da_w[:].bitcast(FP8X4), da_s[:], da[:].rearrange("p t j -> p (t j)"))
-            bank = psum.tile([P, width], F32, name="out_bank", tag="out_bank", bufs=1)
+            bank = psum_bank(7 if t0 == 0 else 3, [P, width])
             nc.tensor.matmul_mx(
                 out=bank[:],
                 lhsT=w1_w[:].bitcast(FP8X4),

@@ -22,7 +22,7 @@ P = 128
 SLOTS = E * C
 PASSES = N // 512
 ROW_TILES = H // P
-EXPERT_UNITS = ((0, 4), (4, 8), (8, 11), (11, 12))
+EXPERT_UNITS = ((0, 4), (4, 8), (8, 10), (10, 12))
 TOKEN_CHUNKS = ((0, 512), (512, 768))
 
 
@@ -42,15 +42,15 @@ def tile_moe_sub_relu_kernel(
         pos_sb = [keep.tile([P, T // 16], U16, name=f"pos{r}_sb") for r in range(2)]
         dy_s = held([P, T], U8, "dy_s")
         dy_w = [held([P, T], U32, f"dy_w{s}") for s in range(PASSES)]
-        w2_s = [held([P, E * PASSES, 256], U8, f"w2_s{h}") for h in range(2)]
-        w2_w = [[held([P, 4 * PASSES, 512], U8, f"w2_w{h}_{c}") for c in range(3)] for h in range(2)]
+        w2_s = held([P, E * PASSES, H], U8, "w2_s")
+        w2_w = [held([P, 2 * PASSES, 2 * H], U8, f"w2_w{c}") for c in range(E // 2)]
         w1_s = held([P, K], U8, "w1_s")
         w1_w = held([P, K], U32, "w1_w")
         slot_s = [held([P, SLOTS], U8, f"slot_s{s}") for s in range(PASSES)]
         slot_w = [held([P, SLOTS], U32, f"slot_w{s}") for s in range(PASSES)]
         y = [held([P, SLOTS], F32, f"y{b}") for b in range(ROW_TILES)]
         gate_sb = [held([P, 2, t1 - t0], F32, f"gate_sb{t0}") for t0, t1 in TOKEN_CHUNKS]
-        a_sb = [held([P, 4, 2 * P], F32, f"a_sb{n}") for n in range(T // (2 * P))]
+        a_sb = [held([P, 4, t1 - t0], F32, f"a_sb{t0}") for t0, t1 in TOKEN_CHUNKS]
         gate_rows = held([P, 2, P], F32, "gate_rows")
         gate_cols = held([P, 2, 8], F32, "gate_cols")
         zeros = held([P, P], F32, "zeros")
@@ -58,27 +58,11 @@ def tile_moe_sub_relu_kernel(
 
         nc.gpsimd.memset(dy_s[:].bitcast(I32), 0)
         nc.vector.memset(zeros[:], 0.0)
-        nc.vector.memset(w2_s[0][:].bitcast(I32), 0)
+        nc.vector.memset(w2_s[:].bitcast(I32), 0)
         nc.gpsimd.memset(slot_s[1][:].bitcast(I32), 0)
-        nc.vector.memset(w2_s[1][:].bitcast(I32), 0)
         nc.gpsimd.memset(w1_s[:].bitcast(I32), 0)
         nc.scalar.activation(ident[:], zeros[:], SIGN)
         make_identity(nc, ident[:], nomemset=True)
-
-        def load_w2_scales(h):
-            rows = w2t_scales.rearrange("e s b i -> b (e s) i")
-            for q in range(4):
-                nc.sync.dma_start(
-                    w2_s[h][32 * q : 32 * q + 4].bitcast(I32),
-                    rows[4 * q : 4 * q + 4, :, 256 * h : 256 * (h + 1)].bitcast(I32),
-                )
-
-        def load_w2_words(h, c):
-            words = w2t_words[4 * c : 4 * c + 4].rearrange("e s p x -> p (e s) x")
-            nc.sync.dma_start(w2_w[h][c][:].bitcast(I32), words[:, :, 512 * h : 512 * (h + 1)].bitcast(I32))
-
-        def load_tokens(n):
-            nc.sync.dma_start(a_sb[n][:], a.rearrange("(p j) t -> p j t", j=4)[:, :, 2 * P * n : 2 * P * (n + 1)])
 
         nc.sync.dma_start(offs_sb[:], offs)
         nc.sync.dma_start(gate_rows[:], gate.rearrange("r p (m n) -> (p m) r n", n=P)[0:P])
@@ -86,18 +70,16 @@ def tile_moe_sub_relu_kernel(
             nc.sync.dma_start(dy_s[32 * q : 32 * q + 8, :].bitcast(I32), dy_scales[:, 4 * q : 4 * q + 4, :].bitcast(I32))
         for s in range(PASSES):
             nc.sync.dma_start(dy_w[s][:].bitcast(I32), dy_words[s].rearrange("p t d -> p (t d)").bitcast(I32))
-        load_tokens(0)
-        load_w2_scales(0)
-        for c in range(3):
-            load_w2_words(0, c)
-        nc.sync.dma_start(pos_sb[0][:], pos1)
-        nc.sync.dma_start(pos_sb[1][:], pos2)
-        load_tokens(1)
-        load_w2_words(1, 0)
-        load_w2_scales(1)
-        load_w2_words(1, 1)
-        load_w2_words(1, 2)
-        load_tokens(2)
+        rows = w2t_scales.rearrange("e s b i -> b (e s) i")
+        for r in range(4):
+            nc.sync.dma_start(w2_s[r:P:32].bitcast(I32), rows[r:16:4].bitcast(I32))
+        for c in range(E // 2):
+            words = w2t_words[2 * c : 2 * c + 2].rearrange("e s p x -> p (e s) x")
+            nc.sync.dma_start(w2_w[c][:].bitcast(I32), words.bitcast(I32))
+            if c in (3, 4):
+                nc.sync.dma_start(pos_sb[c - 3][:], (pos1, pos2)[c - 3])
+        for (t0, t1), saved in zip(TOKEN_CHUNKS, a_sb):
+            nc.sync.dma_start(saved[:], a.rearrange("(p j) t -> p j t", j=4)[:, :, t0:t1])
         nc.sync.dma_start(w1_w[:].bitcast(I32), w1t_words[0].rearrange("p k d -> p (k d)").bitcast(I32))
         for q in range(4):
             nc.sync.dma_start(w1_s[32 * q : 32 * q + 4, :].bitcast(I32), w1t_scales[0, 4 * q : 4 * q + 4, :].bitcast(I32))
@@ -131,15 +113,14 @@ def tile_moe_sub_relu_kernel(
 
 
         def experts_product(e0, e1, b, number):
-            h, half = divmod(b, 2)
             bank = psum_bank(number, [P, (e1 - e0) * C])
             for e in range(e0, e1):
                 cols = slice(e * C, (e + 1) * C)
                 for s in range(PASSES):
                     nc.tensor.matmul_mx(
                         out=bank[:, (e - e0) * C : (e - e0 + 1) * C],
-                        lhsT=w2_w[h][e // 4][:, (e % 4) * PASSES + s, 256 * half : 256 * (half + 1)].bitcast(FP4X4),
-                        lhsT_scale=w2_s[h][:, e * PASSES + s, P * half : P * (half + 1)],
+                        lhsT=w2_w[e // 2][:, (e % 2) * PASSES + s, 2 * P * b : 2 * P * (b + 1)].bitcast(FP4X4),
+                        lhsT_scale=w2_s[:, e * PASSES + s, P * b : P * (b + 1)],
                         rhs=slot_w[s][:, cols].bitcast(FP8X4),
                         rhs_scale=slot_s[s][:, cols],
                         start=(s == 0),
@@ -150,9 +131,9 @@ def tile_moe_sub_relu_kernel(
         for e0, e1 in EXPERT_UNITS:
             for s in range(PASSES):
                 gather_words(e0, e1, s)
-        for (e0, e1), number in zip(EXPERT_UNITS, (0, 2, 4, 5)):
+        for (e0, e1), number in zip(EXPERT_UNITS, (0, 1, 2, 3)):
             experts_product(e0, e1, 0, number)
-        for b, numbers in ((1, (1, 3, 6)), (2, (0, 2, 4)), (3, (1, 3, 5))):
+        for b, numbers in ((1, (4, 5, 6)), (2, (0, 3, 2)), (3, (4, 6, 1))):
             for c, number in enumerate(numbers):
                 experts_product(4 * c, 4 * c + 4, b, number)
 
@@ -160,17 +141,11 @@ def tile_moe_sub_relu_kernel(
         relu_on = [held([P, t1 - t0, 4], BF16, f"mask{t0}") for t0, t1 in TOKEN_CHUNKS]
         for n, (t0, t1) in enumerate(TOKEN_CHUNKS):
             for m in range((t1 - t0) // P):
-                piece = relu_on[n][:, m * P : (m + 1) * P, :].rearrange("p (g x) j -> p g x j", g=8)
-                signs = piece
-                if n == 1:
-                    b = 2 + m
-                    signs = dh_t[0][:, :, :, 32 * b : 32 * (b + 1), :].rearrange("q m u (x y) e -> q (m u) x (y e)", y=2)
-                pair, second = divmod(t0 // P + m, 2)
-                saved = a_sb[pair][:, :, second * P : (second + 1) * P]
-                nc.scalar.activation(signs, saved.rearrange("p j (g x) -> p g x j", g=8), SIGN)
-                nc.scalar.activation(piece, signs, RELU)
+                piece = relu_on[n][:, m * P : (m + 1) * P, :]
+                nc.scalar.activation(piece, a_sb[n][:, :, m * P : (m + 1) * P].rearrange("p j t -> p t j"), SIGN)
+                nc.scalar.activation(piece, piece, RELU)
 
-        for n, b, number in ((0, 0, 4), (0, 1, 5), (1, 0, 4), (0, 2, 2), (0, 3, 3), (1, 1, 4), (1, 2, 5), (1, 3, 2)):
+        for n, b, number in ((0, 0, 5), (0, 1, 0), (0, 2, 4), (0, 3, 3), (1, 0, 2), (1, 1, 6), (1, 2, 1), (1, 3, 5)):
             t0, t1 = TOKEN_CHUNKS[n]
             tiles = (t1 - t0) // P
             gated = []
@@ -202,7 +177,7 @@ def tile_moe_sub_relu_kernel(
             da_w = held([P, width], U32, f"da_w{t0}")
             da_s = held([P, width], U8, f"da_s{t0}")
             for c0 in range(0, width, 2 * P):
-                bank = psum_bank((0, 1, 6)[(t0 + c0) // (2 * P)], [P, 2, 2 * P])
+                bank = psum_bank((7, 0, 4)[(t0 + c0) // (2 * P)], [P, 2, 2 * P])
                 for m in range(2):
                     for u in range(2):
                         words = rounded[:, c0 // P + m, u].rearrange("t p e -> t (p e)").bitcast(F32)
@@ -214,7 +189,7 @@ def tile_moe_sub_relu_kernel(
                     MULT,
                 )
             nc.vector.quantize_mx(da_w[:].bitcast(FP8X4), da_s[:], da[:].rearrange("p t j -> p (t j)"))
-            bank = psum_bank(7 if t0 == 0 else 3, [P, width])
+            bank = psum_bank(3 if t0 == 0 else 7, [P, width])
             nc.tensor.matmul_mx(
                 out=bank[:],
                 lhsT=w1_w[:].bitcast(FP8X4),

@@ -16,13 +16,13 @@ FP8X4 = mybir.dt.float8_e4m3fn_x4
 FP4X4 = mybir.dt.float4_e2m1fn_x4
 MULT = mybir.AluOpType.mult
 SIGN = mybir.ActivationFunctionType.Sign
-RELU = mybir.ActivationFunctionType.Relu
 
 P = 128
 SLOTS = E * C
 PASSES = N // 512
 ROW_TILES = H // P
-EXPERT_UNITS = ((0, 4), (4, 8), (8, 10), (10, 12))
+EXPERT_UNITS = ((0, 4), (4, 8), (8, 11), (11, 12))
+WEIGHT_LOADS = ((0, 2), (2, 4), (4, 6), (6, 8), (8, 10), (10, 11), (11, 12))
 TOKEN_CHUNKS = ((0, 512), (512, 768))
 
 
@@ -42,8 +42,8 @@ def tile_moe_sub_relu_kernel(
         pos_sb = [keep.tile([P, T // 16], U16, name=f"pos{r}_sb") for r in range(2)]
         dy_s = held([P, T], U8, "dy_s")
         dy_w = [held([P, T], U32, f"dy_w{s}") for s in range(PASSES)]
-        w2_s = held([P, E * PASSES, H], U8, "w2_s")
-        w2_w = [held([P, 2 * PASSES, 2 * H], U8, f"w2_w{c}") for c in range(E // 2)]
+        w2_s = [held([P, E * PASSES, H // 2], U8, f"w2_s{h}") for h in range(2)]
+        w2_w = held([P, E * PASSES, 2 * H], U8, "w2_w")
         w1_s = held([P, K], U8, "w1_s")
         w1_w = held([P, K], U32, "w1_w")
         slot_s = [held([P, SLOTS], U8, f"slot_s{s}") for s in range(PASSES)]
@@ -58,26 +58,33 @@ def tile_moe_sub_relu_kernel(
 
         nc.gpsimd.memset(dy_s[:].bitcast(I32), 0)
         nc.vector.memset(zeros[:], 0.0)
-        nc.vector.memset(w2_s[:].bitcast(I32), 0)
+        nc.vector.memset(gate_rows[:], 0.0)
+        nc.vector.memset(w2_s[0][:].bitcast(I32), 0)
+        nc.vector.memset(w2_s[1][:].bitcast(I32), 0)
         nc.gpsimd.memset(slot_s[1][:].bitcast(I32), 0)
         nc.gpsimd.memset(w1_s[:].bitcast(I32), 0)
         nc.scalar.activation(ident[:], zeros[:], SIGN)
         make_identity(nc, ident[:], nomemset=True)
 
         nc.sync.dma_start(offs_sb[:], offs)
-        nc.sync.dma_start(gate_rows[:], gate.rearrange("r p (m n) -> (p m) r n", n=P)[0:P])
         for q in range(4):
             nc.sync.dma_start(dy_s[32 * q : 32 * q + 8, :].bitcast(I32), dy_scales[:, 4 * q : 4 * q + 4, :].bitcast(I32))
         for s in range(PASSES):
             nc.sync.dma_start(dy_w[s][:].bitcast(I32), dy_words[s].rearrange("p t d -> p (t d)").bitcast(I32))
-        rows = w2t_scales.rearrange("e s b i -> b (e s) i")
-        for r in range(4):
-            nc.sync.dma_start(w2_s[r:P:32].bitcast(I32), rows[r:16:4].bitcast(I32))
-        for c in range(E // 2):
-            words = w2t_words[2 * c : 2 * c + 2].rearrange("e s p x -> p (e s) x")
-            nc.sync.dma_start(w2_w[c][:].bitcast(I32), words.bitcast(I32))
-            if c in (3, 4):
-                nc.sync.dma_start(pos_sb[c - 3][:], (pos1, pos2)[c - 3])
+        nc.sync.dma_start(gate_rows[0:8], gate.rearrange("r p (m n) -> (p m) r n", n=P)[0:8])
+
+        def load_w2_scales(h):
+            rows = w2t_scales.rearrange("e s b i -> b (e s) i")[:, :, H // 2 * h : H // 2 * (h + 1)]
+            for r in range(4):
+                nc.sync.dma_start(w2_s[h][r:P:32].bitcast(I32), rows[r:16:4].bitcast(I32))
+
+        load_w2_scales(0)
+        for c, (e0, e1) in enumerate(WEIGHT_LOADS):
+            words = w2t_words[e0:e1].rearrange("e s p x -> p (e s) x")
+            nc.sync.dma_start(w2_w[:, e0 * PASSES : e1 * PASSES].bitcast(I32), words.bitcast(I32))
+            if c in (2, 3):
+                nc.sync.dma_start(pos_sb[c - 2][:], (pos1, pos2)[c - 2])
+        load_w2_scales(1)
         for (t0, t1), saved in zip(TOKEN_CHUNKS, a_sb):
             nc.sync.dma_start(saved[:], a.rearrange("(p j) t -> p j t", j=4)[:, :, t0:t1])
         nc.sync.dma_start(w1_w[:].bitcast(I32), w1t_words[0].rearrange("p k d -> p (k d)").bitcast(I32))
@@ -119,8 +126,8 @@ def tile_moe_sub_relu_kernel(
                 for s in range(PASSES):
                     nc.tensor.matmul_mx(
                         out=bank[:, (e - e0) * C : (e - e0 + 1) * C],
-                        lhsT=w2_w[e // 2][:, (e % 2) * PASSES + s, 2 * P * b : 2 * P * (b + 1)].bitcast(FP4X4),
-                        lhsT_scale=w2_s[:, e * PASSES + s, P * b : P * (b + 1)],
+                        lhsT=w2_w[:, e * PASSES + s, 2 * P * b : 2 * P * (b + 1)].bitcast(FP4X4),
+                        lhsT_scale=w2_s[b // 2][:, e * PASSES + s, P * (b % 2) : P * (b % 2 + 1)],
                         rhs=slot_w[s][:, cols].bitcast(FP8X4),
                         rhs_scale=slot_s[s][:, cols],
                         start=(s == 0),
@@ -133,7 +140,7 @@ def tile_moe_sub_relu_kernel(
                 gather_words(e0, e1, s)
         for (e0, e1), number in zip(EXPERT_UNITS, (0, 1, 2, 3)):
             experts_product(e0, e1, 0, number)
-        for b, numbers in ((1, (4, 5, 6)), (2, (0, 3, 2)), (3, (4, 6, 1))):
+        for b, numbers in ((1, (4, 5, 6)), (2, (0, 1, 2)), (3, (3, 4, 5))):
             for c, number in enumerate(numbers):
                 experts_product(4 * c, 4 * c + 4, b, number)
 
@@ -143,9 +150,8 @@ def tile_moe_sub_relu_kernel(
             for m in range((t1 - t0) // P):
                 piece = relu_on[n][:, m * P : (m + 1) * P, :]
                 nc.scalar.activation(piece, a_sb[n][:, :, m * P : (m + 1) * P].rearrange("p j t -> p t j"), SIGN)
-                nc.scalar.activation(piece, piece, RELU)
 
-        for n, b, number in ((0, 0, 5), (0, 1, 0), (0, 2, 4), (0, 3, 3), (1, 0, 2), (1, 1, 6), (1, 2, 1), (1, 3, 5)):
+        for n, b, number in ((0, 0, 2), (0, 1, 5), (0, 2, 0), (0, 3, 1), (1, 0, 3), (1, 1, 4), (1, 2, 6), (1, 3, 2)):
             t0, t1 = TOKEN_CHUNKS[n]
             tiles = (t1 - t0) // P
             gated = []
@@ -176,8 +182,9 @@ def tile_moe_sub_relu_kernel(
             da = held([P, width, 4], BF16, f"da{t0}")
             da_w = held([P, width], U32, f"da_w{t0}")
             da_s = held([P, width], U8, f"da_s{t0}")
+            nc.vector.tensor_scalar_max(mask[:], mask[:], 0.0)
             for c0 in range(0, width, 2 * P):
-                bank = psum_bank((7, 0, 4)[(t0 + c0) // (2 * P)], [P, 2, 2 * P])
+                bank = psum_bank((7, 0, 1)[(t0 + c0) // (2 * P)], [P, 2, 2 * P])
                 for m in range(2):
                     for u in range(2):
                         words = rounded[:, c0 // P + m, u].rearrange("t p e -> t (p e)").bitcast(F32)

@@ -42,7 +42,7 @@ def tile_moe_sub_relu_kernel(
         pos_sb = [keep.tile([P, T // 16], U16, name=f"pos{r}_sb") for r in range(2)]
         dy_s = held([P, T], U8, "dy_s")
         dy_w = [held([P, T], U32, f"dy_w{s}") for s in range(PASSES)]
-        w2_s = [held([P, E * PASSES, H // 2], U8, f"w2_s{h}") for h in range(2)]
+        w2_s = held([P, E * PASSES, H], U8, "w2_s")
         w2_w = held([P, E * PASSES, 2 * H], U8, "w2_w")
         w1_s = held([P, K], U8, "w1_s")
         w1_w = held([P, K], U32, "w1_w")
@@ -59,10 +59,10 @@ def tile_moe_sub_relu_kernel(
         nc.gpsimd.memset(dy_s[:].bitcast(I32), 0)
         nc.vector.memset(zeros[:], 0.0)
         nc.vector.memset(gate_rows[:], 0.0)
-        nc.vector.memset(w2_s[0][:].bitcast(I32), 0)
-        nc.vector.memset(w2_s[1][:].bitcast(I32), 0)
-        nc.gpsimd.memset(slot_s[1][:].bitcast(I32), 0)
-        nc.gpsimd.memset(w1_s[:].bitcast(I32), 0)
+        nc.gpsimd.memset(w2_s[:, 0:E].bitcast(I32), 0)
+        nc.vector.memset(w2_s[:, E : 2 * E].bitcast(I32), 0)
+        nc.vector.memset(slot_s[1][:].bitcast(I32), 0)
+        nc.vector.memset(w1_s[:].bitcast(I32), 0)
         nc.scalar.activation(ident[:], zeros[:], SIGN)
         make_identity(nc, ident[:], nomemset=True)
 
@@ -72,19 +72,14 @@ def tile_moe_sub_relu_kernel(
         for s in range(PASSES):
             nc.sync.dma_start(dy_w[s][:].bitcast(I32), dy_words[s].rearrange("p t d -> p (t d)").bitcast(I32))
         nc.sync.dma_start(gate_rows[0:8], gate.rearrange("r p (m n) -> (p m) r n", n=P)[0:8])
-
-        def load_w2_scales(h):
-            rows = w2t_scales.rearrange("e s b i -> b (e s) i")[:, :, H // 2 * h : H // 2 * (h + 1)]
-            for r in range(4):
-                nc.sync.dma_start(w2_s[h][r:P:32].bitcast(I32), rows[r:16:4].bitcast(I32))
-
-        load_w2_scales(0)
+        rows = w2t_scales.rearrange("e s b i -> b (e s) i")
+        for r in range(4):
+            nc.gpsimd.dma_start(w2_s[r:P:32].bitcast(I32), rows[r:16:4].bitcast(I32))
         for c, (e0, e1) in enumerate(WEIGHT_LOADS):
             words = w2t_words[e0:e1].rearrange("e s p x -> p (e s) x")
             nc.sync.dma_start(w2_w[:, e0 * PASSES : e1 * PASSES].bitcast(I32), words.bitcast(I32))
             if c in (2, 3):
                 nc.sync.dma_start(pos_sb[c - 2][:], (pos1, pos2)[c - 2])
-        load_w2_scales(1)
         for (t0, t1), saved in zip(TOKEN_CHUNKS, a_sb):
             nc.sync.dma_start(saved[:], a.rearrange("(p j) t -> p j t", j=4)[:, :, t0:t1])
         nc.sync.dma_start(w1_w[:].bitcast(I32), w1t_words[0].rearrange("p k d -> p (k d)").bitcast(I32))
@@ -127,7 +122,7 @@ def tile_moe_sub_relu_kernel(
                     nc.tensor.matmul_mx(
                         out=bank[:, (e - e0) * C : (e - e0 + 1) * C],
                         lhsT=w2_w[:, e * PASSES + s, 2 * P * b : 2 * P * (b + 1)].bitcast(FP4X4),
-                        lhsT_scale=w2_s[b // 2][:, e * PASSES + s, P * (b % 2) : P * (b % 2 + 1)],
+                        lhsT_scale=w2_s[:, e * PASSES + s, P * b : P * (b + 1)],
                         rhs=slot_w[s][:, cols].bitcast(FP8X4),
                         rhs_scale=slot_s[s][:, cols],
                         start=(s == 0),
@@ -140,23 +135,20 @@ def tile_moe_sub_relu_kernel(
                 gather_words(e0, e1, s)
         for (e0, e1), number in zip(EXPERT_UNITS, (0, 1, 2, 3)):
             experts_product(e0, e1, 0, number)
-        for b, numbers in ((1, (4, 5, 6)), (2, (0, 1, 2)), (3, (3, 4, 5))):
+        for b, numbers in ((1, (4, 5, 6)), (2, (0, 2, 3)), (3, (6, 2, 3))):
             for c, number in enumerate(numbers):
                 experts_product(4 * c, 4 * c + 4, b, number)
 
         dh_t = [held([P, (t1 - t0) // P, 2, P, 2], BF16, f"dh_t{t0}") for t0, t1 in TOKEN_CHUNKS]
-        relu_on = [held([P, t1 - t0, 4], BF16, f"mask{t0}") for t0, t1 in TOKEN_CHUNKS]
-        for n, (t0, t1) in enumerate(TOKEN_CHUNKS):
-            for m in range((t1 - t0) // P):
-                piece = relu_on[n][:, m * P : (m + 1) * P, :]
-                nc.scalar.activation(piece, a_sb[n][:, :, m * P : (m + 1) * P].rearrange("p j t -> p t j"), SIGN)
-
-        for n, b, number in ((0, 0, 2), (0, 1, 5), (0, 2, 0), (0, 3, 1), (1, 0, 3), (1, 1, 4), (1, 2, 6), (1, 3, 2)):
+        for n, b, number in ((0, 0, 0), (0, 1, 1), (0, 2, 4), (0, 3, 5), (1, 0, 0), (1, 1, 1), (1, 2, 4), (1, 3, 5)):
             t0, t1 = TOKEN_CHUNKS[n]
             tiles = (t1 - t0) // P
             gated = []
             for r in range(2):
-                u = ring.tile([P, t1 - t0], F32, name="gated", tag="gated")
+                if (n, b) == (0, 0):
+                    u = ring.tile([P, t1 - t0], F32, name="first", tag="first", bufs=2, align_bytes=64)
+                else:
+                    u = ring.tile([P, t1 - t0], F32, name="gated", tag="gated")
                 nc.vector.tensor_tensor(
                     u[:], y[b][:].indirect(pos_sb[r][:, t0 // 16 : t1 // 16]), gate_sb[n][:, r, :], MULT
                 )
@@ -177,6 +169,14 @@ def tile_moe_sub_relu_kernel(
                 bank[:].rearrange("t m (p u e) -> t m u p e", u=2, e=2),
             )
 
+        relu_on = [
+            ring.tile([P, t1 - t0, 4], BF16, name="first", tag="first", bufs=2, align_bytes=64) for t0, t1 in TOKEN_CHUNKS
+        ]
+        for n, (t0, t1) in enumerate(TOKEN_CHUNKS):
+            for m in range((t1 - t0) // P):
+                piece = relu_on[n][:, m * P : (m + 1) * P, :]
+                nc.scalar.activation(piece, a_sb[n][:, :, m * P : (m + 1) * P].rearrange("p j t -> p t j"), SIGN)
+
         for (t0, t1), rounded, mask in zip(TOKEN_CHUNKS, dh_t, relu_on):
             width = t1 - t0
             da = held([P, width, 4], BF16, f"da{t0}")
@@ -184,7 +184,7 @@ def tile_moe_sub_relu_kernel(
             da_s = held([P, width], U8, f"da_s{t0}")
             nc.vector.tensor_scalar_max(mask[:], mask[:], 0.0)
             for c0 in range(0, width, 2 * P):
-                bank = psum_bank((7, 0, 1)[(t0 + c0) // (2 * P)], [P, 2, 2 * P])
+                bank = psum_bank((7, 3, 2)[(t0 + c0) // (2 * P)], [P, 2, 2 * P])
                 for m in range(2):
                     for u in range(2):
                         words = rounded[:, c0 // P + m, u].rearrange("t p e -> t (p e)").bitcast(F32)
@@ -196,7 +196,7 @@ def tile_moe_sub_relu_kernel(
                     MULT,
                 )
             nc.vector.quantize_mx(da_w[:].bitcast(FP8X4), da_s[:], da[:].rearrange("p t j -> p (t j)"))
-            bank = psum_bank(3 if t0 == 0 else 7, [P, width])
+            bank = psum_bank(6 if t0 == 0 else 7, [P, width])
             nc.tensor.matmul_mx(
                 out=bank[:],
                 lhsT=w1_w[:].bitcast(FP8X4),

@@ -22,7 +22,6 @@ SLOTS = E * C
 PASSES = N // 512
 ROW_TILES = H // P
 EXPERT_UNITS = ((0, 4), (4, 8), (8, 11), (11, 12))
-WEIGHT_LOADS = ((0, 2), (2, 4), (4, 6), (6, 8), (8, 10), (10, 11), (11, 12))
 TOKEN_CHUNKS = ((0, 512), (512, 768))
 
 
@@ -32,59 +31,52 @@ def tile_moe_sub_relu_kernel(
     nc = tc.nc
     with ExitStack() as ctx:
         keep = ctx.enter_context(tc.tile_pool(name="keep", bufs=1))
-        ring = ctx.enter_context(tc.tile_pool(name="ring", bufs=10))
+        ring = ctx.enter_context(tc.tile_pool(name="ring", bufs=14))
         psum = ctx.enter_context(tc.psum_pool(name="psum", bufs=1))
 
         def held(shape, dtype, name):
             return keep.tile(shape, dtype, name=name, align_bytes=64)
 
+        def late(shape, dtype, name, tag):
+            return keep.tile(shape, dtype, name=name, tag=tag, align_bytes=64)
+
         offs_sb = keep.tile([P, SLOTS // 16], U16, name="offs_sb")
         pos_sb = [keep.tile([P, T // 16], U16, name=f"pos{r}_sb") for r in range(2)]
-        dy_s = held([P, T], U8, "dy_s")
-        dy_w = [held([P, T], U32, f"dy_w{s}") for s in range(PASSES)]
+        dy_s = late([P, T], U8, "dy_s", "then_w1_s")
+        dy_w = late([P, PASSES, T], U32, "dy_w", "then_w1_w")
         w2_s = held([P, E * PASSES, H], U8, "w2_s")
         w2_w = held([P, E * PASSES, 2 * H], U8, "w2_w")
-        w1_s = held([P, K], U8, "w1_s")
-        w1_w = held([P, K], U32, "w1_w")
-        slot_s = [held([P, SLOTS], U8, f"slot_s{s}") for s in range(PASSES)]
+        slot_rows = late([P, SLOTS], U8, "slot_rows", "then_a")
+        slot_s = held([P, PASSES, SLOTS], U8, "slot_s")
         slot_w = [held([P, SLOTS], U32, f"slot_w{s}") for s in range(PASSES)]
         y = [held([P, SLOTS], F32, f"y{b}") for b in range(ROW_TILES)]
-        gate_sb = [held([P, 2, t1 - t0], F32, f"gate_sb{t0}") for t0, t1 in TOKEN_CHUNKS]
-        a_sb = [held([P, 4, t1 - t0], F32, f"a_sb{t0}") for t0, t1 in TOKEN_CHUNKS]
+        gate_sb = held([P, 2, T], F32, "gate_sb")
         gate_rows = held([P, 2, P], F32, "gate_rows")
         gate_cols = held([P, 2, 8], F32, "gate_cols")
         zeros = held([P, P], F32, "zeros")
         ident = held([P, P], F32, "ident")
 
-        nc.gpsimd.memset(dy_s[:].bitcast(I32), 0)
+        nc.gpsimd.memset(gate_rows[:], 0.0)
         nc.vector.memset(zeros[:], 0.0)
-        nc.vector.memset(gate_rows[:], 0.0)
-        nc.gpsimd.memset(w2_s[:, 0:E].bitcast(I32), 0)
-        nc.vector.memset(w2_s[:, E : 2 * E].bitcast(I32), 0)
-        nc.vector.memset(slot_s[1][:].bitcast(I32), 0)
-        nc.vector.memset(w1_s[:].bitcast(I32), 0)
+        nc.vector.memset(w2_s[:].bitcast(I32), 0)
+        nc.vector.memset(dy_s[32:64].bitcast(I32), 0)
+        nc.vector.memset(dy_s[64:128].bitcast(I32), 0)
+        nc.vector.memset(slot_s[:].bitcast(I32), 0)
         nc.scalar.activation(ident[:], zeros[:], SIGN)
-        make_identity(nc, ident[:], nomemset=True)
 
         nc.sync.dma_start(offs_sb[:], offs)
-        for q in range(4):
-            nc.sync.dma_start(dy_s[32 * q : 32 * q + 8, :].bitcast(I32), dy_scales[:, 4 * q : 4 * q + 4, :].bitcast(I32))
-        for s in range(PASSES):
-            nc.sync.dma_start(dy_w[s][:].bitcast(I32), dy_words[s].rearrange("p t d -> p (t d)").bitcast(I32))
-        nc.sync.dma_start(gate_rows[0:8], gate.rearrange("r p (m n) -> (p m) r n", n=P)[0:8])
+        nc.sync.dma_start(dy_s[0:32].bitcast(I32), dy_scales.rearrange("s b t -> b s t").bitcast(I32))
+        nc.sync.dma_start(dy_w[:].bitcast(I32), dy_words.rearrange("s p t d -> p s (t d)").bitcast(I32))
+        for r in range(2):
+            nc.sync.dma_start(pos_sb[r][:], (pos1, pos2)[r])
+        for e0, e1 in EXPERT_UNITS:
+            words = w2t_words[e0:e1].rearrange("e s p x -> p (e s) x")
+            nc.sync.dma_start(w2_w[:, e0 * PASSES : e1 * PASSES].bitcast(I32), words.bitcast(I32))
+        nc.gpsimd.dma_start(gate_rows[0 : T // P], gate[:, 0, :].rearrange("r (m n) -> m r n", n=P))
         rows = w2t_scales.rearrange("e s b i -> b (e s) i")
         for r in range(4):
             nc.gpsimd.dma_start(w2_s[r:P:32].bitcast(I32), rows[r:16:4].bitcast(I32))
-        for c, (e0, e1) in enumerate(WEIGHT_LOADS):
-            words = w2t_words[e0:e1].rearrange("e s p x -> p (e s) x")
-            nc.sync.dma_start(w2_w[:, e0 * PASSES : e1 * PASSES].bitcast(I32), words.bitcast(I32))
-            if c in (2, 3):
-                nc.sync.dma_start(pos_sb[c - 2][:], (pos1, pos2)[c - 2])
-        for (t0, t1), saved in zip(TOKEN_CHUNKS, a_sb):
-            nc.sync.dma_start(saved[:], a.rearrange("(p j) t -> p j t", j=4)[:, :, t0:t1])
-        nc.sync.dma_start(w1_w[:].bitcast(I32), w1t_words[0].rearrange("p k d -> p (k d)").bitcast(I32))
-        for q in range(4):
-            nc.sync.dma_start(w1_s[32 * q : 32 * q + 4, :].bitcast(I32), w1t_scales[0, 4 * q : 4 * q + 4, :].bitcast(I32))
+        make_identity(nc, ident[:], nomemset=True)
 
         def psum_bank(number, shape):
             return psum.tile(shape, F32, name=f"bank{number}", tag=f"bank{number}")
@@ -93,26 +85,33 @@ def tile_moe_sub_relu_kernel(
         for r in range(2):
             nc.tensor.transpose(bank[:, r, :], gate_rows[:, r, :], ident[:])
         nc.scalar.copy(gate_cols[:], bank[:, :, 0:8])
-        spread = [(0, 0, 4), (0, 1, 5), (1, None, 6)]
-        for n, only, number in spread:
-            t0, t1 = TOKEN_CHUNKS[n]
-            rs = range(2) if only is None else (only,)
-            bank = psum_bank(number, [P, len(rs), t1 - t0])
-            for x, r in enumerate(rs):
-                for m in range((t1 - t0) // P):
-                    column = gate_cols[:, r, t0 // P + m : t0 // P + m + 1].to_broadcast([P, P])
-                    nc.tensor.transpose(bank[:, x, m * P : (m + 1) * P], column, ident[:])
-            nc.scalar.copy(gate_sb[n][:, rs[0] : rs[-1] + 1, :], bank[:])
-
-        def gather_words(e0, e1, s):
-            nc.vector.tensor_copy(
-                slot_w[s][:, e0 * C : e1 * C], dy_w[s][:].indirect(offs_sb[:, e0 * C // 16 : e1 * C // 16])
-            )
+        gate_flat = gate_sb[:].rearrange("p r t -> p (r t)")
+        for third in range(3):
+            bank = psum_bank(4 + third, [P, 4, P])
+            for x in range(4):
+                r, m = divmod(4 * third + x, T // P)
+                nc.tensor.transpose(bank[:, x, :], gate_cols[:, r, m : m + 1].to_broadcast([P, P]), ident[:])
+            nc.scalar.copy(gate_flat[:, 512 * third : 512 * (third + 1)], bank[:].rearrange("p x n -> p (x n)"))
 
         for j0 in range(0, SLOTS, 512):
-            nc.vector.tensor_copy(slot_s[0][:, j0 : j0 + 512], dy_s[:].indirect(offs_sb[:, j0 // 16 : (j0 + 512) // 16]))
-        nc.scalar.dma_start(slot_s[1][0:112, :].bitcast(I32), slot_s[0][4:116, :].bitcast(I32))
+            nc.vector.tensor_copy(slot_rows[:, j0 : j0 + 512], dy_s[:].indirect(offs_sb[:, j0 // 16 : (j0 + 512) // 16]))
+        for q in range(4):
+            nc.scalar.dma_start(slot_s[32 * q : 32 * q + 4].bitcast(I32), slot_rows[8 * q : 8 * q + 8, :].bitcast(I32))
 
+        for e0, e1 in EXPERT_UNITS:
+            for s in range(PASSES):
+                nc.vector.tensor_copy(
+                    slot_w[s][:, e0 * C : e1 * C], dy_w[:, s, :].indirect(offs_sb[:, e0 * C // 16 : e1 * C // 16])
+                )
+
+        a_sb = late([P, 4, T], F32, "a_sb", "then_a")
+        nc.sync.dma_start(a_sb[:], a.rearrange("(p j) t -> p j t", j=4))
+        w1_w = late([P, K], U32, "w1_w", "then_w1_w")
+        w1_s = late([P, K], U8, "w1_s", "then_w1_s")
+        nc.vector.memset(w1_s[:].bitcast(I32), 0)
+        nc.sync.dma_start(w1_w[:].bitcast(I32), w1t_words[0].rearrange("p k d -> p (k d)").bitcast(I32))
+        for q in range(4):
+            nc.sync.dma_start(w1_s[32 * q : 32 * q + 4, :].bitcast(I32), w1t_scales[0, 4 * q : 4 * q + 4, :].bitcast(I32))
 
         def experts_product(e0, e1, b, number):
             bank = psum_bank(number, [P, (e1 - e0) * C])
@@ -124,23 +123,19 @@ def tile_moe_sub_relu_kernel(
                         lhsT=w2_w[:, e * PASSES + s, 2 * P * b : 2 * P * (b + 1)].bitcast(FP4X4),
                         lhsT_scale=w2_s[:, e * PASSES + s, P * b : P * (b + 1)],
                         rhs=slot_w[s][:, cols].bitcast(FP8X4),
-                        rhs_scale=slot_s[s][:, cols],
+                        rhs_scale=slot_s[:, s, cols],
                         start=(s == 0),
                         stop=(s == PASSES - 1),
                     )
             nc.scalar.copy(y[b][:, e0 * C : e1 * C], bank[:])
 
-        for e0, e1 in EXPERT_UNITS:
-            for s in range(PASSES):
-                gather_words(e0, e1, s)
-        for (e0, e1), number in zip(EXPERT_UNITS, (0, 1, 2, 3)):
-            experts_product(e0, e1, 0, number)
-        for b, numbers in ((1, (4, 5, 6)), (2, (0, 2, 3)), (3, (6, 2, 3))):
-            for c, number in enumerate(numbers):
-                experts_product(4 * c, 4 * c + 4, b, number)
+        units = [(0, 4, b) for b in range(4)] + [(4, 8, 0), (4, 8, 1), (8, 11, 0), (11, 12, 0), (8, 12, 1)]
+        units = units + [(e0, e0 + 4, b) for b in (2, 3) for e0 in (4, 8)]
+        for place, (e0, e1, b) in enumerate(units):
+            experts_product(e0, e1, b, place % 8)
 
         dh_t = [held([P, (t1 - t0) // P, 2, P, 2], BF16, f"dh_t{t0}") for t0, t1 in TOKEN_CHUNKS]
-        for n, b, number in ((0, 0, 0), (0, 1, 1), (0, 2, 4), (0, 3, 5), (1, 0, 0), (1, 1, 1), (1, 2, 4), (1, 3, 5)):
+        for n, b, number in ((0, 0, 4), (1, 0, 3), (0, 1, 2), (0, 2, 1), (0, 3, 0), (1, 1, 4), (1, 2, 3), (1, 3, 2)):
             t0, t1 = TOKEN_CHUNKS[n]
             tiles = (t1 - t0) // P
             gated = []
@@ -150,7 +145,7 @@ def tile_moe_sub_relu_kernel(
                 else:
                     u = ring.tile([P, t1 - t0], F32, name="gated", tag="gated")
                 nc.vector.tensor_tensor(
-                    u[:], y[b][:].indirect(pos_sb[r][:, t0 // 16 : t1 // 16]), gate_sb[n][:, r, :], MULT
+                    u[:], y[b][:].indirect(pos_sb[r][:, t0 // 16 : t1 // 16]), gate_sb[:, r, t0:t1], MULT
                 )
                 gated.append(u)
             bank = psum_bank(number, [P, tiles, P])
@@ -175,7 +170,7 @@ def tile_moe_sub_relu_kernel(
         for n, (t0, t1) in enumerate(TOKEN_CHUNKS):
             for m in range((t1 - t0) // P):
                 piece = relu_on[n][:, m * P : (m + 1) * P, :]
-                nc.scalar.activation(piece, a_sb[n][:, :, m * P : (m + 1) * P].rearrange("p j t -> p t j"), SIGN)
+                nc.scalar.activation(piece, a_sb[:, :, t0 + m * P : t0 + (m + 1) * P].rearrange("p j t -> p t j"), SIGN)
 
         for (t0, t1), rounded, mask in zip(TOKEN_CHUNKS, dh_t, relu_on):
             width = t1 - t0
@@ -184,7 +179,7 @@ def tile_moe_sub_relu_kernel(
             da_s = held([P, width], U8, f"da_s{t0}")
             nc.vector.tensor_scalar_max(mask[:], mask[:], 0.0)
             for c0 in range(0, width, 2 * P):
-                bank = psum_bank((7, 3, 2)[(t0 + c0) // (2 * P)], [P, 2, 2 * P])
+                bank = psum_bank((5, 6, 7)[(t0 + c0) // (2 * P)], [P, 2, 2 * P])
                 for m in range(2):
                     for u in range(2):
                         words = rounded[:, c0 // P + m, u].rearrange("t p e -> t (p e)").bitcast(F32)
@@ -196,7 +191,7 @@ def tile_moe_sub_relu_kernel(
                     MULT,
                 )
             nc.vector.quantize_mx(da_w[:].bitcast(FP8X4), da_s[:], da[:].rearrange("p t j -> p (t j)"))
-            bank = psum_bank(6 if t0 == 0 else 7, [P, width])
+            bank = psum_bank(1 if t0 == 0 else 0, [P, width])
             nc.tensor.matmul_mx(
                 out=bank[:],
                 lhsT=w1_w[:].bitcast(FP8X4),

@@ -31,7 +31,6 @@ def tile_moe_sub_relu_kernel(
     nc = tc.nc
     with ExitStack() as ctx:
         keep = ctx.enter_context(tc.tile_pool(name="keep", bufs=1))
-        ring = ctx.enter_context(tc.tile_pool(name="ring", bufs=14))
         psum = ctx.enter_context(tc.psum_pool(name="psum", bufs=1))
 
         def held(shape, dtype, name):
@@ -42,41 +41,46 @@ def tile_moe_sub_relu_kernel(
 
         offs_sb = keep.tile([P, SLOTS // 16], U16, name="offs_sb")
         pos_sb = [keep.tile([P, T // 16], U16, name=f"pos{r}_sb") for r in range(2)]
-        dy_s = late([P, T], U8, "dy_s", "then_w1_s")
-        dy_w = late([P, PASSES, T], U32, "dy_w", "then_w1_w")
-        w2_s = held([P, E * PASSES, H], U8, "w2_s")
-        w2_w = held([P, E * PASSES, 2 * H], U8, "w2_w")
-        slot_rows = late([P, SLOTS], U8, "slot_rows", "then_a")
-        slot_s = held([P, PASSES, SLOTS], U8, "slot_s")
-        slot_w = [held([P, SLOTS], U32, f"slot_w{s}") for s in range(PASSES)]
+        dy_s = late([P, T], U8, "dy_s", "then_w2_s1")
+        dy_w = late([P, PASSES, T], U32, "dy_w", "then_a")
+        slot_s = [late([P, SLOTS], U8, f"slot_s{s}", f"slot_s{s}_then_w1_w") for s in range(PASSES)]
+        slot_w = [late([P, SLOTS], U32, f"slot_w{s}", f"then_relu{s}") for s in range(PASSES)]
         y = [held([P, SLOTS], F32, f"y{b}") for b in range(ROW_TILES)]
         gate_sb = held([P, 2, T], F32, "gate_sb")
         gate_rows = held([P, 2, P], F32, "gate_rows")
-        gate_cols = held([P, 2, 8], F32, "gate_cols")
-        zeros = held([P, P], F32, "zeros")
+        gate_cols = late([P, 2, 8], F32, "gate_cols", "then_w2_w1")
+        zeros = late([P, P], F32, "zeros", "then_w2_w0")
         ident = held([P, P], F32, "ident")
+        w2_words = w2t_words.rearrange("e s p x -> p (e s) x")
+        w2_rows = w2t_scales.rearrange("e s b i -> b (e s) i")
 
+        def load_w2_scales(plane, half):
+            for r in range(4):
+                nc.sync.dma_start(plane[r:P:32].bitcast(I32), w2_rows[r:16:4, :, 2 * P * half : 2 * P * (half + 1)].bitcast(I32))
+
+        def load_w2_words(half):
+            words = late([P, E * PASSES, H], U8, f"w2_w{half}", f"then_w2_w{half}")
+            nc.sync.dma_start(words[:].bitcast(I32), w2_words[:, :, H * half : H * (half + 1)].bitcast(I32))
+            return words
+
+        w2_s = [late([P, E * PASSES, 2 * P], U8, "w2_s0", "then_w1_s")]
+        nc.gpsimd.memset(dy_s[:].bitcast(I32), 0)
         nc.gpsimd.memset(gate_rows[:], 0.0)
         nc.vector.memset(zeros[:], 0.0)
-        nc.vector.memset(w2_s[:].bitcast(I32), 0)
-        nc.vector.memset(dy_s[32:64].bitcast(I32), 0)
-        nc.vector.memset(dy_s[64:128].bitcast(I32), 0)
-        nc.vector.memset(slot_s[:].bitcast(I32), 0)
+        nc.vector.memset(w2_s[0][:].bitcast(I32), 0)
+        nc.vector.memset(slot_s[1][:].bitcast(I32), 0)
         nc.scalar.activation(ident[:], zeros[:], SIGN)
+        make_identity(nc, ident[:], nomemset=True)
 
         nc.sync.dma_start(offs_sb[:], offs)
-        nc.sync.dma_start(dy_s[0:32].bitcast(I32), dy_scales.rearrange("s b t -> b s t").bitcast(I32))
-        nc.sync.dma_start(dy_w[:].bitcast(I32), dy_words.rearrange("s p t d -> p s (t d)").bitcast(I32))
+        for q in range(4):
+            nc.sync.dma_start(dy_s[32 * q : 32 * q + 8, :].bitcast(I32), dy_scales[:, 4 * q : 4 * q + 4, :].bitcast(I32))
         for r in range(2):
             nc.sync.dma_start(pos_sb[r][:], (pos1, pos2)[r])
-        for e0, e1 in EXPERT_UNITS:
-            words = w2t_words[e0:e1].rearrange("e s p x -> p (e s) x")
-            nc.sync.dma_start(w2_w[:, e0 * PASSES : e1 * PASSES].bitcast(I32), words.bitcast(I32))
-        nc.gpsimd.dma_start(gate_rows[0 : T // P], gate[:, 0, :].rearrange("r (m n) -> m r n", n=P))
-        rows = w2t_scales.rearrange("e s b i -> b (e s) i")
-        for r in range(4):
-            nc.gpsimd.dma_start(w2_s[r:P:32].bitcast(I32), rows[r:16:4].bitcast(I32))
-        make_identity(nc, ident[:], nomemset=True)
+        nc.sync.dma_start(dy_w[:].bitcast(I32), dy_words.rearrange("s p t d -> p s (t d)").bitcast(I32))
+        nc.sync.dma_start(gate_rows[0:8], gate.rearrange("r p (m n) -> (p m) r n", n=P)[0:8])
+        load_w2_scales(w2_s[0], 0)
+        w2_w = [load_w2_words(0)]
 
         def psum_bank(number, shape):
             return psum.tile(shape, F32, name=f"bank{number}", tag=f"bank{number}")
@@ -94,9 +98,12 @@ def tile_moe_sub_relu_kernel(
             nc.scalar.copy(gate_flat[:, 512 * third : 512 * (third + 1)], bank[:].rearrange("p x n -> p (x n)"))
 
         for j0 in range(0, SLOTS, 512):
-            nc.vector.tensor_copy(slot_rows[:, j0 : j0 + 512], dy_s[:].indirect(offs_sb[:, j0 // 16 : (j0 + 512) // 16]))
-        for q in range(4):
-            nc.scalar.dma_start(slot_s[32 * q : 32 * q + 4].bitcast(I32), slot_rows[8 * q : 8 * q + 8, :].bitcast(I32))
+            nc.vector.tensor_copy(slot_s[0][:, j0 : j0 + 512], dy_s[:].indirect(offs_sb[:, j0 // 16 : (j0 + 512) // 16]))
+        nc.scalar.dma_start(slot_s[1][0:112, :].bitcast(I32), slot_s[0][4:116, :].bitcast(I32))
+        w2_w.append(load_w2_words(1))
+        w2_s.append(late([P, E * PASSES, 2 * P], U8, "w2_s1", "then_w2_s1"))
+        nc.gpsimd.memset(w2_s[1][:].bitcast(I32), 0)
+        load_w2_scales(w2_s[1], 1)
 
         for e0, e1 in EXPERT_UNITS:
             for s in range(PASSES):
@@ -106,44 +113,32 @@ def tile_moe_sub_relu_kernel(
 
         a_sb = late([P, 4, T], F32, "a_sb", "then_a")
         nc.sync.dma_start(a_sb[:], a.rearrange("(p j) t -> p j t", j=4))
-        w1_w = late([P, K], U32, "w1_w", "then_w1_w")
-        w1_s = late([P, K], U8, "w1_s", "then_w1_s")
-        nc.vector.memset(w1_s[:].bitcast(I32), 0)
-        nc.sync.dma_start(w1_w[:].bitcast(I32), w1t_words[0].rearrange("p k d -> p (k d)").bitcast(I32))
-        for q in range(4):
-            nc.sync.dma_start(w1_s[32 * q : 32 * q + 4, :].bitcast(I32), w1t_scales[0, 4 * q : 4 * q + 4, :].bitcast(I32))
 
         def experts_product(e0, e1, b, number):
+            half, part = divmod(b, 2)
             bank = psum_bank(number, [P, (e1 - e0) * C])
             for e in range(e0, e1):
                 cols = slice(e * C, (e + 1) * C)
                 for s in range(PASSES):
                     nc.tensor.matmul_mx(
                         out=bank[:, (e - e0) * C : (e - e0 + 1) * C],
-                        lhsT=w2_w[:, e * PASSES + s, 2 * P * b : 2 * P * (b + 1)].bitcast(FP4X4),
-                        lhsT_scale=w2_s[:, e * PASSES + s, P * b : P * (b + 1)],
+                        lhsT=w2_w[half][:, e * PASSES + s, 2 * P * part : 2 * P * (part + 1)].bitcast(FP4X4),
+                        lhsT_scale=w2_s[half][:, e * PASSES + s, P * part : P * (part + 1)],
                         rhs=slot_w[s][:, cols].bitcast(FP8X4),
-                        rhs_scale=slot_s[:, s, cols],
+                        rhs_scale=slot_s[s][:, cols],
                         start=(s == 0),
                         stop=(s == PASSES - 1),
                     )
             nc.scalar.copy(y[b][:, e0 * C : e1 * C], bank[:])
 
-        units = [(0, 4, b) for b in range(4)] + [(4, 8, 0), (4, 8, 1), (8, 11, 0), (11, 12, 0), (8, 12, 1)]
-        units = units + [(e0, e0 + 4, b) for b in (2, 3) for e0 in (4, 8)]
-        for place, (e0, e1, b) in enumerate(units):
-            experts_product(e0, e1, b, place % 8)
-
         dh_t = [held([P, (t1 - t0) // P, 2, P, 2], BF16, f"dh_t{t0}") for t0, t1 in TOKEN_CHUNKS]
-        for n, b, number in ((0, 0, 4), (1, 0, 3), (0, 1, 2), (0, 2, 1), (0, 3, 0), (1, 1, 4), (1, 2, 3), (1, 3, 2)):
+
+        def token_step(n, b, number):
             t0, t1 = TOKEN_CHUNKS[n]
             tiles = (t1 - t0) // P
             gated = []
             for r in range(2):
-                if (n, b) == (0, 0):
-                    u = ring.tile([P, t1 - t0], F32, name="first", tag="first", bufs=2, align_bytes=64)
-                else:
-                    u = ring.tile([P, t1 - t0], F32, name="gated", tag="gated")
+                u = held([P, t1 - t0], F32, f"gated{n}{b}{r}")
                 nc.vector.tensor_tensor(
                     u[:], y[b][:].indirect(pos_sb[r][:, t0 // 16 : t1 // 16]), gate_sb[:, r, t0:t1], MULT
                 )
@@ -164,8 +159,25 @@ def tile_moe_sub_relu_kernel(
                 bank[:].rearrange("t m (p u e) -> t m u p e", u=2, e=2),
             )
 
+        units = [(0, 4, 0), (0, 4, 1), (4, 8, 0), (4, 8, 1), (8, 11, 0), (11, 12, 0), (8, 12, 1)]
+        for number, (e0, e1, b) in enumerate(units):
+            experts_product(e0, e1, b, number)
+        token_step(0, 0, 7)
+        for number in range(6):
+            experts_product(4 * (number % 3), 4 * (number % 3) + 4, 2 + number // 3, number)
+
+        w1_s = late([P, K], U8, "w1_s", "then_w1_s")
+        nc.gpsimd.memset(w1_s[:].bitcast(I32), 0)
+        for q in range(4):
+            nc.sync.dma_start(w1_s[32 * q : 32 * q + 4, :].bitcast(I32), w1t_scales[0, 4 * q : 4 * q + 4, :].bitcast(I32))
+        w1_w = late([P, K], U32, "w1_w", "slot_s0_then_w1_w")
+        nc.sync.dma_start(w1_w[:].bitcast(I32), w1t_words[0].rearrange("p k d -> p (k d)").bitcast(I32))
+
+        for n, b, number in ((1, 0, 5), (0, 1, 4), (1, 1, 3), (0, 2, 2), (0, 3, 1), (1, 2, 0), (1, 3, 6)):
+            token_step(n, b, number)
+
         relu_on = [
-            ring.tile([P, t1 - t0, 4], BF16, name="first", tag="first", bufs=2, align_bytes=64) for t0, t1 in TOKEN_CHUNKS
+            late([P, t1 - t0, 4], BF16, f"relu_on{n}", f"then_relu{n}") for n, (t0, t1) in enumerate(TOKEN_CHUNKS)
         ]
         for n, (t0, t1) in enumerate(TOKEN_CHUNKS):
             for m in range((t1 - t0) // P):
@@ -179,7 +191,7 @@ def tile_moe_sub_relu_kernel(
             da_s = held([P, width], U8, f"da_s{t0}")
             nc.vector.tensor_scalar_max(mask[:], mask[:], 0.0)
             for c0 in range(0, width, 2 * P):
-                bank = psum_bank((5, 6, 7)[(t0 + c0) // (2 * P)], [P, 2, 2 * P])
+                bank = psum_bank((7, 5, 4)[(t0 + c0) // (2 * P)], [P, 2, 2 * P])
                 for m in range(2):
                     for u in range(2):
                         words = rounded[:, c0 // P + m, u].rearrange("t p e -> t (p e)").bitcast(F32)
@@ -191,7 +203,7 @@ def tile_moe_sub_relu_kernel(
                     MULT,
                 )
             nc.vector.quantize_mx(da_w[:].bitcast(FP8X4), da_s[:], da[:].rearrange("p t j -> p (t j)"))
-            bank = psum_bank(1 if t0 == 0 else 0, [P, width])
+            bank = psum_bank(3 if t0 == 0 else 2, [P, width])
             nc.tensor.matmul_mx(
                 out=bank[:],
                 lhsT=w1_w[:].bitcast(FP8X4),

@@ -41,15 +41,15 @@ def tile_moe_sub_relu_kernel(
 
         offs_sb = keep.tile([P, SLOTS // 16], U16, name="offs_sb")
         pos_sb = [keep.tile([P, T // 16], U16, name=f"pos{r}_sb") for r in range(2)]
-        dy_s = late([P, T], U8, "dy_s", "then_w2_s1")
-        dy_w = late([P, PASSES, T], U32, "dy_w", "then_a")
+        dy_s = held([P, T], U8, "dy_s")
+        dy_w = held([P, PASSES, T], U32, "dy_w")
         slot_s = [late([P, SLOTS], U8, f"slot_s{s}", f"slot_s{s}_then_w1_w") for s in range(PASSES)]
         slot_w = [late([P, SLOTS], U32, f"slot_w{s}", f"then_relu{s}") for s in range(PASSES)]
         y = [held([P, SLOTS], F32, f"y{b}") for b in range(ROW_TILES)]
         gate_sb = held([P, 2, T], F32, "gate_sb")
         gate_rows = held([P, 2, P], F32, "gate_rows")
         gate_cols = late([P, 2, 8], F32, "gate_cols", "then_w2_w1")
-        zeros = late([P, P], F32, "zeros", "then_w2_w0")
+        zeros = late([P, 2 * P], F32, "zeros", "then_w2_w0")
         ident = held([P, P], F32, "ident")
         w2_words = w2t_words.rearrange("e s p x -> p (e s) x")
         w2_rows = w2t_scales.rearrange("e s b i -> b (e s) i")
@@ -65,12 +65,13 @@ def tile_moe_sub_relu_kernel(
 
         w2_s = [late([P, E * PASSES, 2 * P], U8, "w2_s0", "then_w1_s")]
         nc.gpsimd.memset(dy_s[:].bitcast(I32), 0)
-        nc.gpsimd.memset(gate_rows[:], 0.0)
+        make_identity(nc, ident[:])
         nc.vector.memset(zeros[:], 0.0)
         nc.vector.memset(w2_s[0][:].bitcast(I32), 0)
         nc.vector.memset(slot_s[1][:].bitcast(I32), 0)
-        nc.scalar.activation(ident[:], zeros[:], SIGN)
-        make_identity(nc, ident[:], nomemset=True)
+        w2_s.append(held([P, E * PASSES, 2 * P], U8, "w2_s1"))
+        nc.vector.memset(w2_s[1][:].bitcast(I32), 0)
+        nc.scalar.activation(gate_rows[:].rearrange("p r n -> p (r n)"), zeros[:], SIGN)
 
         nc.sync.dma_start(offs_sb[:], offs)
         for q in range(4):
@@ -100,19 +101,14 @@ def tile_moe_sub_relu_kernel(
         for j0 in range(0, SLOTS, 512):
             nc.vector.tensor_copy(slot_s[0][:, j0 : j0 + 512], dy_s[:].indirect(offs_sb[:, j0 // 16 : (j0 + 512) // 16]))
         nc.scalar.dma_start(slot_s[1][0:112, :].bitcast(I32), slot_s[0][4:116, :].bitcast(I32))
-        w2_w.append(load_w2_words(1))
-        w2_s.append(late([P, E * PASSES, 2 * P], U8, "w2_s1", "then_w2_s1"))
-        nc.gpsimd.memset(w2_s[1][:].bitcast(I32), 0)
         load_w2_scales(w2_s[1], 1)
+        w2_w.append(load_w2_words(1))
 
         for e0, e1 in EXPERT_UNITS:
             for s in range(PASSES):
                 nc.vector.tensor_copy(
                     slot_w[s][:, e0 * C : e1 * C], dy_w[:, s, :].indirect(offs_sb[:, e0 * C // 16 : e1 * C // 16])
                 )
-
-        a_sb = late([P, 4, T], F32, "a_sb", "then_a")
-        nc.sync.dma_start(a_sb[:], a.rearrange("(p j) t -> p j t", j=4))
 
         def experts_product(e0, e1, b, number):
             half, part = divmod(b, 2)
@@ -162,12 +158,14 @@ def tile_moe_sub_relu_kernel(
         units = [(0, 4, 0), (0, 4, 1), (4, 8, 0), (4, 8, 1), (8, 11, 0), (11, 12, 0), (8, 12, 1)]
         for number, (e0, e1, b) in enumerate(units):
             experts_product(e0, e1, b, number)
+        a_sb = late([P, 4, T], F32, "a_sb", "then_w2_w0")
+        nc.sync.dma_start(a_sb[:], a.rearrange("(p j) t -> p j t", j=4))
         token_step(0, 0, 7)
         for number in range(6):
             experts_product(4 * (number % 3), 4 * (number % 3) + 4, 2 + number // 3, number)
 
         w1_s = late([P, K], U8, "w1_s", "then_w1_s")
-        nc.gpsimd.memset(w1_s[:].bitcast(I32), 0)
+        nc.vector.memset(w1_s[:].bitcast(I32), 0)
         for q in range(4):
             nc.sync.dma_start(w1_s[32 * q : 32 * q + 4, :].bitcast(I32), w1t_scales[0, 4 * q : 4 * q + 4, :].bitcast(I32))
         w1_w = late([P, K], U32, "w1_w", "slot_s0_then_w1_w")

@@ -22,6 +22,7 @@ SLOTS = E * C
 PASSES = N // 512
 ROW_TILES = H // P
 EXPERT_UNITS = ((0, 4), (4, 8), (8, 11), (11, 12))
+WEIGHT_LOADS = (EXPERT_UNITS, ((0, 4), (4, 8), (8, 12)))
 TOKEN_CHUNKS = ((0, 512), (512, 768))
 
 
@@ -60,7 +61,9 @@ def tile_moe_sub_relu_kernel(
 
         def load_w2_words(half):
             words = late([P, E * PASSES, H], U8, f"w2_w{half}", f"then_w2_w{half}")
-            nc.sync.dma_start(words[:].bitcast(I32), w2_words[:, :, H * half : H * (half + 1)].bitcast(I32))
+            for e0, e1 in WEIGHT_LOADS[half]:
+                rows = slice(e0 * PASSES, e1 * PASSES)
+                nc.sync.dma_start(words[:, rows].bitcast(I32), w2_words[:, rows, H * half : H * (half + 1)].bitcast(I32))
             return words
 
         w2_s = [late([P, E * PASSES, 2 * P], U8, "w2_s0", "then_w1_s")]
@@ -159,10 +162,10 @@ def tile_moe_sub_relu_kernel(
         for number, (e0, e1, b) in enumerate(units):
             experts_product(e0, e1, b, number)
         a_sb = late([P, 4, T], F32, "a_sb", "then_w2_w0")
-        nc.sync.dma_start(a_sb[:], a.rearrange("(p j) t -> p j t", j=4))
-        token_step(0, 0, 7)
+        for t0, t1 in TOKEN_CHUNKS:
+            nc.sync.dma_start(a_sb[:, :, t0:t1], a.rearrange("(p j) t -> p j t", j=4)[:, :, t0:t1])
         for number in range(6):
-            experts_product(4 * (number % 3), 4 * (number % 3) + 4, 2 + number // 3, number)
+            experts_product(4 * (number // 2), 4 * (number // 2) + 4, 2 + number % 2, (number + 7) % 8)
 
         w1_s = late([P, K], U8, "w1_s", "then_w1_s")
         nc.vector.memset(w1_s[:].bitcast(I32), 0)
@@ -171,7 +174,7 @@ def tile_moe_sub_relu_kernel(
         w1_w = late([P, K], U32, "w1_w", "slot_s0_then_w1_w")
         nc.sync.dma_start(w1_w[:].bitcast(I32), w1t_words[0].rearrange("p k d -> p (k d)").bitcast(I32))
 
-        for n, b, number in ((1, 0, 5), (0, 1, 4), (1, 1, 3), (0, 2, 2), (0, 3, 1), (1, 2, 0), (1, 3, 6)):
+        for n, b, number in ((0, 0, 4), (1, 0, 3), (0, 1, 2), (1, 1, 1), (0, 2, 0), (0, 3, 7), (1, 2, 6), (1, 3, 5)):
             token_step(n, b, number)
 
         relu_on = [
@@ -189,7 +192,7 @@ def tile_moe_sub_relu_kernel(
             da_s = held([P, width], U8, f"da_s{t0}")
             nc.vector.tensor_scalar_max(mask[:], mask[:], 0.0)
             for c0 in range(0, width, 2 * P):
-                bank = psum_bank((7, 5, 4)[(t0 + c0) // (2 * P)], [P, 2, 2 * P])
+                bank = psum_bank((4, 3, 2)[(t0 + c0) // (2 * P)], [P, 2, 2 * P])
                 for m in range(2):
                     for u in range(2):
                         words = rounded[:, c0 // P + m, u].rearrange("t p e -> t (p e)").bitcast(F32)
@@ -201,7 +204,7 @@ def tile_moe_sub_relu_kernel(
                     MULT,
                 )
             nc.vector.quantize_mx(da_w[:].bitcast(FP8X4), da_s[:], da[:].rearrange("p t j -> p (t j)"))
-            bank = psum_bank(3 if t0 == 0 else 2, [P, width])
+            bank = psum_bank(1 if t0 == 0 else 0, [P, width])
             nc.tensor.matmul_mx(
                 out=bank[:],
                 lhsT=w1_w[:].bitcast(FP8X4),

@@ -15,6 +15,7 @@ U8 = mybir.dt.uint8
 FP8X4 = mybir.dt.float8_e4m3fn_x4
 FP4X4 = mybir.dt.float4_e2m1fn_x4
 MULT = mybir.AluOpType.mult
+IS_GT = mybir.AluOpType.is_gt
 SIGN = mybir.ActivationFunctionType.Sign
 
 P = 128
@@ -132,31 +133,33 @@ def tile_moe_sub_relu_kernel(
 
         dh_t = [held([P, (t1 - t0) // P, 2, P, 2], BF16, f"dh_t{t0}") for t0, t1 in TOKEN_CHUNKS]
 
-        def token_step(n, b, number):
+        def token_step(n, b, *numbers):
             t0, t1 = TOKEN_CHUNKS[n]
             tiles = (t1 - t0) // P
             gated = []
             for r in range(2):
-                u = held([P, t1 - t0], F32, f"gated{n}{b}{r}")
+                u = late([P, t1 - t0], F32, f"gated{n}{b}{r}", f"gated{n}{b}{r}")
                 nc.vector.tensor_tensor(
                     u[:], y[b][:].indirect(pos_sb[r][:, t0 // 16 : t1 // 16]), gate_sb[:, r, t0:t1], MULT
                 )
                 gated.append(u)
-            bank = psum_bank(number, [P, tiles, P])
-            for m in range(tiles):
-                for r in range(2):
-                    nc.tensor.matmul(
-                        bank[:, m, :],
-                        gated[r][:, m * P : (m + 1) * P],
-                        ident[:],
-                        start=(r == 0),
-                        stop=(r == 1),
-                        is_transpose=True,
-                    )
-            nc.scalar.copy(
-                dh_t[n][:, :, :, 32 * b : 32 * (b + 1), :],
-                bank[:].rearrange("t m (p u e) -> t m u p e", u=2, e=2),
-            )
+            share = tiles // len(numbers)
+            for m0, number in zip(range(0, tiles, share), numbers):
+                bank = psum_bank(number, [P, share, P])
+                for m in range(m0, m0 + share):
+                    for r in range(2):
+                        nc.tensor.matmul(
+                            bank[:, m - m0, :],
+                            gated[r][:, m * P : (m + 1) * P],
+                            ident[:],
+                            start=(r == 0),
+                            stop=(r == 1),
+                            is_transpose=True,
+                        )
+                nc.scalar.copy(
+                    dh_t[n][:, m0 : m0 + share, :, 32 * b : 32 * (b + 1), :],
+                    bank[:].rearrange("t m (p u e) -> t m u p e", u=2, e=2),
+                )
 
         units = [(0, 4, 0), (0, 4, 1), (4, 8, 0), (4, 8, 1), (8, 11, 0), (11, 12, 0), (8, 12, 1)]
         for number, (e0, e1, b) in enumerate(units):
@@ -164,8 +167,11 @@ def tile_moe_sub_relu_kernel(
         a_sb = late([P, 4, T], F32, "a_sb", "then_w2_w0")
         for t0, t1 in TOKEN_CHUNKS:
             nc.sync.dma_start(a_sb[:, :, t0:t1], a.rearrange("(p j) t -> p j t", j=4)[:, :, t0:t1])
-        for number in range(6):
-            experts_product(4 * (number // 2), 4 * (number // 2) + 4, 2 + number % 2, (number + 7) % 8)
+        for group, banks in enumerate(((7, 0), (1, 2), (3, 4))):
+            for b, number in zip((2, 3), banks):
+                experts_product(4 * group, 4 * group + 4, b, number)
+            if group < 2:
+                token_step(group, 0, banks[0])
 
         w1_s = late([P, K], U8, "w1_s", "then_w1_s")
         nc.vector.memset(w1_s[:].bitcast(I32), 0)
@@ -174,37 +180,39 @@ def tile_moe_sub_relu_kernel(
         w1_w = late([P, K], U32, "w1_w", "slot_s0_then_w1_w")
         nc.sync.dma_start(w1_w[:].bitcast(I32), w1t_words[0].rearrange("p k d -> p (k d)").bitcast(I32))
 
-        for n, b, number in ((0, 0, 4), (1, 0, 3), (0, 1, 2), (1, 1, 1), (0, 2, 0), (0, 3, 7), (1, 2, 6), (1, 3, 5)):
+        for n, b, number in ((0, 1, 4), (1, 1, 3), (0, 2, 2), (0, 3, 0), (1, 2, 7)):
             token_step(n, b, number)
+        token_step(1, 3, 1, 4)
 
-        relu_on = [
-            late([P, t1 - t0, 4], BF16, f"relu_on{n}", f"then_relu{n}") for n, (t0, t1) in enumerate(TOKEN_CHUNKS)
-        ]
-        for n, (t0, t1) in enumerate(TOKEN_CHUNKS):
-            for m in range((t1 - t0) // P):
-                piece = relu_on[n][:, m * P : (m + 1) * P, :]
-                nc.scalar.activation(piece, a_sb[:, :, t0 + m * P : t0 + (m + 1) * P].rearrange("p j t -> p t j"), SIGN)
+        def side_by_side(mask, t0, t1):
+            return mask.rearrange("p (c i) j -> p c j i", i=2), a_sb[:, :, t0:t1].rearrange("p j (c i) -> p c j i", i=2)
 
-        for (t0, t1), rounded, mask in zip(TOKEN_CHUNKS, dh_t, relu_on):
+        (t0, t1), (t2, t3) = TOKEN_CHUNKS
+        relu_on = [late([P, t1 - t0, 4], BF16, "relu_on0", "then_relu0"), late([P, t3 - t2, 4], BF16, "relu_on1", "gated030")]
+        for m in range(t0, t1, P):
+            nc.scalar.activation(*side_by_side(relu_on[0][:, m - t0 : m - t0 + P, :], m, m + P), SIGN)
+        nc.vector.tensor_scalar_max(relu_on[0][:], relu_on[0][:], 0.0)
+        nc.vector.tensor_single_scalar(*side_by_side(relu_on[1][:], t2, t3), 0.0, IS_GT)
+
+        def masked_words(da, n, m0, tiles, number):
+            bank = psum_bank(number, [P, 2, tiles * P])
+            for m in range(tiles):
+                for u in range(2):
+                    words = dh_t[n][:, m0 + m, u].rearrange("t p e -> t (p e)").bitcast(F32)
+                    nc.tensor.transpose(bank[:, u, m * P : (m + 1) * P], words, ident[:])
+            nc.vector.tensor_tensor(
+                da.rearrange("p t (u e) -> p t u e", u=2),
+                bank[:].bitcast(BF16).rearrange("p u (t e) -> p t u e", e=2),
+                relu_on[n][:, m0 * P : (m0 + tiles) * P, :].rearrange("p t (u e) -> p t u e", u=2),
+                MULT,
+            )
+
+        def first_layer(da, t0, t1, number):
             width = t1 - t0
-            da = held([P, width, 4], BF16, f"da{t0}")
             da_w = held([P, width], U32, f"da_w{t0}")
             da_s = held([P, width], U8, f"da_s{t0}")
-            nc.vector.tensor_scalar_max(mask[:], mask[:], 0.0)
-            for c0 in range(0, width, 2 * P):
-                bank = psum_bank((4, 3, 2)[(t0 + c0) // (2 * P)], [P, 2, 2 * P])
-                for m in range(2):
-                    for u in range(2):
-                        words = rounded[:, c0 // P + m, u].rearrange("t p e -> t (p e)").bitcast(F32)
-                        nc.tensor.transpose(bank[:, u, m * P : (m + 1) * P], words, ident[:])
-                nc.vector.tensor_tensor(
-                    da[:, c0 : c0 + 2 * P, :].rearrange("p t (u e) -> p t u e", u=2),
-                    bank[:].bitcast(BF16).rearrange("p u (t e) -> p t u e", e=2),
-                    mask[:, c0 : c0 + 2 * P, :].rearrange("p t (u e) -> p t u e", u=2),
-                    MULT,
-                )
-            nc.vector.quantize_mx(da_w[:].bitcast(FP8X4), da_s[:], da[:].rearrange("p t j -> p (t j)"))
-            bank = psum_bank(1 if t0 == 0 else 0, [P, width])
+            nc.vector.quantize_mx(da_w[:].bitcast(FP8X4), da_s[:], da.rearrange("p t j -> p (t j)"))
+            bank = psum_bank(number, [P, width])
             nc.tensor.matmul_mx(
                 out=bank[:],
                 lhsT=w1_w[:].bitcast(FP8X4),
@@ -217,3 +225,12 @@ def tile_moe_sub_relu_kernel(
             result = held([P, width], F32, f"result{t0}")
             nc.scalar.copy(result[:], bank[:])
             nc.sync.dma_start(out[:, t0:t1], result[:])
+
+        da = held([P, T, 4], BF16, "da")
+        for m0, number in ((0, 5), (2, 6)):
+            masked_words(da[:, m0 * P : (m0 + 2) * P, :], 0, m0, 2, number)
+        first_layer(da[:, t0:t1, :], t0, t1, 3)
+        for m0, number in ((0, 2), (1, 0)):
+            masked_words(da[:, t2 + m0 * P : t2 + (m0 + 1) * P, :], 1, m0, 1, number)
+        for m0, number in ((0, 7), (1, 1)):
+            first_layer(da[:, t2 + m0 * P : t2 + (m0 + 1) * P, :], t2 + m0 * P, t2 + (m0 + 1) * P, number)

@@ -1,7 +1,6 @@
 from contextlib import ExitStack
 
 import concourse.mybir as mybir
-from concourse.masks import make_identity
 
 K, T, E, C, H, N = 128, 768, 12, 128, 512, 1024
 FLOPS = 2 * N * H * E * C + 2 * H * K * T
@@ -15,7 +14,7 @@ U8 = mybir.dt.uint8
 FP8X4 = mybir.dt.float8_e4m3fn_x4
 FP4X4 = mybir.dt.float4_e2m1fn_x4
 MULT = mybir.AluOpType.mult
-IS_GT = mybir.AluOpType.is_gt
+NOT_EQUAL = mybir.AluOpType.not_equal
 SIGN = mybir.ActivationFunctionType.Sign
 
 P = 128
@@ -69,12 +68,16 @@ def tile_moe_sub_relu_kernel(
 
         w2_s = [late([P, E * PASSES, 2 * P], U8, "w2_s0", "then_w1_s")]
         nc.gpsimd.memset(dy_s[:].bitcast(I32), 0)
-        make_identity(nc, ident[:])
         nc.vector.memset(zeros[:], 0.0)
         nc.vector.memset(w2_s[0][:].bitcast(I32), 0)
+        blank = late([P, P], F32, "blank", "then_w2_s1")
+        nc.vector.memset(blank[:], 0.0)
+        nc.gpsimd.affine_select(
+            out=ident[:], in_=blank[:], compare_op=NOT_EQUAL, fill=1.0, base=0, pattern=[[-1, P]], channel_multiplier=1
+        )
         nc.vector.memset(slot_s[1][:].bitcast(I32), 0)
-        w2_s.append(held([P, E * PASSES, 2 * P], U8, "w2_s1"))
-        nc.vector.memset(w2_s[1][:].bitcast(I32), 0)
+        w2_s.append(late([P, E * PASSES, 2 * P], U8, "w2_s1", "then_w2_s1"))
+        nc.gpsimd.memset(w2_s[1][:].bitcast(I32), 0)
         nc.scalar.activation(gate_rows[:].rearrange("p r n -> p (r n)"), zeros[:], SIGN)
 
         nc.sync.dma_start(offs_sb[:], offs)
@@ -161,7 +164,7 @@ def tile_moe_sub_relu_kernel(
                     bank[:].rearrange("t m (p u e) -> t m u p e", u=2, e=2),
                 )
 
-        units = [(0, 4, 0), (0, 4, 1), (4, 8, 0), (4, 8, 1), (8, 11, 0), (11, 12, 0), (8, 12, 1)]
+        units = [(0, 4, 0), (0, 4, 1), (4, 8, 0), (8, 11, 0), (11, 12, 0), (4, 8, 1), (8, 12, 1)]
         for number, (e0, e1, b) in enumerate(units):
             experts_product(e0, e1, b, number)
         a_sb = late([P, 4, T], F32, "a_sb", "then_w2_w0")
@@ -182,17 +185,17 @@ def tile_moe_sub_relu_kernel(
 
         for n, b, number in ((0, 1, 4), (1, 1, 3), (0, 2, 2), (0, 3, 0), (1, 2, 7)):
             token_step(n, b, number)
-        token_step(1, 3, 1, 4)
 
         def side_by_side(mask, t0, t1):
             return mask.rearrange("p (c i) j -> p c j i", i=2), a_sb[:, :, t0:t1].rearrange("p j (c i) -> p c j i", i=2)
 
         (t0, t1), (t2, t3) = TOKEN_CHUNKS
-        relu_on = [late([P, t1 - t0, 4], BF16, "relu_on0", "then_relu0"), late([P, t3 - t2, 4], BF16, "relu_on1", "gated030")]
-        for m in range(t0, t1, P):
-            nc.scalar.activation(*side_by_side(relu_on[0][:, m - t0 : m - t0 + P, :], m, m + P), SIGN)
-        nc.vector.tensor_scalar_max(relu_on[0][:], relu_on[0][:], 0.0)
-        nc.vector.tensor_single_scalar(*side_by_side(relu_on[1][:], t2, t3), 0.0, IS_GT)
+        relu_on = [late([P, c1 - c0, 4], BF16, f"relu_on{n}", f"then_relu{n}") for n, (c0, c1) in enumerate(TOKEN_CHUNKS)]
+        for mask, (c0, c1) in zip(relu_on, TOKEN_CHUNKS):
+            for m in range(c0, c1, P):
+                piece = mask[:, m - c0 : m - c0 + P, :]
+                nc.scalar.activation(*side_by_side(piece, m, m + P), SIGN)
+            nc.vector.tensor_scalar_max(mask[:], mask[:], 0.0)
 
         def masked_words(da, n, m0, tiles, number):
             bank = psum_bank(number, [P, 2, tiles * P])
@@ -229,8 +232,9 @@ def tile_moe_sub_relu_kernel(
         da = held([P, T, 4], BF16, "da")
         for m0, number in ((0, 5), (2, 6)):
             masked_words(da[:, m0 * P : (m0 + 2) * P, :], 0, m0, 2, number)
+        token_step(1, 3, 0, 7)
         first_layer(da[:, t0:t1, :], t0, t1, 3)
-        for m0, number in ((0, 2), (1, 0)):
+        for m0, number in ((0, 2), (1, 1)):
             masked_words(da[:, t2 + m0 * P : t2 + (m0 + 1) * P, :], 1, m0, 1, number)
-        for m0, number in ((0, 7), (1, 1)):
+        for m0, number in ((0, 4), (1, 5)):
             first_layer(da[:, t2 + m0 * P : t2 + (m0 + 1) * P, :], t2 + m0 * P, t2 + (m0 + 1) * P, number)

@@ -22,8 +22,8 @@ SLOTS = E * C
 PASSES = N // 512
 ROW_TILES = H // P
 EXPERT_UNITS = ((0, 4), (4, 8), (8, 11), (11, 12))
-WEIGHT_LOADS = (EXPERT_UNITS, ((0, 4), (4, 8), (8, 12)))
-TOKEN_CHUNKS = ((0, 512), (512, 768))
+GATE_ROWS, GATE_RUN = 16, 96
+PIECES = ((0, 2), (2, 4), (4, 5), (5, 6))
 
 
 def tile_moe_sub_relu_kernel(
@@ -44,72 +44,74 @@ def tile_moe_sub_relu_kernel(
         pos_sb = [keep.tile([P, T // 16], U16, name=f"pos{r}_sb") for r in range(2)]
         dy_s = held([P, T], U8, "dy_s")
         dy_w = held([P, PASSES, T], U32, "dy_w")
-        slot_s = [late([P, SLOTS], U8, f"slot_s{s}", f"slot_s{s}_then_w1_w") for s in range(PASSES)]
+        slot_rows = held([P, SLOTS], U8, "slot_rows")
         slot_w = [late([P, SLOTS], U32, f"slot_w{s}", f"then_relu{s}") for s in range(PASSES)]
         y = [held([P, SLOTS], F32, f"y{b}") for b in range(ROW_TILES)]
-        gate_sb = held([P, 2, T], F32, "gate_sb")
-        gate_rows = held([P, 2, P], F32, "gate_rows")
-        gate_cols = late([P, 2, 8], F32, "gate_cols", "then_w2_w1")
-        zeros = late([P, 2 * P], F32, "zeros", "then_w2_w0")
+        gate_sb = held([P, 2 * T], F32, "gate_sb")
+        gate_rows = late([P, P], F32, "gate_rows", "then_w2_s1")
+        gate_cols = held([P, GATE_ROWS], F32, "gate_cols")
         ident = held([P, P], F32, "ident")
         w2_words = w2t_words.rearrange("e s p x -> p (e s) x")
         w2_rows = w2t_scales.rearrange("e s b i -> b (e s) i")
 
-        def load_w2_scales(plane, half):
-            for r in range(4):
-                nc.sync.dma_start(plane[r:P:32].bitcast(I32), w2_rows[r:16:4, :, 2 * P * half : 2 * P * (half + 1)].bitcast(I32))
+        def load_w2_scales(queue, half, r):
+            queue.dma_start(w2_s[half][r:P:32].bitcast(I32), w2_rows[r:16:4, :, 2 * P * half : 2 * P * (half + 1)].bitcast(I32))
 
-        def load_w2_words(half):
-            words = late([P, E * PASSES, H], U8, f"w2_w{half}", f"then_w2_w{half}")
-            for e0, e1 in WEIGHT_LOADS[half]:
-                rows = slice(e0 * PASSES, e1 * PASSES)
-                nc.sync.dma_start(words[:, rows].bitcast(I32), w2_words[:, rows, H * half : H * (half + 1)].bitcast(I32))
-            return words
+        def load_w2_words(half, e0, e1):
+            rows = slice(e0 * PASSES, e1 * PASSES)
+            nc.sync.dma_start(w2_w[half][:, rows].bitcast(I32), w2_words[:, rows, H * half : H * (half + 1)].bitcast(I32))
 
+        w2_w = [held([P, E * PASSES, H], U8, f"w2_w{half}") for half in range(2)]
         w2_s = [late([P, E * PASSES, 2 * P], U8, "w2_s0", "then_w1_s")]
-        nc.gpsimd.memset(dy_s[:].bitcast(I32), 0)
-        nc.vector.memset(zeros[:], 0.0)
+        nc.vector.memset(dy_s[:].bitcast(I32), 0)
+        nc.vector.memset(gate_rows[:], 0.0)
         nc.vector.memset(w2_s[0][:].bitcast(I32), 0)
-        blank = late([P, P], F32, "blank", "then_w2_s1")
+        blank = late([P, P], F32, "blank", "then_slot_s")
         nc.vector.memset(blank[:], 0.0)
         nc.gpsimd.affine_select(
             out=ident[:], in_=blank[:], compare_op=NOT_EQUAL, fill=1.0, base=0, pattern=[[-1, P]], channel_multiplier=1
         )
-        nc.vector.memset(slot_s[1][:].bitcast(I32), 0)
-        w2_s.append(late([P, E * PASSES, 2 * P], U8, "w2_s1", "then_w2_s1"))
-        nc.gpsimd.memset(w2_s[1][:].bitcast(I32), 0)
-        nc.scalar.activation(gate_rows[:].rearrange("p r n -> p (r n)"), zeros[:], SIGN)
+        slot_s = late([P, PASSES, SLOTS], U8, "slot_s", "then_slot_s")
+        nc.gpsimd.memset(slot_s[:].bitcast(I32), 0)
 
         nc.sync.dma_start(offs_sb[:], offs)
-        for q in range(4):
-            nc.sync.dma_start(dy_s[32 * q : 32 * q + 8, :].bitcast(I32), dy_scales[:, 4 * q : 4 * q + 4, :].bitcast(I32))
+        nc.scalar.dma_start(dy_s[0:32, :].bitcast(I32), dy_scales.rearrange("s b t -> b s t").bitcast(I32))
+        nc.sync.dma_start(gate_rows[0:GATE_ROWS, 0:GATE_RUN], gate[:, 0, :].rearrange("r (m n) -> r m n", n=GATE_RUN))
+        nc.sync.dma_start(dy_w[:].bitcast(I32), dy_words.rearrange("s p t d -> p s (t d)").bitcast(I32))
+        for r in range(4):
+            load_w2_scales((nc.sync, nc.scalar)[r // 2], 0, r)
+        load_w2_words(0, 0, 8)
+        load_w2_words(0, 8, 12)
         for r in range(2):
             nc.sync.dma_start(pos_sb[r][:], (pos1, pos2)[r])
-        nc.sync.dma_start(dy_w[:].bitcast(I32), dy_words.rearrange("s p t d -> p s (t d)").bitcast(I32))
-        nc.sync.dma_start(gate_rows[0:8], gate.rearrange("r p (m n) -> (p m) r n", n=P)[0:8])
-        load_w2_scales(w2_s[0], 0)
-        w2_w = [load_w2_words(0)]
 
         def psum_bank(number, shape):
             return psum.tile(shape, F32, name=f"bank{number}", tag=f"bank{number}")
 
-        bank = psum_bank(7, [P, 2, P])
-        for r in range(2):
-            nc.tensor.transpose(bank[:, r, :], gate_rows[:, r, :], ident[:])
-        nc.scalar.copy(gate_cols[:], bank[:, :, 0:8])
-        gate_flat = gate_sb[:].rearrange("p r t -> p (r t)")
-        for third in range(3):
-            bank = psum_bank(4 + third, [P, 4, P])
+        bank = psum_bank(7, [P, P])
+        nc.tensor.transpose(bank[:], gate_rows[:], ident[:])
+        nc.scalar.copy(gate_cols[:], bank[:, 0:GATE_ROWS])
+        w2_s.append(late([P, E * PASSES, 2 * P], U8, "w2_s1", "then_w2_s1"))
+        nc.gpsimd.memset(w2_s[1][:].bitcast(I32), 0)
+        for quarter in range(4):
+            bank = psum_bank(4 + quarter, [P, 4, P])
             for x in range(4):
-                r, m = divmod(4 * third + x, T // P)
-                nc.tensor.transpose(bank[:, x, :], gate_cols[:, r, m : m + 1].to_broadcast([P, P]), ident[:])
-            nc.scalar.copy(gate_flat[:, 512 * third : 512 * (third + 1)], bank[:].rearrange("p x n -> p (x n)"))
+                row = 4 * quarter + x
+                nc.tensor.transpose(bank[:, x, :], gate_cols[:, row : row + 1].to_broadcast([P, P]), ident[:])
+            nc.scalar.copy(
+                gate_sb[:, 4 * GATE_RUN * quarter : 4 * GATE_RUN * (quarter + 1)].rearrange("p (x n) -> p x n", x=4),
+                bank[:, :, 0:GATE_RUN],
+            )
 
         for j0 in range(0, SLOTS, 512):
-            nc.vector.tensor_copy(slot_s[0][:, j0 : j0 + 512], dy_s[:].indirect(offs_sb[:, j0 // 16 : (j0 + 512) // 16]))
-        nc.scalar.dma_start(slot_s[1][0:112, :].bitcast(I32), slot_s[0][4:116, :].bitcast(I32))
-        load_w2_scales(w2_s[1], 1)
-        w2_w.append(load_w2_words(1))
+            nc.vector.tensor_copy(slot_rows[:, j0 : j0 + 512], dy_s[:].indirect(offs_sb[:, j0 // 16 : (j0 + 512) // 16]))
+        for q in range(4):
+            nc.scalar.dma_start(slot_s[32 * q : 32 * q + 4].bitcast(I32), slot_rows[8 * q : 8 * q + 8, :].bitcast(I32))
+        load_w2_scales(nc.sync, 1, 0)
+        load_w2_words(1, 0, 8)
+        for r in range(1, 4):
+            load_w2_scales(nc.sync, 1, r)
+        load_w2_words(1, 8, 12)
 
         for e0, e1 in EXPERT_UNITS:
             for s in range(PASSES):
@@ -128,93 +130,103 @@ def tile_moe_sub_relu_kernel(
                         lhsT=w2_w[half][:, e * PASSES + s, 2 * P * part : 2 * P * (part + 1)].bitcast(FP4X4),
                         lhsT_scale=w2_s[half][:, e * PASSES + s, P * part : P * (part + 1)],
                         rhs=slot_w[s][:, cols].bitcast(FP8X4),
-                        rhs_scale=slot_s[s][:, cols],
+                        rhs_scale=slot_s[:, s, cols],
                         start=(s == 0),
                         stop=(s == PASSES - 1),
                     )
             nc.scalar.copy(y[b][:, e0 * C : e1 * C], bank[:])
 
-        dh_t = [held([P, (t1 - t0) // P, 2, P, 2], BF16, f"dh_t{t0}") for t0, t1 in TOKEN_CHUNKS]
+        dh_t = [held([P, m1 - m0, 2, P, 2], BF16, f"dh_t{m0}") for m0, m1 in PIECES]
 
-        def token_step(n, b, *numbers):
-            t0, t1 = TOKEN_CHUNKS[n]
-            tiles = (t1 - t0) // P
+        def gated_gathers(b, m0, m1):
             gated = []
             for r in range(2):
-                u = late([P, t1 - t0], F32, f"gated{n}{b}{r}", f"gated{n}{b}{r}")
+                u = held([P, (m1 - m0) * P], F32, f"gated{b}{m0}{r}")
                 nc.vector.tensor_tensor(
-                    u[:], y[b][:].indirect(pos_sb[r][:, t0 // 16 : t1 // 16]), gate_sb[:, r, t0:t1], MULT
+                    u[:],
+                    y[b][:].indirect(pos_sb[r][:, m0 * P // 16 : m1 * P // 16]),
+                    gate_sb[:, r * T + m0 * P : r * T + m1 * P],
+                    MULT,
                 )
                 gated.append(u)
-            share = tiles // len(numbers)
-            for m0, number in zip(range(0, tiles, share), numbers):
-                bank = psum_bank(number, [P, share, P])
-                for m in range(m0, m0 + share):
-                    for r in range(2):
-                        nc.tensor.matmul(
-                            bank[:, m - m0, :],
-                            gated[r][:, m * P : (m + 1) * P],
-                            ident[:],
-                            start=(r == 0),
-                            stop=(r == 1),
-                            is_transpose=True,
-                        )
+            return m0, gated
+
+        def summed(gathered, b, pieces, number):
+            first, gated = gathered
+            base = PIECES[pieces[0]][0]
+            bank = psum_bank(number, [P, PIECES[pieces[-1]][1] - base, P])
+            for m in range(base, PIECES[pieces[-1]][1]):
+                for r in range(2):
+                    nc.tensor.matmul(
+                        bank[:, m - base, :],
+                        gated[r][:, (m - first) * P : (m - first + 1) * P],
+                        ident[:],
+                        start=(r == 0),
+                        stop=(r == 1),
+                        is_transpose=True,
+                    )
+            for n in pieces:
+                m0, m1 = PIECES[n]
                 nc.scalar.copy(
-                    dh_t[n][:, m0 : m0 + share, :, 32 * b : 32 * (b + 1), :],
-                    bank[:].rearrange("t m (p u e) -> t m u p e", u=2, e=2),
+                    dh_t[n][:, :, :, 32 * b : 32 * (b + 1), :],
+                    bank[:, m0 - base : m1 - base, :].rearrange("t m (p u e) -> t m u p e", u=2, e=2),
                 )
 
         units = [(0, 4, 0), (0, 4, 1), (4, 8, 0), (8, 11, 0), (11, 12, 0), (4, 8, 1), (8, 12, 1)]
         for number, (e0, e1, b) in enumerate(units):
             experts_product(e0, e1, b, number)
-        a_sb = late([P, 4, T], F32, "a_sb", "then_w2_w0")
-        for t0, t1 in TOKEN_CHUNKS:
+        a_sb = held([P, 4, T], F32, "a_sb")
+        for t0, t1 in ((0, 512), (512, T)):
             nc.sync.dma_start(a_sb[:, :, t0:t1], a.rearrange("(p j) t -> p j t", j=4)[:, :, t0:t1])
-        for group, banks in enumerate(((7, 0), (1, 2), (3, 4))):
-            for b, number in zip((2, 3), banks):
-                experts_product(4 * group, 4 * group + 4, b, number)
-            if group < 2:
-                token_step(group, 0, banks[0])
+        gathered = [gated_gathers(b, 0, 6) for b in range(2)]
+        for e0, b, number in ((0, 2, 7), (4, 2, 0), (0, 3, 1), (4, 3, 2)):
+            experts_product(e0, e0 + 4, b, number)
+        summed(gathered[0], 0, (0, 1), 7)
+        summed(gathered[0], 0, (2, 3), 0)
+        for b, number in ((2, 3), (3, 4)):
+            experts_product(8, 12, b, number)
+        summed(gathered[1], 1, (0, 1), 3)
+        summed(gathered[1], 1, (2, 3), 4)
 
         w1_s = late([P, K], U8, "w1_s", "then_w1_s")
         nc.vector.memset(w1_s[:].bitcast(I32), 0)
         for q in range(4):
             nc.sync.dma_start(w1_s[32 * q : 32 * q + 4, :].bitcast(I32), w1t_scales[0, 4 * q : 4 * q + 4, :].bitcast(I32))
-        w1_w = late([P, K], U32, "w1_w", "slot_s0_then_w1_w")
+        w1_w = late([P, K], U32, "w1_w", "then_slot_s")
         nc.sync.dma_start(w1_w[:].bitcast(I32), w1t_words[0].rearrange("p k d -> p (k d)").bitcast(I32))
-
-        for n, b, number in ((0, 1, 4), (1, 1, 3), (0, 2, 2), (0, 3, 0), (1, 2, 7)):
-            token_step(n, b, number)
 
         def side_by_side(mask, t0, t1):
             return mask.rearrange("p (c i) j -> p c j i", i=2), a_sb[:, :, t0:t1].rearrange("p j (c i) -> p c j i", i=2)
 
-        (t0, t1), (t2, t3) = TOKEN_CHUNKS
-        relu_on = [late([P, c1 - c0, 4], BF16, f"relu_on{n}", f"then_relu{n}") for n, (c0, c1) in enumerate(TOKEN_CHUNKS)]
-        for mask, (c0, c1) in zip(relu_on, TOKEN_CHUNKS):
-            for m in range(c0, c1, P):
-                piece = mask[:, m - c0 : m - c0 + P, :]
-                nc.scalar.activation(*side_by_side(piece, m, m + P), SIGN)
-            nc.vector.tensor_scalar_max(mask[:], mask[:], 0.0)
+        relu_on = [late([P, c1 - c0, 4], BF16, f"relu_on{n}", f"then_relu{n}") for n, (c0, c1) in enumerate(((0, 512), (512, T)))]
 
-        def masked_words(da, n, m0, tiles, number):
-            bank = psum_bank(number, [P, 2, tiles * P])
-            for m in range(tiles):
+        def relu_mask(n, c0, c1):
+            for m in range(c0, c1, P):
+                nc.scalar.activation(*side_by_side(relu_on[n][:, m - c0 : m - c0 + P, :], m, m + P), SIGN)
+            nc.vector.tensor_scalar_max(relu_on[n][:], relu_on[n][:], 0.0)
+
+        da = held([P, T, 4], BF16, "da")
+
+        def masked_words(n, number):
+            m0, m1 = PIECES[n]
+            bank = psum_bank(number, [P, 2, (m1 - m0) * P])
+            for m in range(m1 - m0):
                 for u in range(2):
-                    words = dh_t[n][:, m0 + m, u].rearrange("t p e -> t (p e)").bitcast(F32)
+                    words = dh_t[n][:, m, u].rearrange("t p e -> t (p e)").bitcast(F32)
                     nc.tensor.transpose(bank[:, u, m * P : (m + 1) * P], words, ident[:])
+            mask = relu_on[m0 // 4][:, (m0 % 4) * P : (m0 % 4 + m1 - m0) * P, :]
             nc.vector.tensor_tensor(
-                da.rearrange("p t (u e) -> p t u e", u=2),
+                da[:, m0 * P : m1 * P, :].rearrange("p t (u e) -> p t u e", u=2),
                 bank[:].bitcast(BF16).rearrange("p u (t e) -> p t u e", e=2),
-                relu_on[n][:, m0 * P : (m0 + tiles) * P, :].rearrange("p t (u e) -> p t u e", u=2),
+                mask.rearrange("p t (u e) -> p t u e", u=2),
                 MULT,
             )
 
-        def first_layer(da, t0, t1, number):
+        def first_layer(t0, t1, number):
             width = t1 - t0
             da_w = held([P, width], U32, f"da_w{t0}")
             da_s = held([P, width], U8, f"da_s{t0}")
-            nc.vector.quantize_mx(da_w[:].bitcast(FP8X4), da_s[:], da.rearrange("p t j -> p (t j)"))
+            nc.vector.quantize_mx(da_w[:].bitcast(FP8X4), da_s[:], da[:, t0:t1, :].rearrange("p t j -> p (t j)"))
             bank = psum_bank(number, [P, width])
             nc.tensor.matmul_mx(
                 out=bank[:],
@@ -229,12 +241,19 @@ def tile_moe_sub_relu_kernel(
             nc.scalar.copy(result[:], bank[:])
             nc.sync.dma_start(out[:, t0:t1], result[:])
 
-        da = held([P, T, 4], BF16, "da")
-        for m0, number in ((0, 5), (2, 6)):
-            masked_words(da[:, m0 * P : (m0 + 2) * P, :], 0, m0, 2, number)
-        token_step(1, 3, 0, 7)
-        first_layer(da[:, t0:t1, :], t0, t1, 3)
-        for m0, number in ((0, 2), (1, 1)):
-            masked_words(da[:, t2 + m0 * P : t2 + (m0 + 1) * P, :], 1, m0, 1, number)
-        for m0, number in ((0, 4), (1, 5)):
-            first_layer(da[:, t2 + m0 * P : t2 + (m0 + 1) * P, :], t2 + m0 * P, t2 + (m0 + 1) * P, number)
+        summed(gated_gathers(2, 0, 4), 2, (0, 1), 5)
+        relu_mask(0, 0, 512)
+        last_of_first = gated_gathers(3, 0, 4)
+        summed(last_of_first, 3, (0,), 6)
+        summed(last_of_first, 3, (1,), 1)
+        masked_words(0, 2)
+        masked_words(1, 7)
+        summed(gated_gathers(2, 4, 6), 2, (2, 3), 6)
+        relu_mask(1, 512, T)
+        summed(gated_gathers(3, 4, 5), 3, (2,), 1)
+        masked_words(2, 0)
+        summed(gated_gathers(3, 5, 6), 3, (3,), 6)
+        first_layer(0, 512, 3)
+        masked_words(3, 4)
+        first_layer(512, 640, 5)
+        first_layer(640, T, 1)

@@ -23,7 +23,7 @@ PASSES = N // 512
 ROW_TILES = H // P
 EXPERT_UNITS = ((0, 4), (4, 8), (8, 11), (11, 12))
 GATE_ROWS, GATE_RUN = 16, 96
-PIECES = ((0, 2), (2, 4), (4, 5), (5, 6))
+TOKEN_CHUNKS = ((0, 512), (512, 768))
 
 
 def tile_moe_sub_relu_kernel(
@@ -42,13 +42,11 @@ def tile_moe_sub_relu_kernel(
 
         offs_sb = keep.tile([P, SLOTS // 16], U16, name="offs_sb")
         pos_sb = [keep.tile([P, T // 16], U16, name=f"pos{r}_sb") for r in range(2)]
-        dy_s = held([P, T], U8, "dy_s")
+        dy_s = late([P, T], U8, "dy_s", "then_gate")
         dy_w = held([P, PASSES, T], U32, "dy_w")
-        slot_rows = held([P, SLOTS], U8, "slot_rows")
         slot_w = [late([P, SLOTS], U32, f"slot_w{s}", f"then_relu{s}") for s in range(PASSES)]
         y = [held([P, SLOTS], F32, f"y{b}") for b in range(ROW_TILES)]
-        gate_sb = held([P, 2 * T], F32, "gate_sb")
-        gate_rows = late([P, P], F32, "gate_rows", "then_w2_s1")
+        gate_rows = held([P, P], F32, "gate_rows")
         gate_cols = held([P, GATE_ROWS], F32, "gate_cols")
         ident = held([P, P], F32, "ident")
         w2_words = w2t_words.rearrange("e s p x -> p (e s) x")
@@ -62,26 +60,28 @@ def tile_moe_sub_relu_kernel(
             nc.sync.dma_start(w2_w[half][:, rows].bitcast(I32), w2_words[:, rows, H * half : H * (half + 1)].bitcast(I32))
 
         w2_w = [held([P, E * PASSES, H], U8, f"w2_w{half}") for half in range(2)]
-        w2_s = [late([P, E * PASSES, 2 * P], U8, "w2_s0", "then_w1_s")]
+        w2_s = [late([P, E * PASSES, 2 * P], U8, "w2_s0", "then_w1_s"), held([P, E * PASSES, 2 * P], U8, "w2_s1")]
         nc.vector.memset(dy_s[:].bitcast(I32), 0)
         nc.vector.memset(gate_rows[:], 0.0)
-        nc.vector.memset(w2_s[0][:].bitcast(I32), 0)
         blank = late([P, P], F32, "blank", "then_slot_s")
-        nc.vector.memset(blank[:], 0.0)
+        nc.gpsimd.memset(blank[:], 0.0)
         nc.gpsimd.affine_select(
             out=ident[:], in_=blank[:], compare_op=NOT_EQUAL, fill=1.0, base=0, pattern=[[-1, P]], channel_multiplier=1
         )
-        slot_s = late([P, PASSES, SLOTS], U8, "slot_s", "then_slot_s")
-        nc.gpsimd.memset(slot_s[:].bitcast(I32), 0)
+        slot_s = [held([P, SLOTS], U8, "slot_s0"), late([P, SLOTS], U8, "slot_s1", "then_slot_s")]
+        nc.gpsimd.memset(slot_s[1][:].bitcast(I32), 0)
+        nc.vector.memset(w2_s[0][:].bitcast(I32), 0)
+        nc.vector.memset(w2_s[1][:].bitcast(I32), 0)
 
         nc.sync.dma_start(offs_sb[:], offs)
-        nc.scalar.dma_start(dy_s[0:32, :].bitcast(I32), dy_scales.rearrange("s b t -> b s t").bitcast(I32))
-        nc.sync.dma_start(gate_rows[0:GATE_ROWS, 0:GATE_RUN], gate[:, 0, :].rearrange("r (m n) -> r m n", n=GATE_RUN))
+        nc.scalar.dma_start(gate_rows[0:GATE_ROWS, 0:GATE_RUN], gate[:, 0, :].rearrange("r (m n) -> r m n", n=GATE_RUN))
+        for q in range(4):
+            nc.sync.dma_start(dy_s[32 * q : 32 * q + 8, :].bitcast(I32), dy_scales[:, 4 * q : 4 * q + 4, :].bitcast(I32))
         nc.sync.dma_start(dy_w[:].bitcast(I32), dy_words.rearrange("s p t d -> p s (t d)").bitcast(I32))
         for r in range(4):
-            load_w2_scales((nc.sync, nc.scalar)[r // 2], 0, r)
-        load_w2_words(0, 0, 8)
-        load_w2_words(0, 8, 12)
+            load_w2_scales(nc.sync, 0, r)
+        for e0 in range(0, E, 4):
+            load_w2_words(0, e0, e0 + 4)
         for r in range(2):
             nc.sync.dma_start(pos_sb[r][:], (pos1, pos2)[r])
 
@@ -91,8 +91,13 @@ def tile_moe_sub_relu_kernel(
         bank = psum_bank(7, [P, P])
         nc.tensor.transpose(bank[:], gate_rows[:], ident[:])
         nc.scalar.copy(gate_cols[:], bank[:, 0:GATE_ROWS])
-        w2_s.append(late([P, E * PASSES, 2 * P], U8, "w2_s1", "then_w2_s1"))
-        nc.gpsimd.memset(w2_s[1][:].bitcast(I32), 0)
+
+        for j0 in range(0, SLOTS, 512):
+            nc.vector.tensor_copy(slot_s[0][:, j0 : j0 + 512], dy_s[:].indirect(offs_sb[:, j0 // 16 : (j0 + 512) // 16]))
+        for j0, j1 in ((0, 512), (512, SLOTS)):
+            nc.scalar.dma_start(slot_s[1][0:112, j0:j1].bitcast(I32), slot_s[0][4:116, j0:j1].bitcast(I32))
+
+        gate_sb = late([P, 2 * T], F32, "gate_sb", "then_gate")
         for quarter in range(4):
             bank = psum_bank(4 + quarter, [P, 4, P])
             for x in range(4):
@@ -102,16 +107,10 @@ def tile_moe_sub_relu_kernel(
                 gate_sb[:, 4 * GATE_RUN * quarter : 4 * GATE_RUN * (quarter + 1)].rearrange("p (x n) -> p x n", x=4),
                 bank[:, :, 0:GATE_RUN],
             )
-
-        for j0 in range(0, SLOTS, 512):
-            nc.vector.tensor_copy(slot_rows[:, j0 : j0 + 512], dy_s[:].indirect(offs_sb[:, j0 // 16 : (j0 + 512) // 16]))
-        for q in range(4):
-            nc.scalar.dma_start(slot_s[32 * q : 32 * q + 4].bitcast(I32), slot_rows[8 * q : 8 * q + 8, :].bitcast(I32))
-        load_w2_scales(nc.sync, 1, 0)
-        load_w2_words(1, 0, 8)
-        for r in range(1, 4):
+        for r in range(4):
             load_w2_scales(nc.sync, 1, r)
-        load_w2_words(1, 8, 12)
+        for e0 in range(0, E, 4):
+            load_w2_words(1, e0, e0 + 4)
 
         for e0, e1 in EXPERT_UNITS:
             for s in range(PASSES):
@@ -130,63 +129,53 @@ def tile_moe_sub_relu_kernel(
                         lhsT=w2_w[half][:, e * PASSES + s, 2 * P * part : 2 * P * (part + 1)].bitcast(FP4X4),
                         lhsT_scale=w2_s[half][:, e * PASSES + s, P * part : P * (part + 1)],
                         rhs=slot_w[s][:, cols].bitcast(FP8X4),
-                        rhs_scale=slot_s[:, s, cols],
+                        rhs_scale=slot_s[s][:, cols],
                         start=(s == 0),
                         stop=(s == PASSES - 1),
                     )
             nc.scalar.copy(y[b][:, e0 * C : e1 * C], bank[:])
 
-        dh_t = [held([P, m1 - m0, 2, P, 2], BF16, f"dh_t{m0}") for m0, m1 in PIECES]
+        dh_t = [held([P, (t1 - t0) // P, 2, P, 2], BF16, f"dh_t{t0}") for t0, t1 in TOKEN_CHUNKS]
 
-        def gated_gathers(b, m0, m1):
+        def token_step(n, b, *numbers):
+            t0, t1 = TOKEN_CHUNKS[n]
+            tiles = (t1 - t0) // P
             gated = []
             for r in range(2):
-                u = held([P, (m1 - m0) * P], F32, f"gated{b}{m0}{r}")
+                u = late([P, t1 - t0], F32, f"gated{n}{b}{r}", f"gated{n}{b}{r}")
                 nc.vector.tensor_tensor(
-                    u[:],
-                    y[b][:].indirect(pos_sb[r][:, m0 * P // 16 : m1 * P // 16]),
-                    gate_sb[:, r * T + m0 * P : r * T + m1 * P],
-                    MULT,
+                    u[:], y[b][:].indirect(pos_sb[r][:, t0 // 16 : t1 // 16]), gate_sb[:, r * T + t0 : r * T + t1], MULT
                 )
                 gated.append(u)
-            return m0, gated
-
-        def summed(gathered, b, pieces, number):
-            first, gated = gathered
-            base = PIECES[pieces[0]][0]
-            bank = psum_bank(number, [P, PIECES[pieces[-1]][1] - base, P])
-            for m in range(base, PIECES[pieces[-1]][1]):
-                for r in range(2):
-                    nc.tensor.matmul(
-                        bank[:, m - base, :],
-                        gated[r][:, (m - first) * P : (m - first + 1) * P],
-                        ident[:],
-                        start=(r == 0),
-                        stop=(r == 1),
-                        is_transpose=True,
-                    )
-            for n in pieces:
-                m0, m1 = PIECES[n]
+            share = tiles // len(numbers)
+            for m0, number in zip(range(0, tiles, share), numbers):
+                bank = psum_bank(number, [P, share, P])
+                for m in range(m0, m0 + share):
+                    for r in range(2):
+                        nc.tensor.matmul(
+                            bank[:, m - m0, :],
+                            gated[r][:, m * P : (m + 1) * P],
+                            ident[:],
+                            start=(r == 0),
+                            stop=(r == 1),
+                            is_transpose=True,
+                        )
                 nc.scalar.copy(
-                    dh_t[n][:, :, :, 32 * b : 32 * (b + 1), :],
-                    bank[:, m0 - base : m1 - base, :].rearrange("t m (p u e) -> t m u p e", u=2, e=2),
+                    dh_t[n][:, m0 : m0 + share, :, 32 * b : 32 * (b + 1), :],
+                    bank[:].rearrange("t m (p u e) -> t m u p e", u=2, e=2),
                 )
 
         units = [(0, 4, 0), (0, 4, 1), (4, 8, 0), (8, 11, 0), (11, 12, 0), (4, 8, 1), (8, 12, 1)]
         for number, (e0, e1, b) in enumerate(units):
             experts_product(e0, e1, b, number)
         a_sb = held([P, 4, T], F32, "a_sb")
-        for t0, t1 in ((0, 512), (512, T)):
+        for t0, t1 in TOKEN_CHUNKS:
             nc.sync.dma_start(a_sb[:, :, t0:t1], a.rearrange("(p j) t -> p j t", j=4)[:, :, t0:t1])
-        gathered = [gated_gathers(b, 0, 6) for b in range(2)]
-        for e0, b, number in ((0, 2, 7), (4, 2, 0), (0, 3, 1), (4, 3, 2)):
-            experts_product(e0, e0 + 4, b, number)
-        summed(gathered[0], 0, (0, 1), 7)
-        summed(gathered[0], 0, (2, 3), 0)
-        for b, number in ((2, 3), (3, 4)):
-            experts_product(8, 12, b, number)
-        summed(gathered[1], 1, (0, 1), 3)
-        summed(gathered[1], 1, (2, 3), 4)
+        for group, banks in enumerate(((7, 0), (1, 2), (3, 4))):
+            for b, number in zip((2, 3), banks):
+                experts_product(4 * group, 4 * group + 4, b, number)
+            if group < 2:
+                token_step(group, 0, banks[0])
 
         w1_s = late([P, K], U8, "w1_s", "then_w1_s")
         nc.vector.memset(w1_s[:].bitcast(I32), 0)
@@ -195,38 +184,38 @@ def tile_moe_sub_relu_kernel(
         w1_w = late([P, K], U32, "w1_w", "then_slot_s")
         nc.sync.dma_start(w1_w[:].bitcast(I32), w1t_words[0].rearrange("p k d -> p (k d)").bitcast(I32))
 
+        for n, b, number in ((0, 1, 4), (1, 1, 3), (0, 2, 2), (0, 3, 0), (1, 2, 7)):
+            token_step(n, b, number)
+
         def side_by_side(mask, t0, t1):
             return mask.rearrange("p (c i) j -> p c j i", i=2), a_sb[:, :, t0:t1].rearrange("p j (c i) -> p c j i", i=2)
 
-        relu_on = [late([P, c1 - c0, 4], BF16, f"relu_on{n}", f"then_relu{n}") for n, (c0, c1) in enumerate(((0, 512), (512, T)))]
-
-        def relu_mask(n, c0, c1):
+        (t0, t1), (t2, t3) = TOKEN_CHUNKS
+        relu_on = [late([P, c1 - c0, 4], BF16, f"relu_on{n}", f"then_relu{n}") for n, (c0, c1) in enumerate(TOKEN_CHUNKS)]
+        for mask, (c0, c1) in zip(relu_on, TOKEN_CHUNKS):
             for m in range(c0, c1, P):
-                nc.scalar.activation(*side_by_side(relu_on[n][:, m - c0 : m - c0 + P, :], m, m + P), SIGN)
-            nc.vector.tensor_scalar_max(relu_on[n][:], relu_on[n][:], 0.0)
+                piece = mask[:, m - c0 : m - c0 + P, :]
+                nc.scalar.activation(*side_by_side(piece, m, m + P), SIGN)
+            nc.vector.tensor_scalar_max(mask[:], mask[:], 0.0)
 
-        da = held([P, T, 4], BF16, "da")
-
-        def masked_words(n, number):
-            m0, m1 = PIECES[n]
-            bank = psum_bank(number, [P, 2, (m1 - m0) * P])
-            for m in range(m1 - m0):
+        def masked_words(da, n, m0, tiles, number):
+            bank = psum_bank(number, [P, 2, tiles * P])
+            for m in range(tiles):
                 for u in range(2):
-                    words = dh_t[n][:, m, u].rearrange("t p e -> t (p e)").bitcast(F32)
+                    words = dh_t[n][:, m0 + m, u].rearrange("t p e -> t (p e)").bitcast(F32)
                     nc.tensor.transpose(bank[:, u, m * P : (m + 1) * P], words, ident[:])
-            mask = relu_on[m0 // 4][:, (m0 % 4) * P : (m0 % 4 + m1 - m0) * P, :]
             nc.vector.tensor_tensor(
-                da[:, m0 * P : m1 * P, :].rearrange("p t (u e) -> p t u e", u=2),
+                da.rearrange("p t (u e) -> p t u e", u=2),
                 bank[:].bitcast(BF16).rearrange("p u (t e) -> p t u e", e=2),
-                mask.rearrange("p t (u e) -> p t u e", u=2),
+                relu_on[n][:, m0 * P : (m0 + tiles) * P, :].rearrange("p t (u e) -> p t u e", u=2),
                 MULT,
             )
 
-        def first_layer(t0, t1, number):
+        def first_layer(da, t0, t1, number):
             width = t1 - t0
             da_w = held([P, width], U32, f"da_w{t0}")
             da_s = held([P, width], U8, f"da_s{t0}")
-            nc.vector.quantize_mx(da_w[:].bitcast(FP8X4), da_s[:], da[:, t0:t1, :].rearrange("p t j -> p (t j)"))
+            nc.vector.quantize_mx(da_w[:].bitcast(FP8X4), da_s[:], da.rearrange("p t j -> p (t j)"))
             bank = psum_bank(number, [P, width])
             nc.tensor.matmul_mx(
                 out=bank[:],
@@ -241,19 +230,12 @@ def tile_moe_sub_relu_kernel(
             nc.scalar.copy(result[:], bank[:])
             nc.sync.dma_start(out[:, t0:t1], result[:])
 
-        summed(gated_gathers(2, 0, 4), 2, (0, 1), 5)
-        relu_mask(0, 0, 512)
-        last_of_first = gated_gathers(3, 0, 4)
-        summed(last_of_first, 3, (0,), 6)
-        summed(last_of_first, 3, (1,), 1)
-        masked_words(0, 2)
-        masked_words(1, 7)
-        summed(gated_gathers(2, 4, 6), 2, (2, 3), 6)
-        relu_mask(1, 512, T)
-        summed(gated_gathers(3, 4, 5), 3, (2,), 1)
-        masked_words(2, 0)
-        summed(gated_gathers(3, 5, 6), 3, (3,), 6)
-        first_layer(0, 512, 3)
-        masked_words(3, 4)
-        first_layer(512, 640, 5)
-        first_layer(640, T, 1)
+        da = held([P, T, 4], BF16, "da")
+        for m0, number in ((0, 5), (2, 6)):
+            masked_words(da[:, m0 * P : (m0 + 2) * P, :], 0, m0, 2, number)
+        token_step(1, 3, 0, 7)
+        first_layer(da[:, t0:t1, :], t0, t1, 3)
+        for m0, number in ((0, 2), (1, 1)):
+            masked_words(da[:, t2 + m0 * P : t2 + (m0 + 1) * P, :], 1, m0, 1, number)
+        for m0, number in ((0, 4), (1, 5)):
+            first_layer(da[:, t2 + m0 * P : t2 + (m0 + 1) * P, :], t2 + m0 * P, t2 + (m0 + 1) * P, number)

@@ -42,7 +42,7 @@ def tile_moe_sub_relu_kernel(
 
         offs_sb = keep.tile([P, SLOTS // 16], U16, name="offs_sb")
         pos_sb = [keep.tile([P, T // 16], U16, name=f"pos{r}_sb") for r in range(2)]
-        dy_s = late([P, T], U8, "dy_s", "then_gate")
+        dy_s = held([P, T], U8, "dy_s")
         dy_w = held([P, PASSES, T], U32, "dy_w")
         slot_w = [late([P, SLOTS], U32, f"slot_w{s}", f"then_relu{s}") for s in range(PASSES)]
         y = [held([P, SLOTS], F32, f"y{b}") for b in range(ROW_TILES)]
@@ -80,10 +80,7 @@ def tile_moe_sub_relu_kernel(
         nc.sync.dma_start(dy_w[:].bitcast(I32), dy_words.rearrange("s p t d -> p s (t d)").bitcast(I32))
         for r in range(4):
             load_w2_scales(nc.sync, 0, r)
-        for e0 in range(0, E, 4):
-            load_w2_words(0, e0, e0 + 4)
-        for r in range(2):
-            nc.sync.dma_start(pos_sb[r][:], (pos1, pos2)[r])
+        load_w2_words(0, 0, 4)
 
         def psum_bank(number, shape):
             return psum.tile(shape, F32, name=f"bank{number}", tag=f"bank{number}")
@@ -94,10 +91,14 @@ def tile_moe_sub_relu_kernel(
 
         for j0 in range(0, SLOTS, 512):
             nc.vector.tensor_copy(slot_s[0][:, j0 : j0 + 512], dy_s[:].indirect(offs_sb[:, j0 // 16 : (j0 + 512) // 16]))
-        for j0, j1 in ((0, 512), (512, SLOTS)):
-            nc.scalar.dma_start(slot_s[1][0:112, j0:j1].bitcast(I32), slot_s[0][4:116, j0:j1].bitcast(I32))
+        for x in range(4):
+            nc.sync.dma_start(slot_s[1][x:P:32].bitcast(I32), slot_s[0][4 + x : P : 32].bitcast(I32))
+        for e0 in range(4, E, 4):
+            load_w2_words(0, e0, e0 + 4)
+        for r in range(2):
+            nc.sync.dma_start(pos_sb[r][:], (pos1, pos2)[r])
 
-        gate_sb = late([P, 2 * T], F32, "gate_sb", "then_gate")
+        gate_sb = held([P, 2 * T], F32, "gate_sb")
         for quarter in range(4):
             bank = psum_bank(4 + quarter, [P, 4, P])
             for x in range(4):

@@ -23,7 +23,7 @@ PASSES = N // 512
 ROW_TILES = H // P
 EXPERT_UNITS = ((0, 4), (4, 8), (8, 11), (11, 12))
 GATE_ROWS, GATE_RUN = 16, 96
-TOKEN_CHUNKS = ((0, 512), (512, 768))
+PIECES = ((0, 2), (2, 4), (4, 5), (5, 6))
 
 
 def tile_moe_sub_relu_kernel(
@@ -63,15 +63,14 @@ def tile_moe_sub_relu_kernel(
         w2_s = [late([P, E * PASSES, 2 * P], U8, "w2_s0", "then_w1_s"), held([P, E * PASSES, 2 * P], U8, "w2_s1")]
         nc.vector.memset(dy_s[:].bitcast(I32), 0)
         nc.vector.memset(gate_rows[:], 0.0)
-        blank = late([P, P], F32, "blank", "then_slot_s")
-        nc.gpsimd.memset(blank[:], 0.0)
+        nc.gpsimd.memset(ident[:], 0.0)
         nc.gpsimd.affine_select(
-            out=ident[:], in_=blank[:], compare_op=NOT_EQUAL, fill=1.0, base=0, pattern=[[-1, P]], channel_multiplier=1
+            out=ident[:], in_=ident[:], compare_op=NOT_EQUAL, fill=1.0, base=0, pattern=[[-1, P]], channel_multiplier=1
         )
         slot_s = [held([P, SLOTS], U8, "slot_s0"), late([P, SLOTS], U8, "slot_s1", "then_slot_s")]
-        nc.gpsimd.memset(slot_s[1][:].bitcast(I32), 0)
         nc.vector.memset(w2_s[0][:].bitcast(I32), 0)
         nc.vector.memset(w2_s[1][:].bitcast(I32), 0)
+        nc.vector.memset(slot_s[1][:].bitcast(I32), 0)
 
         nc.sync.dma_start(offs_sb[:], offs)
         nc.scalar.dma_start(gate_rows[0:GATE_ROWS, 0:GATE_RUN], gate[:, 0, :].rearrange("r (m n) -> r m n", n=GATE_RUN))
@@ -80,7 +79,7 @@ def tile_moe_sub_relu_kernel(
         nc.sync.dma_start(dy_w[:].bitcast(I32), dy_words.rearrange("s p t d -> p s (t d)").bitcast(I32))
         for r in range(4):
             load_w2_scales(nc.sync, 0, r)
-        load_w2_words(0, 0, 4)
+        load_w2_words(0, 0, 6)
 
         def psum_bank(number, shape):
             return psum.tile(shape, F32, name=f"bank{number}", tag=f"bank{number}")
@@ -93,8 +92,8 @@ def tile_moe_sub_relu_kernel(
             nc.vector.tensor_copy(slot_s[0][:, j0 : j0 + 512], dy_s[:].indirect(offs_sb[:, j0 // 16 : (j0 + 512) // 16]))
         for x in range(4):
             nc.sync.dma_start(slot_s[1][x:P:32].bitcast(I32), slot_s[0][4 + x : P : 32].bitcast(I32))
-        for e0 in range(4, E, 4):
-            load_w2_words(0, e0, e0 + 4)
+        load_w2_words(0, 6, 10)
+        load_w2_words(0, 10, E)
         for r in range(2):
             nc.sync.dma_start(pos_sb[r][:], (pos1, pos2)[r])
 
@@ -110,8 +109,8 @@ def tile_moe_sub_relu_kernel(
             )
         for r in range(4):
             load_w2_scales(nc.sync, 1, r)
-        for e0 in range(0, E, 4):
-            load_w2_words(1, e0, e0 + 4)
+        for e0, e1 in ((0, 4), (4, 8), (8, 10), (10, E)):
+            load_w2_words(1, e0, e1)
 
         for e0, e1 in EXPERT_UNITS:
             for s in range(PASSES):
@@ -136,47 +135,56 @@ def tile_moe_sub_relu_kernel(
                     )
             nc.scalar.copy(y[b][:, e0 * C : e1 * C], bank[:])
 
-        dh_t = [held([P, (t1 - t0) // P, 2, P, 2], BF16, f"dh_t{t0}") for t0, t1 in TOKEN_CHUNKS]
+        dh_t = [held([P, m1 - m0, 2, P, 2], BF16, f"dh_t{m0}") for m0, m1 in PIECES]
 
-        def token_step(n, b, *numbers):
-            t0, t1 = TOKEN_CHUNKS[n]
-            tiles = (t1 - t0) // P
+        def gated_gathers(b, m0, m1):
             gated = []
             for r in range(2):
-                u = late([P, t1 - t0], F32, f"gated{n}{b}{r}", f"gated{n}{b}{r}")
+                u = held([P, (m1 - m0) * P], F32, f"gated{b}{m0}{r}")
                 nc.vector.tensor_tensor(
-                    u[:], y[b][:].indirect(pos_sb[r][:, t0 // 16 : t1 // 16]), gate_sb[:, r * T + t0 : r * T + t1], MULT
+                    u[:],
+                    y[b][:].indirect(pos_sb[r][:, m0 * P // 16 : m1 * P // 16]),
+                    gate_sb[:, r * T + m0 * P : r * T + m1 * P],
+                    MULT,
                 )
                 gated.append(u)
-            share = tiles // len(numbers)
-            for m0, number in zip(range(0, tiles, share), numbers):
-                bank = psum_bank(number, [P, share, P])
-                for m in range(m0, m0 + share):
-                    for r in range(2):
-                        nc.tensor.matmul(
-                            bank[:, m - m0, :],
-                            gated[r][:, m * P : (m + 1) * P],
-                            ident[:],
-                            start=(r == 0),
-                            stop=(r == 1),
-                            is_transpose=True,
-                        )
+            return m0, gated
+
+        def summed(gathered, b, pieces, number):
+            first, gated = gathered
+            base = PIECES[pieces[0]][0]
+            bank = psum_bank(number, [P, PIECES[pieces[-1]][1] - base, P])
+            for m in range(base, PIECES[pieces[-1]][1]):
+                for r in range(2):
+                    nc.tensor.matmul(
+                        bank[:, m - base, :],
+                        gated[r][:, (m - first) * P : (m - first + 1) * P],
+                        ident[:],
+                        start=(r == 0),
+                        stop=(r == 1),
+                        is_transpose=True,
+                    )
+            for n in pieces:
+                m0, m1 = PIECES[n]
                 nc.scalar.copy(
-                    dh_t[n][:, m0 : m0 + share, :, 32 * b : 32 * (b + 1), :],
-                    bank[:].rearrange("t m (p u e) -> t m u p e", u=2, e=2),
+                    dh_t[n][:, :, :, 32 * b : 32 * (b + 1), :],
+                    bank[:, m0 - base : m1 - base, :].rearrange("t m (p u e) -> t m u p e", u=2, e=2),
                 )
 
-        units = [(0, 4, 0), (0, 4, 1), (4, 8, 0), (8, 11, 0), (11, 12, 0), (4, 8, 1), (8, 12, 1)]
-        for number, (e0, e1, b) in enumerate(units):
+        units = [(0, 4, 0, 0), (0, 4, 1, 1), (4, 8, 0, 2), (8, 11, 0, 3), (11, 12, 0, 4), (4, 8, 1, 3), (8, 12, 1, 6)]
+        for e0, e1, b, number in units:
             experts_product(e0, e1, b, number)
         a_sb = held([P, 4, T], F32, "a_sb")
-        for t0, t1 in TOKEN_CHUNKS:
+        for t0, t1 in ((0, 512), (512, T)):
             nc.sync.dma_start(a_sb[:, :, t0:t1], a.rearrange("(p j) t -> p j t", j=4)[:, :, t0:t1])
-        for group, banks in enumerate(((7, 0), (1, 2), (3, 4))):
+        for group, (m0, m1, pieces, banks) in enumerate(((0, 4, (0, 1), (7, 0)), (4, 6, (2, 3), (1, 2)))):
             for b, number in zip((2, 3), banks):
                 experts_product(4 * group, 4 * group + 4, b, number)
-            if group < 2:
-                token_step(group, 0, banks[0])
+            summed(gated_gathers(0, m0, m1), 0, pieces, banks[0])
+        for e0, e1, b, number in ((8, 10, 2, 3), (10, E, 2, 5), (8, E, 3, 4)):
+            experts_product(e0, e1, b, number)
+        summed(gated_gathers(1, 0, 4), 1, (0, 1), 4)
+        summed(gated_gathers(1, 4, 6), 1, (2, 3), 3)
 
         w1_s = late([P, K], U8, "w1_s", "then_w1_s")
         nc.vector.memset(w1_s[:].bitcast(I32), 0)
@@ -185,38 +193,42 @@ def tile_moe_sub_relu_kernel(
         w1_w = late([P, K], U32, "w1_w", "then_slot_s")
         nc.sync.dma_start(w1_w[:].bitcast(I32), w1t_words[0].rearrange("p k d -> p (k d)").bitcast(I32))
 
-        for n, b, number in ((0, 1, 4), (1, 1, 3), (0, 2, 2), (0, 3, 0), (1, 2, 7)):
-            token_step(n, b, number)
-
         def side_by_side(mask, t0, t1):
             return mask.rearrange("p (c i) j -> p c j i", i=2), a_sb[:, :, t0:t1].rearrange("p j (c i) -> p c j i", i=2)
 
-        (t0, t1), (t2, t3) = TOKEN_CHUNKS
-        relu_on = [late([P, c1 - c0, 4], BF16, f"relu_on{n}", f"then_relu{n}") for n, (c0, c1) in enumerate(TOKEN_CHUNKS)]
-        for mask, (c0, c1) in zip(relu_on, TOKEN_CHUNKS):
-            for m in range(c0, c1, P):
-                piece = mask[:, m - c0 : m - c0 + P, :]
-                nc.scalar.activation(*side_by_side(piece, m, m + P), SIGN)
-            nc.vector.tensor_scalar_max(mask[:], mask[:], 0.0)
+        relu_on = [late([P, c1 - c0, 4], BF16, f"relu_on{n}", f"then_relu{n}") for n, (c0, c1) in enumerate(((0, 512), (512, T)))]
 
-        def masked_words(da, n, m0, tiles, number):
-            bank = psum_bank(number, [P, 2, tiles * P])
-            for m in range(tiles):
+        def relu_mask(n, c0, c1):
+            for m in range(c0, c1, P):
+                nc.scalar.activation(*side_by_side(relu_on[n][:, m - c0 : m - c0 + P, :], m, m + P), SIGN)
+            nc.vector.tensor_scalar_max(relu_on[n][:], relu_on[n][:], 0.0)
+
+        da = held([P, T, 4], BF16, "da")
+
+        def turned_words(n, number):
+            m0, m1 = PIECES[n]
+            bank = psum_bank(number, [P, 2, (m1 - m0) * P])
+            for m in range(m1 - m0):
                 for u in range(2):
-                    words = dh_t[n][:, m0 + m, u].rearrange("t p e -> t (p e)").bitcast(F32)
+                    words = dh_t[n][:, m, u].rearrange("t p e -> t (p e)").bitcast(F32)
                     nc.tensor.transpose(bank[:, u, m * P : (m + 1) * P], words, ident[:])
+            return bank
+
+        def masked(n, bank):
+            m0, m1 = PIECES[n]
+            mask = relu_on[m0 // 4][:, (m0 % 4) * P : (m0 % 4 + m1 - m0) * P, :]
             nc.vector.tensor_tensor(
-                da.rearrange("p t (u e) -> p t u e", u=2),
+                da[:, m0 * P : m1 * P, :].rearrange("p t (u e) -> p t u e", u=2),
                 bank[:].bitcast(BF16).rearrange("p u (t e) -> p t u e", e=2),
-                relu_on[n][:, m0 * P : (m0 + tiles) * P, :].rearrange("p t (u e) -> p t u e", u=2),
+                mask.rearrange("p t (u e) -> p t u e", u=2),
                 MULT,
             )
 
-        def first_layer(da, t0, t1, number):
+        def first_layer(t0, t1, number, copy_out):
             width = t1 - t0
             da_w = held([P, width], U32, f"da_w{t0}")
             da_s = held([P, width], U8, f"da_s{t0}")
-            nc.vector.quantize_mx(da_w[:].bitcast(FP8X4), da_s[:], da.rearrange("p t j -> p (t j)"))
+            nc.vector.quantize_mx(da_w[:].bitcast(FP8X4), da_s[:], da[:, t0:t1, :].rearrange("p t j -> p (t j)"))
             bank = psum_bank(number, [P, width])
             nc.tensor.matmul_mx(
                 out=bank[:],
@@ -228,15 +240,25 @@ def tile_moe_sub_relu_kernel(
                 stop=True,
             )
             result = held([P, width], F32, f"result{t0}")
-            nc.scalar.copy(result[:], bank[:])
+            copy_out(result[:], bank[:])
             nc.sync.dma_start(out[:, t0:t1], result[:])
 
-        da = held([P, T, 4], BF16, "da")
-        for m0, number in ((0, 5), (2, 6)):
-            masked_words(da[:, m0 * P : (m0 + 2) * P, :], 0, m0, 2, number)
-        token_step(1, 3, 0, 7)
-        first_layer(da[:, t0:t1, :], t0, t1, 3)
-        for m0, number in ((0, 2), (1, 1)):
-            masked_words(da[:, t2 + m0 * P : t2 + (m0 + 1) * P, :], 1, m0, 1, number)
-        for m0, number in ((0, 4), (1, 5)):
-            first_layer(da[:, t2 + m0 * P : t2 + (m0 + 1) * P, :], t2 + m0 * P, t2 + (m0 + 1) * P, number)
+        turned = []
+        for n, banks in enumerate(((2, 0, 6), (7, 1, 5))):
+            for b in (2, 3):
+                summed(gated_gathers(b, *PIECES[n]), b, (n,), banks[b - 2])
+            turned.append(turned_words(n, banks[2]))
+        summed(gated_gathers(2, 4, 6), 2, (2, 3), 4)
+        relu_mask(0, 0, 512)
+        relu_mask(1, 512, T)
+        for n in range(2):
+            masked(n, turned[n])
+        last = gated_gathers(3, 4, 6)
+        summed(last, 3, (2,), 3)
+        summed(last, 3, (3,), 2)
+        first_layer(0, 256, 1, nc.scalar.copy)
+        masked(2, turned_words(2, 0))
+        first_layer(256, 512, 6, nc.scalar.copy)
+        masked(3, turned_words(3, 7))
+        first_layer(512, 640, 4, nc.scalar.copy)
+        first_layer(640, T, 3, nc.vector.tensor_copy)

@@ -79,7 +79,7 @@ def tile_moe_sub_relu_kernel(
         nc.sync.dma_start(dy_w[:].bitcast(I32), dy_words.rearrange("s p t d -> p s (t d)").bitcast(I32))
         for r in range(4):
             load_w2_scales(nc.sync, 0, r)
-        load_w2_words(0, 0, 6)
+        load_w2_words(0, 0, 4)
 
         def psum_bank(number, shape):
             return psum.tile(shape, F32, name=f"bank{number}", tag=f"bank{number}")
@@ -92,8 +92,8 @@ def tile_moe_sub_relu_kernel(
             nc.vector.tensor_copy(slot_s[0][:, j0 : j0 + 512], dy_s[:].indirect(offs_sb[:, j0 // 16 : (j0 + 512) // 16]))
         for x in range(4):
             nc.sync.dma_start(slot_s[1][x:P:32].bitcast(I32), slot_s[0][4 + x : P : 32].bitcast(I32))
-        load_w2_words(0, 6, 10)
-        load_w2_words(0, 10, E)
+        load_w2_words(0, 4, 8)
+        load_w2_words(0, 8, E)
         for r in range(2):
             nc.sync.dma_start(pos_sb[r][:], (pos1, pos2)[r])
 

@@ -73,9 +73,9 @@ def tile_moe_sub_relu_kernel(
         nc.vector.memset(slot_s[1][:].bitcast(I32), 0)
 
         nc.sync.dma_start(offs_sb[:], offs)
-        nc.scalar.dma_start(gate_rows[0:GATE_ROWS, 0:GATE_RUN], gate[:, 0, :].rearrange("r (m n) -> r m n", n=GATE_RUN))
-        for q in range(4):
-            nc.sync.dma_start(dy_s[32 * q : 32 * q + 8, :].bitcast(I32), dy_scales[:, 4 * q : 4 * q + 4, :].bitcast(I32))
+        nc.scalar.dma_start(gate_rows[0:GATE_ROWS, 0:GATE_RUN], gate[:, 0, :].rearrange("r (m n) -> m r n", n=GATE_RUN))
+        for r in range(4):
+            nc.sync.dma_start(dy_s[r:P:16].bitcast(I32), dy_scales.rearrange("s (q r) t -> r q s t", r=4)[r].bitcast(I32))
         nc.sync.dma_start(dy_w[:].bitcast(I32), dy_words.rearrange("s p t d -> p s (t d)").bitcast(I32))
         for r in range(4):
             load_w2_scales(nc.sync, 0, r)
@@ -91,7 +91,7 @@ def tile_moe_sub_relu_kernel(
         for j0 in range(0, SLOTS, 512):
             nc.vector.tensor_copy(slot_s[0][:, j0 : j0 + 512], dy_s[:].indirect(offs_sb[:, j0 // 16 : (j0 + 512) // 16]))
         for x in range(4):
-            nc.sync.dma_start(slot_s[1][x:P:32].bitcast(I32), slot_s[0][4 + x : P : 32].bitcast(I32))
+            nc.sync.dma_start(slot_s[1][x:P:32].bitcast(I32), slot_s[0][16 + x : P : 32].bitcast(I32))
         load_w2_words(0, 4, 8)
         load_w2_words(0, 8, E)
         for r in range(2):
@@ -104,8 +104,8 @@ def tile_moe_sub_relu_kernel(
                 row = 4 * quarter + x
                 nc.tensor.transpose(bank[:, x, :], gate_cols[:, row : row + 1].to_broadcast([P, P]), ident[:])
             nc.scalar.copy(
-                gate_sb[:, 4 * GATE_RUN * quarter : 4 * GATE_RUN * (quarter + 1)].rearrange("p (x n) -> p x n", x=4),
-                bank[:, :, 0:GATE_RUN],
+                gate_sb[:].rearrange("p (r m n) -> p m r n", r=2, n=GATE_RUN)[:, 2 * quarter : 2 * quarter + 2],
+                bank[:, :, 0:GATE_RUN].rearrange("p (m r) n -> p m r n", r=2),
             )
         for r in range(4):
             load_w2_scales(nc.sync, 1, r)
@@ -177,14 +177,15 @@ def tile_moe_sub_relu_kernel(
         a_sb = held([P, 4, T], F32, "a_sb")
         for t0, t1 in ((0, 512), (512, T)):
             nc.sync.dma_start(a_sb[:, :, t0:t1], a.rearrange("(p j) t -> p j t", j=4)[:, :, t0:t1])
-        for group, (m0, m1, pieces, banks) in enumerate(((0, 4, (0, 1), (7, 0)), (4, 6, (2, 3), (1, 2)))):
-            for b, number in zip((2, 3), banks):
-                experts_product(4 * group, 4 * group + 4, b, number)
-            summed(gated_gathers(0, m0, m1), 0, pieces, banks[0])
-        for e0, e1, b, number in ((8, 10, 2, 3), (10, E, 2, 5), (8, E, 3, 4)):
+        for e0, e1, b, number in ((0, 4, 2, 7), (0, 4, 3, 0)):
             experts_product(e0, e1, b, number)
-        summed(gated_gathers(1, 0, 4), 1, (0, 1), 4)
-        summed(gated_gathers(1, 4, 6), 1, (2, 3), 3)
+        summed(gated_gathers(0, 0, 4), 0, (0, 1), 7)
+        for e0, e1, b, number in ((4, 8, 2, 1), (4, 8, 3, 2), (8, 10, 2, 3), (10, E, 2, 5), (8, E, 3, 4)):
+            experts_product(e0, e1, b, number)
+        summed(gated_gathers(0, 4, 6), 0, (2, 3), 5)
+        gathered = gated_gathers(1, 0, 6)
+        summed(gathered, 1, (0, 1), 4)
+        summed(gathered, 1, (2, 3), 3)
 
         w1_s = late([P, K], U8, "w1_s", "then_w1_s")
         nc.vector.memset(w1_s[:].bitcast(I32), 0)
@@ -198,10 +199,9 @@ def tile_moe_sub_relu_kernel(
 
         relu_on = [late([P, c1 - c0, 4], BF16, f"relu_on{n}", f"then_relu{n}") for n, (c0, c1) in enumerate(((0, 512), (512, T)))]
 
-        def relu_mask(n, c0, c1):
+        def signs(n, c0, c1):
             for m in range(c0, c1, P):
                 nc.scalar.activation(*side_by_side(relu_on[n][:, m - c0 : m - c0 + P, :], m, m + P), SIGN)
-            nc.vector.tensor_scalar_max(relu_on[n][:], relu_on[n][:], 0.0)
 
         da = held([P, T, 4], BF16, "da")
 
@@ -243,22 +243,24 @@ def tile_moe_sub_relu_kernel(
             copy_out(result[:], bank[:])
             nc.sync.dma_start(out[:, t0:t1], result[:])
 
+        for n, (c0, c1) in enumerate(((0, 512), (512, T))):
+            signs(n, c0, c1)
+        summed(gated_gathers(2, 0, 4), 2, (0, 1), 4)
         turned = []
-        for n, banks in enumerate(((2, 0, 6), (7, 1, 5))):
-            for b in (2, 3):
-                summed(gated_gathers(b, *PIECES[n]), b, (n,), banks[b - 2])
-            turned.append(turned_words(n, banks[2]))
-        summed(gated_gathers(2, 4, 6), 2, (2, 3), 4)
-        relu_mask(0, 0, 512)
-        relu_mask(1, 512, T)
-        for n in range(2):
-            masked(n, turned[n])
+        for n, banks in enumerate(((3, 6), (4, 0))):
+            summed(gated_gathers(3, *PIECES[n]), 3, (n,), banks[0])
+            turned.append(turned_words(n, banks[1]))
+        summed(gated_gathers(2, 4, 6), 2, (2, 3), 3)
         last = gated_gathers(3, 4, 6)
-        summed(last, 3, (2,), 3)
-        summed(last, 3, (3,), 2)
-        first_layer(0, 256, 1, nc.scalar.copy)
-        masked(2, turned_words(2, 0))
-        first_layer(256, 512, 6, nc.scalar.copy)
-        masked(3, turned_words(3, 7))
+        summed(last, 3, (2,), 4)
+        summed(last, 3, (3,), 3)
+        for n in range(2):
+            nc.vector.tensor_scalar_max(relu_on[n][:], relu_on[n][:], 0.0)
+        masked(0, turned[0])
+        masked(1, turned[1])
+        first_layer(0, 256, 5, nc.scalar.copy)
+        masked(2, turned_words(2, 1))
+        first_layer(256, 512, 7, nc.scalar.copy)
+        masked(3, turned_words(3, 2))
         first_layer(512, 640, 4, nc.scalar.copy)
         first_layer(640, T, 3, nc.vector.tensor_copy)

@@ -14,7 +14,8 @@ U8 = mybir.dt.uint8
 FP8X4 = mybir.dt.float8_e4m3fn_x4
 FP4X4 = mybir.dt.float4_e2m1fn_x4
 MULT = mybir.AluOpType.mult
-NOT_EQUAL = mybir.AluOpType.not_equal
+ABS = mybir.ActivationFunctionType.Abs
+RELU = mybir.ActivationFunctionType.Relu
 SIGN = mybir.ActivationFunctionType.Sign
 
 P = 128
@@ -63,10 +64,7 @@ def tile_moe_sub_relu_kernel(
         w2_s = [late([P, E * PASSES, 2 * P], U8, "w2_s0", "then_w1_s"), held([P, E * PASSES, 2 * P], U8, "w2_s1")]
         nc.vector.memset(dy_s[:].bitcast(I32), 0)
         nc.vector.memset(gate_rows[:], 0.0)
-        nc.gpsimd.memset(ident[:], 0.0)
-        nc.gpsimd.affine_select(
-            out=ident[:], in_=ident[:], compare_op=NOT_EQUAL, fill=1.0, base=0, pattern=[[-1, P]], channel_multiplier=1
-        )
+        nc.gpsimd.iota(ident[:], pattern=[[-1, P]], base=0, channel_multiplier=1, allow_small_or_imprecise_dtypes=True)
         slot_s = [held([P, SLOTS], U8, "slot_s0"), late([P, SLOTS], U8, "slot_s1", "then_slot_s")]
         nc.vector.memset(w2_s[0][:].bitcast(I32), 0)
         nc.vector.memset(w2_s[1][:].bitcast(I32), 0)
@@ -80,6 +78,9 @@ def tile_moe_sub_relu_kernel(
         for r in range(4):
             load_w2_scales(nc.sync, 0, r)
         load_w2_words(0, 0, 4)
+
+        nc.scalar.activation(ident[:], ident[:], ABS)
+        nc.scalar.activation(ident[:], ident[:], RELU, bias=1.0, scale=-1.0)
 
         def psum_bank(number, shape):
             return psum.tile(shape, F32, name=f"bank{number}", tag=f"bank{number}")

@@ -246,12 +246,12 @@ def tile_moe_sub_relu_kernel(
 
         for n, (c0, c1) in enumerate(((0, 512), (512, T))):
             signs(n, c0, c1)
-        summed(gated_gathers(2, 0, 4), 2, (0, 1), 4)
+        summed(gated_gathers(2, 0, 4), 2, (0, 1), 5)
         turned = []
-        for n, banks in enumerate(((3, 6), (4, 0))):
+        for n, banks in enumerate(((4, 6), (3, 0))):
             summed(gated_gathers(3, *PIECES[n]), 3, (n,), banks[0])
             turned.append(turned_words(n, banks[1]))
-        summed(gated_gathers(2, 4, 6), 2, (2, 3), 3)
+        summed(gated_gathers(2, 4, 6), 2, (2, 3), 5)
         last = gated_gathers(3, 4, 6)
         summed(last, 3, (2,), 4)
         summed(last, 3, (3,), 3)
@@ -259,9 +259,10 @@ def tile_moe_sub_relu_kernel(
             nc.vector.tensor_scalar_max(relu_on[n][:], relu_on[n][:], 0.0)
         masked(0, turned[0])
         masked(1, turned[1])
-        first_layer(0, 256, 5, nc.scalar.copy)
-        masked(2, turned_words(2, 1))
-        first_layer(256, 512, 7, nc.scalar.copy)
-        masked(3, turned_words(3, 2))
-        first_layer(512, 640, 4, nc.scalar.copy)
-        first_layer(640, T, 3, nc.vector.tensor_copy)
+        turned.extend([turned_words(2, 1), turned_words(3, 2)])
+        first_layer(0, 256, 3, nc.scalar.copy)
+        masked(2, turned[2])
+        first_layer(256, 512, 4, nc.scalar.copy)
+        masked(3, turned[3])
+        first_layer(512, 640, 5, nc.scalar.copy)
+        first_layer(640, T, 7, nc.vector.tensor_copy)

@@ -14,17 +14,19 @@ U8 = mybir.dt.uint8
 FP8X4 = mybir.dt.float8_e4m3fn_x4
 FP4X4 = mybir.dt.float4_e2m1fn_x4
 MULT = mybir.AluOpType.mult
+ADD = mybir.AluOpType.add
+IS_GT = mybir.AluOpType.is_gt
 ABS = mybir.ActivationFunctionType.Abs
 RELU = mybir.ActivationFunctionType.Relu
-SIGN = mybir.ActivationFunctionType.Sign
+COPY = mybir.ActivationFunctionType.Copy
 
 P = 128
 SLOTS = E * C
 PASSES = N // 512
 ROW_TILES = H // P
-EXPERT_UNITS = ((0, 4), (4, 8), (8, 11), (11, 12))
-GATE_ROWS, GATE_RUN = 16, 96
-PIECES = ((0, 2), (2, 4), (4, 5), (5, 6))
+BLOCKS = T // P
+GATE_ROWS, GATE_RUN = 4, 384
+SPREAD = 5
 
 
 def tile_moe_sub_relu_kernel(
@@ -35,59 +37,62 @@ def tile_moe_sub_relu_kernel(
         keep = ctx.enter_context(tc.tile_pool(name="keep", bufs=1))
         psum = ctx.enter_context(tc.psum_pool(name="psum", bufs=1))
 
-        def held(shape, dtype, name):
-            return keep.tile(shape, dtype, name=name, align_bytes=64)
+        def held(shape, dtype, name, tag=None):
+            return keep.tile(shape, dtype, name=name, tag=tag or name, align_bytes=64)
 
-        def late(shape, dtype, name, tag):
-            return keep.tile(shape, dtype, name=name, tag=tag, align_bytes=64)
+        def psum_bank(number, shape):
+            return psum.tile(shape, F32, name=f"bank{number}", tag=f"bank{number}")
 
         offs_sb = keep.tile([P, SLOTS // 16], U16, name="offs_sb")
         pos_sb = [keep.tile([P, T // 16], U16, name=f"pos{r}_sb") for r in range(2)]
         dy_s = held([P, T], U8, "dy_s")
         dy_w = held([P, PASSES, T], U32, "dy_w")
-        slot_w = [late([P, SLOTS], U32, f"slot_w{s}", f"then_relu{s}") for s in range(PASSES)]
+        slot_w = [held([P, SLOTS], U32, f"slot_w{s}") for s in range(PASSES)]
+        slot_s = [held([P, SLOTS], U8, f"slot_s{s}") for s in range(PASSES)]
         y = [held([P, SLOTS], F32, f"y{b}") for b in range(ROW_TILES)]
-        gate_rows = held([P, P], F32, "gate_rows")
-        gate_cols = held([P, GATE_ROWS], F32, "gate_cols")
+        gate_rows = held([P, GATE_RUN], F32, "gate_rows")
+        gate_cols = held([P, GATE_RUN // P, GATE_ROWS], F32, "gate_cols")
+        gate_wide = held([P, 2, SPREAD * P], F32, "gate_wide")
         ident = held([P, P], F32, "ident")
+        w2_w = [held([P, E * PASSES, H], U8, f"w2_w{half}") for half in range(2)]
+        w2_s = [held([P, E * PASSES, 2 * P], U8, f"w2_s{half}") for half in range(2)]
         w2_words = w2t_words.rearrange("e s p x -> p (e s) x")
         w2_rows = w2t_scales.rearrange("e s b i -> b (e s) i")
 
-        def load_w2_scales(queue, half, r):
-            queue.dma_start(w2_s[half][r:P:32].bitcast(I32), w2_rows[r:16:4, :, 2 * P * half : 2 * P * (half + 1)].bitcast(I32))
+        def load_w2_scales(half):
+            for r in range(4):
+                nc.sync.dma_start(
+                    w2_s[half][r:P:32].bitcast(I32), w2_rows[r:16:4, :, 2 * P * half : 2 * P * (half + 1)].bitcast(I32)
+                )
 
         def load_w2_words(half, e0, e1):
             rows = slice(e0 * PASSES, e1 * PASSES)
             nc.sync.dma_start(w2_w[half][:, rows].bitcast(I32), w2_words[:, rows, H * half : H * (half + 1)].bitcast(I32))
 
-        w2_w = [held([P, E * PASSES, H], U8, f"w2_w{half}") for half in range(2)]
-        w2_s = [late([P, E * PASSES, 2 * P], U8, "w2_s0", "then_w1_s"), held([P, E * PASSES, 2 * P], U8, "w2_s1")]
+        def gate_col(r, m):
+            return gate_cols[:, m % 3, 2 * r + m // 3 : 2 * r + m // 3 + 1]
+
         nc.vector.memset(dy_s[:].bitcast(I32), 0)
         nc.vector.memset(gate_rows[:], 0.0)
         nc.gpsimd.iota(ident[:], pattern=[[-1, P]], base=0, channel_multiplier=1, allow_small_or_imprecise_dtypes=True)
-        slot_s = [held([P, SLOTS], U8, "slot_s0"), late([P, SLOTS], U8, "slot_s1", "then_slot_s")]
         nc.vector.memset(w2_s[0][:].bitcast(I32), 0)
         nc.vector.memset(w2_s[1][:].bitcast(I32), 0)
         nc.vector.memset(slot_s[1][:].bitcast(I32), 0)
 
         nc.sync.dma_start(offs_sb[:], offs)
-        nc.scalar.dma_start(gate_rows[0:GATE_ROWS, 0:GATE_RUN], gate[:, 0, :].rearrange("r (m n) -> m r n", n=GATE_RUN))
+        nc.scalar.dma_start(gate_rows[0:GATE_ROWS, :], gate[:, 0, :].rearrange("r (h x) -> r h x", x=GATE_RUN))
         for r in range(4):
             nc.sync.dma_start(dy_s[r:P:16].bitcast(I32), dy_scales.rearrange("s (q r) t -> r q s t", r=4)[r].bitcast(I32))
         nc.sync.dma_start(dy_w[:].bitcast(I32), dy_words.rearrange("s p t d -> p s (t d)").bitcast(I32))
-        for r in range(4):
-            load_w2_scales(nc.sync, 0, r)
+        load_w2_scales(0)
         load_w2_words(0, 0, 4)
 
         nc.scalar.activation(ident[:], ident[:], ABS)
         nc.scalar.activation(ident[:], ident[:], RELU, bias=1.0, scale=-1.0)
-
-        def psum_bank(number, shape):
-            return psum.tile(shape, F32, name=f"bank{number}", tag=f"bank{number}")
-
-        bank = psum_bank(7, [P, P])
-        nc.tensor.transpose(bank[:], gate_rows[:], ident[:])
-        nc.scalar.copy(gate_cols[:], bank[:, 0:GATE_ROWS])
+        bank = psum_bank(7, [P, GATE_RUN // P, P])
+        for k in range(GATE_RUN // P):
+            nc.tensor.transpose(bank[:, k, :], gate_rows[:, k * P : (k + 1) * P], ident[:])
+        nc.scalar.copy(gate_cols[:], bank[:, :, 0:GATE_ROWS])
 
         for j0 in range(0, SLOTS, 512):
             nc.vector.tensor_copy(slot_s[0][:, j0 : j0 + 512], dy_s[:].indirect(offs_sb[:, j0 // 16 : (j0 + 512) // 16]))
@@ -98,22 +103,28 @@ def tile_moe_sub_relu_kernel(
         for r in range(2):
             nc.sync.dma_start(pos_sb[r][:], (pos1, pos2)[r])
 
-        gate_sb = held([P, 2 * T], F32, "gate_sb")
-        for quarter in range(4):
-            bank = psum_bank(4 + quarter, [P, 4, P])
-            for x in range(4):
-                row = 4 * quarter + x
-                nc.tensor.transpose(bank[:, x, :], gate_cols[:, row : row + 1].to_broadcast([P, P]), ident[:])
-            nc.scalar.copy(
-                gate_sb[:].rearrange("p (r m n) -> p m r n", r=2, n=GATE_RUN)[:, 2 * quarter : 2 * quarter + 2],
-                bank[:, :, 0:GATE_RUN].rearrange("p (m r) n -> p m r n", r=2),
-            )
-        for r in range(4):
-            load_w2_scales(nc.sync, 1, r)
-        for e0, e1 in ((0, 4), (4, 8), (8, 10), (10, E)):
-            load_w2_words(1, e0, e1)
+        wide_runs = gate_wide[:].rearrange("p r (m n) -> p (r m) n", n=P)
+        for x0 in range(0, 2 * SPREAD, 4):
+            x1 = min(x0 + 4, 2 * SPREAD)
+            bank = psum_bank(4 + x0 // 4, [P, x1 - x0, P])
+            for x in range(x0, x1):
+                nc.tensor.transpose(bank[:, x - x0, :], gate_col(*divmod(x, SPREAD)).to_broadcast([P, P]), ident[:])
+            nc.scalar.copy(wide_runs[:, x0:x1, :], bank[:])
 
-        for e0, e1 in EXPERT_UNITS:
+        load_w2_scales(1)
+        for e0, e1 in ((0, 4), (4, 8), (8, E)):
+            load_w2_words(1, e0, e1)
+        a_sb = held([P, 4, T], F32, "a_sb")
+        for t0, t1 in ((0, 256), (256, 512), (512, T)):
+            nc.sync.dma_start(a_sb[:, :, t0:t1], a.rearrange("(p j) t -> p j t", j=4)[:, :, t0:t1])
+        w1_s = held([P, K], U8, "w1_s")
+        nc.vector.memset(w1_s[:].bitcast(I32), 0)
+        for q in range(4):
+            nc.sync.dma_start(w1_s[32 * q : 32 * q + 4, :].bitcast(I32), w1t_scales[0, 4 * q : 4 * q + 4, :].bitcast(I32))
+        w1_w = held([P, K], U32, "w1_w")
+        nc.sync.dma_start(w1_w[:].bitcast(I32), w1t_words[0].rearrange("p k d -> p (k d)").bitcast(I32))
+
+        for e0, e1 in ((0, 4), (4, 8), (8, 11), (11, E)):
             for s in range(PASSES):
                 nc.vector.tensor_copy(
                     slot_w[s][:, e0 * C : e1 * C], dy_w[:, s, :].indirect(offs_sb[:, e0 * C // 16 : e1 * C // 16])
@@ -136,100 +147,92 @@ def tile_moe_sub_relu_kernel(
                     )
             nc.scalar.copy(y[b][:, e0 * C : e1 * C], bank[:])
 
-        dh_t = [held([P, m1 - m0, 2, P, 2], BF16, f"dh_t{m0}") for m0, m1 in PIECES]
+        dh_t = [held([P, 2, P, 2], BF16, f"dh_t{m}") for m in range(BLOCKS)]
+        fetched = {}
 
-        def gated_gathers(b, m0, m1):
-            gated = []
+        def fetch(b, m0, m1, gated):
             for r in range(2):
-                u = held([P, (m1 - m0) * P], F32, f"gated{b}{m0}{r}")
-                nc.vector.tensor_tensor(
-                    u[:],
-                    y[b][:].indirect(pos_sb[r][:, m0 * P // 16 : m1 * P // 16]),
-                    gate_sb[:, r * T + m0 * P : r * T + m1 * P],
-                    MULT,
-                )
-                gated.append(u)
-            return m0, gated
+                u = held([P, (m1 - m0) * P], F32, f"fetched{b}{m0}{r}")
+                window = y[b][:].indirect(pos_sb[r][:, m0 * P // 16 : m1 * P // 16])
+                if gated:
+                    nc.vector.tensor_tensor(u[:], window, gate_wide[:, r, m0 * P : m1 * P], MULT)
+                else:
+                    nc.scalar.activation(u[:], window, COPY)
+                for m in range(m0, m1):
+                    fetched[b, m, r] = u[:, (m - m0) * P : (m - m0 + 1) * P]
 
-        def summed(gathered, b, pieces, number):
-            first, gated = gathered
-            base = PIECES[pieces[0]][0]
-            bank = psum_bank(number, [P, PIECES[pieces[-1]][1] - base, P])
-            for m in range(base, PIECES[pieces[-1]][1]):
+        def sum_gated(pairs, number):
+            bank = psum_bank(number, [P, len(pairs), P])
+            for n, (b, m) in enumerate(pairs):
                 for r in range(2):
-                    nc.tensor.matmul(
-                        bank[:, m - base, :],
-                        gated[r][:, (m - first) * P : (m - first + 1) * P],
-                        ident[:],
-                        start=(r == 0),
-                        stop=(r == 1),
-                        is_transpose=True,
+                    nc.tensor.matmul(bank[:, n, :], fetched[b, m, r], ident[:], start=(r == 0), stop=(r == 1), is_transpose=True)
+            for n, (b, m) in enumerate(pairs):
+                if n + 1 < len(pairs) and pairs[n + 1] == (b + 1, m) and b % 2 == 0:
+                    nc.scalar.copy(
+                        dh_t[m][:, :, 32 * b : 32 * (b + 2), :],
+                        bank[:, n : n + 2, :].rearrange("t b (q u e) -> t u (b q) e", u=2, e=2),
                     )
-            for n in pieces:
-                m0, m1 = PIECES[n]
-                nc.scalar.copy(
-                    dh_t[n][:, :, :, 32 * b : 32 * (b + 1), :],
-                    bank[:, m0 - base : m1 - base, :].rearrange("t m (p u e) -> t m u p e", u=2, e=2),
-                )
+                elif not (n > 0 and pairs[n - 1] == (b - 1, m) and b % 2 == 1):
+                    nc.scalar.copy(
+                        dh_t[m][:, :, 32 * b : 32 * (b + 1), :], bank[:, n, :].rearrange("t (q u e) -> t u q e", u=2, e=2)
+                    )
 
-        units = [(0, 4, 0, 0), (0, 4, 1, 1), (4, 8, 0, 2), (8, 11, 0, 3), (11, 12, 0, 4), (4, 8, 1, 3), (8, 12, 1, 6)]
-        for e0, e1, b, number in units:
-            experts_product(e0, e1, b, number)
-        a_sb = held([P, 4, T], F32, "a_sb")
-        for t0, t1 in ((0, 512), (512, T)):
-            nc.sync.dma_start(a_sb[:, :, t0:t1], a.rearrange("(p j) t -> p j t", j=4)[:, :, t0:t1])
-        for e0, e1, b, number in ((0, 4, 2, 7), (0, 4, 3, 0)):
-            experts_product(e0, e1, b, number)
-        summed(gated_gathers(0, 0, 4), 0, (0, 1), 7)
-        for e0, e1, b, number in ((4, 8, 2, 1), (4, 8, 3, 2), (8, 10, 2, 3), (10, E, 2, 5), (8, E, 3, 4)):
-            experts_product(e0, e1, b, number)
-        summed(gated_gathers(0, 4, 6), 0, (2, 3), 5)
-        gathered = gated_gathers(1, 0, 6)
-        summed(gathered, 1, (0, 1), 4)
-        summed(gathered, 1, (2, 3), 3)
+        def sum_plain(b0, m, number):
+            bank = psum_bank(number, [P, 2, 2, 2, 32, 2])
+            for r in range(2):
+                for bb in range(2):
+                    nc.tensor.transpose(
+                        bank[:, r, :, bb].rearrange("t u q e -> t q u e"), fetched[b0 + bb, m, r], ident[:]
+                    )
+            first = held([P, 2, P], F32, f"first{b0}{m}")
+            nc.scalar.activation(
+                first[:].rearrange("t u x -> t (u x)"), bank[:, 0].rearrange("t u b q e -> t (u b q e)"), COPY, scale=gate_col(0, m)
+            )
+            nc.vector.scalar_tensor_tensor(
+                dh_t[m][:, :, 32 * b0 : 32 * (b0 + 2), :].rearrange("t u p e -> t u (p e)"),
+                bank[:, 1].rearrange("t u b q e -> t u (b q e)"),
+                gate_col(1, m),
+                first[:],
+                MULT,
+                ADD,
+            )
 
-        w1_s = late([P, K], U8, "w1_s", "then_w1_s")
-        nc.vector.memset(w1_s[:].bitcast(I32), 0)
-        for q in range(4):
-            nc.sync.dma_start(w1_s[32 * q : 32 * q + 4, :].bitcast(I32), w1t_scales[0, 4 * q : 4 * q + 4, :].bitcast(I32))
-        w1_w = late([P, K], U32, "w1_w", "then_slot_s")
-        nc.sync.dma_start(w1_w[:].bitcast(I32), w1t_words[0].rearrange("p k d -> p (k d)").bitcast(I32))
+        relu_on = {}
 
-        def side_by_side(mask, t0, t1):
-            return mask.rearrange("p (c i) j -> p c j i", i=2), a_sb[:, :, t0:t1].rearrange("p j (c i) -> p c j i", i=2)
+        def relu_mask(m0, m1):
+            mask = held([P, (m1 - m0) * P, 4], BF16, f"relu_on{m0}")
+            nc.vector.tensor_scalar(
+                mask[:].rearrange("p (c i) j -> p c j i", i=2),
+                a_sb[:, :, m0 * P : m1 * P].rearrange("p j (c i) -> p c j i", i=2),
+                0.0,
+                None,
+                IS_GT,
+            )
+            for m in range(m0, m1):
+                relu_on[m] = (mask, m0)
 
-        relu_on = [late([P, c1 - c0, 4], BF16, f"relu_on{n}", f"then_relu{n}") for n, (c0, c1) in enumerate(((0, 512), (512, T)))]
+        da = {}
 
-        def signs(n, c0, c1):
-            for m in range(c0, c1, P):
-                nc.scalar.activation(*side_by_side(relu_on[n][:, m - c0 : m - c0 + P, :], m, m + P), SIGN)
-
-        da = held([P, T, 4], BF16, "da")
-
-        def turned_words(n, number):
-            m0, m1 = PIECES[n]
+        def masked(m0, m1, number):
             bank = psum_bank(number, [P, 2, (m1 - m0) * P])
-            for m in range(m1 - m0):
+            for m in range(m0, m1):
                 for u in range(2):
-                    words = dh_t[n][:, m, u].rearrange("t p e -> t (p e)").bitcast(F32)
-                    nc.tensor.transpose(bank[:, u, m * P : (m + 1) * P], words, ident[:])
-            return bank
-
-        def masked(n, bank):
-            m0, m1 = PIECES[n]
-            mask = relu_on[m0 // 4][:, (m0 % 4) * P : (m0 % 4 + m1 - m0) * P, :]
+                    words = dh_t[m][:, u].rearrange("t p e -> t (p e)").bitcast(F32)
+                    nc.tensor.transpose(bank[:, u, (m - m0) * P : (m - m0 + 1) * P], words, ident[:])
+            mask, base = relu_on[m0]
+            da[m0] = held([P, (m1 - m0) * P, 4], BF16, f"da{m0}")
             nc.vector.tensor_tensor(
-                da[:, m0 * P : m1 * P, :].rearrange("p t (u e) -> p t u e", u=2),
+                da[m0][:].rearrange("p t (u e) -> p t u e", u=2),
                 bank[:].bitcast(BF16).rearrange("p u (t e) -> p t u e", e=2),
-                mask.rearrange("p t (u e) -> p t u e", u=2),
+                mask[:, (m0 - base) * P : (m1 - base) * P, :].rearrange("p t (u e) -> p t u e", u=2),
                 MULT,
             )
 
-        def first_layer(t0, t1, number, copy_out):
-            width = t1 - t0
-            da_w = held([P, width], U32, f"da_w{t0}")
-            da_s = held([P, width], U8, f"da_s{t0}")
-            nc.vector.quantize_mx(da_w[:].bitcast(FP8X4), da_s[:], da[:, t0:t1, :].rearrange("p t j -> p (t j)"))
+        def first_layer(m0, m1, number, copy_out):
+            width = (m1 - m0) * P
+            da_w = held([P, width], U32, f"da_w{m0}")
+            da_s = held([P, width], U8, f"da_s{m0}")
+            nc.vector.quantize_mx(da_w[:].bitcast(FP8X4), da_s[:], da[m0][:].rearrange("p t j -> p (t j)"))
             bank = psum_bank(number, [P, width])
             nc.tensor.matmul_mx(
                 out=bank[:],
@@ -240,29 +243,46 @@ def tile_moe_sub_relu_kernel(
                 start=True,
                 stop=True,
             )
-            result = held([P, width], F32, f"result{t0}")
+            result = held([P, width], F32, f"result{m0}")
             copy_out(result[:], bank[:])
-            nc.sync.dma_start(out[:, t0:t1], result[:])
+            nc.sync.dma_start(out[:, m0 * P : m1 * P], result[:])
 
-        for n, (c0, c1) in enumerate(((0, 512), (512, T))):
-            signs(n, c0, c1)
-        summed(gated_gathers(2, 0, 4), 2, (0, 1), 5)
-        turned = []
-        for n, banks in enumerate(((4, 6), (3, 0))):
-            summed(gated_gathers(3, *PIECES[n]), 3, (n,), banks[0])
-            turned.append(turned_words(n, banks[1]))
-        summed(gated_gathers(2, 4, 6), 2, (2, 3), 5)
-        last = gated_gathers(3, 4, 6)
-        summed(last, 3, (2,), 4)
-        summed(last, 3, (3,), 3)
-        for n in range(2):
-            nc.vector.tensor_scalar_max(relu_on[n][:], relu_on[n][:], 0.0)
-        masked(0, turned[0])
-        masked(1, turned[1])
-        turned.extend([turned_words(2, 1), turned_words(3, 2)])
-        first_layer(0, 256, 3, nc.scalar.copy)
-        masked(2, turned[2])
-        first_layer(256, 512, 4, nc.scalar.copy)
-        masked(3, turned[3])
-        first_layer(512, 640, 5, nc.scalar.copy)
-        first_layer(640, T, 7, nc.vector.tensor_copy)
+        for e0, e1, b, number in (
+            (0, 4, 0, 0), (0, 4, 1, 1), (4, 8, 0, 2), (4, 8, 1, 3), (8, 11, 0, 4), (11, E, 0, 5), (8, E, 1, 6),
+        ):
+            experts_product(e0, e1, b, number)
+        fetch(0, 0, 5, True)
+        fetch(0, 5, 6, False)
+        experts_product(0, 4, 2, 7)
+        experts_product(0, 4, 3, 0)
+        fetch(1, 0, 5, True)
+        fetch(1, 5, 6, False)
+        for e0, e1, b, number in ((4, 8, 2, 1), (4, 8, 3, 2), (8, 10, 2, 3), (10, E, 2, 4), (8, 10, 3, 5), (10, E, 3, 6)):
+            experts_product(e0, e1, b, number)
+        fetch(2, 0, 3, True)
+        fetch(2, 4, 6, False)
+        sum_plain(0, 5, 3)
+        fetch(3, 4, 6, False)
+        sum_gated([(0, 0), (1, 0), (0, 1), (1, 1)], 4)
+        fetch(3, 0, 2, True)
+        sum_gated([(0, 4), (1, 4), (0, 2), (1, 2)], 5)
+        fetch(3, 2, 3, True)
+        fetch(2, 3, 4, False)
+        fetch(3, 3, 4, False)
+        sum_gated([(0, 3), (1, 3)], 6)
+        relu_mask(0, 2)
+        sum_plain(2, 4, 0)
+        sum_plain(2, 5, 1)
+        sum_gated([(2, 0), (3, 0), (2, 1), (3, 1)], 7)
+        relu_mask(4, 6)
+        sum_plain(2, 3, 3)
+        sum_gated([(2, 2), (3, 2)], 2)
+        relu_mask(2, 4)
+        masked(4, 6, 5)
+        masked(0, 2, 4)
+        first_layer(4, 6, 6, nc.scalar.copy)
+        masked(3, 4, 7)
+        first_layer(0, 2, 0, nc.scalar.copy)
+        masked(2, 3, 1)
+        first_layer(3, 4, 2, nc.scalar.copy)
+        first_layer(2, 3, 3, nc.vector.tensor_copy)

from contextlib import ExitStack

import concourse.mybir as mybir

K, T, E, C, H, N = 128, 768, 12, 128, 512, 1024
FLOPS = 2 * N * H * E * C + 2 * H * K * T

F32 = mybir.dt.float32
BF16 = mybir.dt.bfloat16
I32 = mybir.dt.int32
U32 = mybir.dt.uint32
U16 = mybir.dt.uint16
U8 = mybir.dt.uint8
FP8X4 = mybir.dt.float8_e4m3fn_x4
FP4X4 = mybir.dt.float4_e2m1fn_x4
MULT = mybir.AluOpType.mult
ADD = mybir.AluOpType.add
IS_GT = mybir.AluOpType.is_gt
ABS = mybir.ActivationFunctionType.Abs
RELU = mybir.ActivationFunctionType.Relu
COPY = mybir.ActivationFunctionType.Copy

P = 128
SLOTS = E * C
PASSES = N // 512
ROW_TILES = H // P
BLOCKS = T // P
GATE_ROWS, GATE_RUN = 4, 384
SPREAD = 5


def tile_moe_sub_relu_kernel(
    tc, dy_words, dy_scales, w2t_words, w2t_scales, w1t_words, w1t_scales, a, gate, offs, pos1, pos2, out
):
    nc = tc.nc
    with ExitStack() as ctx:
        keep = ctx.enter_context(tc.tile_pool(name="keep", bufs=1))
        psum = ctx.enter_context(tc.psum_pool(name="psum", bufs=1))

        def held(shape, dtype, name, tag=None):
            return keep.tile(shape, dtype, name=name, tag=tag or name, align_bytes=64)

        def psum_bank(number, shape):
            return psum.tile(shape, F32, name=f"bank{number}", tag=f"bank{number}")

        offs_sb = keep.tile([P, SLOTS // 16], U16, name="offs_sb")
        pos_sb = [keep.tile([P, T // 16], U16, name=f"pos{r}_sb") for r in range(2)]
        dy_s = held([P, T], U8, "dy_s")
        dy_w = held([P, PASSES, T], U32, "dy_w")
        slot_w = [held([P, SLOTS], U32, f"slot_w{s}") for s in range(PASSES)]
        slot_s = [held([P, SLOTS], U8, f"slot_s{s}") for s in range(PASSES)]
        y = [held([P, SLOTS], F32, f"y{b}") for b in range(ROW_TILES)]
        gate_rows = held([P, GATE_RUN], F32, "gate_rows")
        gate_cols = held([P, GATE_RUN // P, GATE_ROWS], F32, "gate_cols")
        gate_wide = held([P, 2, SPREAD * P], F32, "gate_wide")
        ident = held([P, P], F32, "ident")
        w2_w = [held([P, E * PASSES, H], U8, f"w2_w{half}") for half in range(2)]
        w2_s = [held([P, E * PASSES, 2 * P], U8, f"w2_s{half}") for half in range(2)]
        w2_words = w2t_words.rearrange("e s p x -> p (e s) x")
        w2_rows = w2t_scales.rearrange("e s b i -> b (e s) i")

        def load_w2_scales(half):
            for r in range(4):
                nc.sync.dma_start(
                    w2_s[half][r:P:32].bitcast(I32), w2_rows[r:16:4, :, 2 * P * half : 2 * P * (half + 1)].bitcast(I32)
                )

        def load_w2_words(half, e0, e1):
            rows = slice(e0 * PASSES, e1 * PASSES)
            nc.sync.dma_start(w2_w[half][:, rows].bitcast(I32), w2_words[:, rows, H * half : H * (half + 1)].bitcast(I32))

        def gate_col(r, m):
            return gate_cols[:, m % 3, 2 * r + m // 3 : 2 * r + m // 3 + 1]

        nc.vector.memset(dy_s[:].bitcast(I32), 0)
        nc.vector.memset(gate_rows[:], 0.0)
        nc.gpsimd.iota(ident[:], pattern=[[-1, P]], base=0, channel_multiplier=1, allow_small_or_imprecise_dtypes=True)
        nc.vector.memset(w2_s[0][:].bitcast(I32), 0)
        nc.vector.memset(w2_s[1][:].bitcast(I32), 0)
        nc.vector.memset(slot_s[1][:].bitcast(I32), 0)

        nc.sync.dma_start(offs_sb[:], offs)
        nc.scalar.dma_start(gate_rows[0:GATE_ROWS, :], gate[:, 0, :].rearrange("r (h x) -> r h x", x=GATE_RUN))
        for r in range(4):
            nc.sync.dma_start(dy_s[r:P:16].bitcast(I32), dy_scales.rearrange("s (q r) t -> r q s t", r=4)[r].bitcast(I32))
        nc.sync.dma_start(dy_w[:].bitcast(I32), dy_words.rearrange("s p t d -> p s (t d)").bitcast(I32))
        load_w2_scales(0)
        load_w2_words(0, 0, 4)

        nc.scalar.activation(ident[:], ident[:], ABS)
        nc.scalar.activation(ident[:], ident[:], RELU, bias=1.0, scale=-1.0)
        bank = psum_bank(7, [P, GATE_RUN // P, P])
        for k in range(GATE_RUN // P):
            nc.tensor.transpose(bank[:, k, :], gate_rows[:, k * P : (k + 1) * P], ident[:])
        nc.scalar.copy(gate_cols[:], bank[:, :, 0:GATE_ROWS])

        for j0 in range(0, SLOTS, 512):
            nc.vector.tensor_copy(slot_s[0][:, j0 : j0 + 512], dy_s[:].indirect(offs_sb[:, j0 // 16 : (j0 + 512) // 16]))
        for x in range(4):
            nc.sync.dma_start(slot_s[1][x:P:32].bitcast(I32), slot_s[0][16 + x : P : 32].bitcast(I32))
        load_w2_words(0, 4, 8)
        load_w2_words(0, 8, E)
        for r in range(2):
            nc.sync.dma_start(pos_sb[r][:], (pos1, pos2)[r])

        wide_runs = gate_wide[:].rearrange("p r (m n) -> p (r m) n", n=P)
        for x0 in range(0, 2 * SPREAD, 4):
            x1 = min(x0 + 4, 2 * SPREAD)
            bank = psum_bank(4 + x0 // 4, [P, x1 - x0, P])
            for x in range(x0, x1):
                nc.tensor.transpose(bank[:, x - x0, :], gate_col(*divmod(x, SPREAD)).to_broadcast([P, P]), ident[:])
            nc.scalar.copy(wide_runs[:, x0:x1, :], bank[:])

        load_w2_scales(1)
        for e0, e1 in ((0, 4), (4, 8), (8, E)):
            load_w2_words(1, e0, e1)
        a_sb = held([P, 4, T], F32, "a_sb")
        for t0, t1 in ((0, 256), (256, 512), (512, T)):
            nc.sync.dma_start(a_sb[:, :, t0:t1], a.rearrange("(p j) t -> p j t", j=4)[:, :, t0:t1])
        w1_s = held([P, K], U8, "w1_s")
        nc.vector.memset(w1_s[:].bitcast(I32), 0)
        for q in range(4):
            nc.sync.dma_start(w1_s[32 * q : 32 * q + 4, :].bitcast(I32), w1t_scales[0, 4 * q : 4 * q + 4, :].bitcast(I32))
        w1_w = held([P, K], U32, "w1_w")
        nc.sync.dma_start(w1_w[:].bitcast(I32), w1t_words[0].rearrange("p k d -> p (k d)").bitcast(I32))

        for e0, e1 in ((0, 4), (4, 8), (8, 11), (11, E)):
            for s in range(PASSES):
                nc.vector.tensor_copy(
                    slot_w[s][:, e0 * C : e1 * C], dy_w[:, s, :].indirect(offs_sb[:, e0 * C // 16 : e1 * C // 16])
                )

        def experts_product(e0, e1, b, number):
            half, part = divmod(b, 2)
            bank = psum_bank(number, [P, (e1 - e0) * C])
            for e in range(e0, e1):
                cols = slice(e * C, (e + 1) * C)
                for s in range(PASSES):
                    nc.tensor.matmul_mx(
                        out=bank[:, (e - e0) * C : (e - e0 + 1) * C],
                        lhsT=w2_w[half][:, e * PASSES + s, 2 * P * part : 2 * P * (part + 1)].bitcast(FP4X4),
                        lhsT_scale=w2_s[half][:, e * PASSES + s, P * part : P * (part + 1)],
                        rhs=slot_w[s][:, cols].bitcast(FP8X4),
                        rhs_scale=slot_s[s][:, cols],
                        start=(s == 0),
                        stop=(s == PASSES - 1),
                    )
            nc.scalar.copy(y[b][:, e0 * C : e1 * C], bank[:])

        dh_t = [held([P, 2, P, 2], BF16, f"dh_t{m}") for m in range(BLOCKS)]
        fetched = {}

        def fetch(b, m0, m1, gated):
            for r in range(2):
                u = held([P, (m1 - m0) * P], F32, f"fetched{b}{m0}{r}")
                window = y[b][:].indirect(pos_sb[r][:, m0 * P // 16 : m1 * P // 16])
                if gated:
                    nc.vector.tensor_tensor(u[:], window, gate_wide[:, r, m0 * P : m1 * P], MULT)
                else:
                    nc.scalar.activation(u[:], window, COPY)
                for m in range(m0, m1):
                    fetched[b, m, r] = u[:, (m - m0) * P : (m - m0 + 1) * P]

        def sum_gated(pairs, number):
            bank = psum_bank(number, [P, len(pairs), P])
            for n, (b, m) in enumerate(pairs):
                for r in range(2):
                    nc.tensor.matmul(bank[:, n, :], fetched[b, m, r], ident[:], start=(r == 0), stop=(r == 1), is_transpose=True)
            for n, (b, m) in enumerate(pairs):
                if n + 1 < len(pairs) and pairs[n + 1] == (b + 1, m) and b % 2 == 0:
                    nc.scalar.copy(
                        dh_t[m][:, :, 32 * b : 32 * (b + 2), :],
                        bank[:, n : n + 2, :].rearrange("t b (q u e) -> t u (b q) e", u=2, e=2),
                    )
                elif not (n > 0 and pairs[n - 1] == (b - 1, m) and b % 2 == 1):
                    nc.scalar.copy(
                        dh_t[m][:, :, 32 * b : 32 * (b + 1), :], bank[:, n, :].rearrange("t (q u e) -> t u q e", u=2, e=2)
                    )

        def sum_plain(b0, m, number):
            bank = psum_bank(number, [P, 2, 2, 2, 32, 2])
            for r in range(2):
                for bb in range(2):
                    nc.tensor.transpose(
                        bank[:, r, :, bb].rearrange("t u q e -> t q u e"), fetched[b0 + bb, m, r], ident[:]
                    )
            first = held([P, 2, P], F32, f"first{b0}{m}")
            nc.scalar.activation(
                first[:].rearrange("t u x -> t (u x)"), bank[:, 0].rearrange("t u b q e -> t (u b q e)"), COPY, scale=gate_col(0, m)
            )
            nc.vector.scalar_tensor_tensor(
                dh_t[m][:, :, 32 * b0 : 32 * (b0 + 2), :].rearrange("t u p e -> t u (p e)"),
                bank[:, 1].rearrange("t u b q e -> t u (b q e)"),
                gate_col(1, m),
                first[:],
                MULT,
                ADD,
            )

        relu_on = {}

        def relu_mask(m0, m1):
            mask = held([P, (m1 - m0) * P, 4], BF16, f"relu_on{m0}")
            nc.vector.tensor_scalar(
                mask[:].rearrange("p (c i) j -> p c j i", i=2),
                a_sb[:, :, m0 * P : m1 * P].rearrange("p j (c i) -> p c j i", i=2),
                0.0,
                None,
                IS_GT,
            )
            for m in range(m0, m1):
                relu_on[m] = (mask, m0)

        da = {}

        def masked(m0, m1, number):
            bank = psum_bank(number, [P, 2, (m1 - m0) * P])
            for m in range(m0, m1):
                for u in range(2):
                    words = dh_t[m][:, u].rearrange("t p e -> t (p e)").bitcast(F32)
                    nc.tensor.transpose(bank[:, u, (m - m0) * P : (m - m0 + 1) * P], words, ident[:])
            mask, base = relu_on[m0]
            da[m0] = held([P, (m1 - m0) * P, 4], BF16, f"da{m0}")
            nc.vector.tensor_tensor(
                da[m0][:].rearrange("p t (u e) -> p t u e", u=2),
                bank[:].bitcast(BF16).rearrange("p u (t e) -> p t u e", e=2),
                mask[:, (m0 - base) * P : (m1 - base) * P, :].rearrange("p t (u e) -> p t u e", u=2),
                MULT,
            )

        def first_layer(m0, m1, number, copy_out):
            width = (m1 - m0) * P
            da_w = held([P, width], U32, f"da_w{m0}")
            da_s = held([P, width], U8, f"da_s{m0}")
            nc.vector.quantize_mx(da_w[:].bitcast(FP8X4), da_s[:], da[m0][:].rearrange("p t j -> p (t j)"))
            bank = psum_bank(number, [P, width])
            nc.tensor.matmul_mx(
                out=bank[:],
                lhsT=w1_w[:].bitcast(FP8X4),
                lhsT_scale=w1_s[:],
                rhs=da_w[:].bitcast(FP8X4),
                rhs_scale=da_s[:],
                start=True,
                stop=True,
            )
            result = held([P, width], F32, f"result{m0}")
            copy_out(result[:], bank[:])
            nc.sync.dma_start(out[:, m0 * P : m1 * P], result[:])

        for e0, e1, b, number in (
            (0, 4, 0, 0), (0, 4, 1, 1), (4, 8, 0, 2), (4, 8, 1, 3), (8, 11, 0, 4), (11, E, 0, 5), (8, E, 1, 6),
        ):
            experts_product(e0, e1, b, number)
        fetch(0, 0, 5, True)
        fetch(0, 5, 6, False)
        experts_product(0, 4, 2, 7)
        experts_product(0, 4, 3, 0)
        fetch(1, 0, 5, True)
        fetch(1, 5, 6, False)
        for e0, e1, b, number in ((4, 8, 2, 1), (4, 8, 3, 2), (8, 10, 2, 3), (10, E, 2, 4), (8, 10, 3, 5), (10, E, 3, 6)):
            experts_product(e0, e1, b, number)
        fetch(2, 0, 3, True)
        fetch(2, 4, 6, False)
        sum_plain(0, 5, 3)
        fetch(3, 4, 6, False)
        sum_gated([(0, 0), (1, 0), (0, 1), (1, 1)], 4)
        fetch(3, 0, 2, True)
        sum_gated([(0, 4), (1, 4), (0, 2), (1, 2)], 5)
        fetch(3, 2, 3, True)
        fetch(2, 3, 4, False)
        fetch(3, 3, 4, False)
        sum_gated([(0, 3), (1, 3)], 6)
        relu_mask(0, 2)
        sum_plain(2, 4, 0)
        sum_plain(2, 5, 1)
        sum_gated([(2, 0), (3, 0), (2, 1), (3, 1)], 7)
        relu_mask(4, 6)
        sum_plain(2, 3, 3)
        sum_gated([(2, 2), (3, 2)], 2)
        relu_mask(2, 4)
        masked(4, 6, 5)
        masked(0, 2, 4)
        first_layer(4, 6, 6, nc.scalar.copy)
        masked(3, 4, 7)
        first_layer(0, 2, 0, nc.scalar.copy)
        masked(2, 3, 1)
        first_layer(3, 4, 2, nc.scalar.copy)
        first_layer(2, 3, 3, nc.vector.tensor_copy)
